import numpy as np
import ml_dtypes


def mxq(x, axis, fmt="e4m3"):
    dtype, down = {"e4m3": (ml_dtypes.float8_e4m3fn, 7), "e5m2": (ml_dtypes.float8_e5m2, 14)}[fmt]
    v = np.moveaxis(np.asarray(x, np.float32).astype(ml_dtypes.bfloat16).astype(np.float64), axis, -1)
    blocks = v.reshape(v.shape[:-1] + (-1, 32))
    amax = np.abs(blocks).max(-1, keepdims=True)
    byte = np.maximum(np.where(amax > 0, np.frexp(amax)[1] - 1 + 127, 0) - down, 1)
    scale = np.exp2(byte - 127.0)
    codes = (blocks / scale).astype(np.float32).astype(dtype).astype(np.float64)
    return np.moveaxis((codes * scale).reshape(v.shape), -1, axis)


WIDE = False


def mx_kscale(k):
    if not WIDE:
        return np.ones(k)
    levels = np.array([10, -10, 5, -5, 0])
    if k % 512:
        return np.exp2(np.random.permutation(np.resize(levels, k // 32))).repeat(32)
    a = np.empty((k // 512, 16))
    for p in range(k // 512):
        a[p, :8] = np.random.permutation(np.resize(levels, 8))
        for g in range(8):
            far = levels[np.abs(levels - a[p, g]) >= 10]
            a[p, g + 8] = far[np.random.randint(len(far))]
    return np.exp2(a.ravel()).repeat(32)


def f64(x):
    return np.asarray(x).astype(np.float64)


def striped(idx):
    return np.tile(idx.reshape(-1, 16).T, (8, 1)).astype(np.uint16)


def unstriped(offs):
    return offs[:16].T.reshape(-1).astype(np.int64)


E2M1 = np.array([0.0, 0.5, 1.0, 1.5, 2.0, 3.0, 4.0, 6.0, -0.0, -0.5, -1.0, -1.5, -2.0, -3.0, -4.0, -6.0])


def pack_weight(w, fmt):
    k, n = w.shape
    w = f64(np.asarray(w, np.float32).astype(ml_dtypes.bfloat16)).reshape(k // 32, 32, n)
    amax = np.abs(w).max(1)
    if fmt == "e4m3":
        byte = np.frexp(amax)[1] - 1 + 127 - 7
    else:
        mant, ex = np.frexp(amax / 6.0)
        byte = np.where(mant > 0.5, ex, ex - 1) + 127
    byte = np.clip(np.where(amax > 0, byte, 1), 1, 254)
    scaled = (w * np.exp2(127.0 - byte)[:, None, :]).reshape(k, n).astype(np.float32)
    by_word = np.ascontiguousarray(scaled.reshape(k // 512, 128, 4, n).transpose(0, 1, 3, 2))
    if fmt == "e4m3":
        words = by_word.astype(ml_dtypes.float8_e4m3fn).view(np.uint8)
    else:
        c = by_word.astype(ml_dtypes.float4_e2m1fn).view(np.uint8) & 0xF
        words = (c[..., 0::2] | (c[..., 1::2] << 4)).reshape(k // 512, 128, 2 * n)
    return np.ascontiguousarray(words), np.ascontiguousarray(byte.astype(np.uint8).reshape(k // 512, 16, n))


def unpack_weight(words, scales, fmt):
    g, _, n = scales.shape
    words = np.ascontiguousarray(words).reshape(g, 128, n, -1)
    if fmt == "e4m3":
        vals = words.view(ml_dtypes.float8_e4m3fn).astype(np.float64)
    else:
        nib = np.empty((g, 128, n, 4), np.uint8)
        nib[..., 0::2] = words & 0xF
        nib[..., 1::2] = words >> 4
        vals = E2M1[nib]
    vals = vals * np.repeat(np.exp2(scales.astype(np.float64) - 127.0), 8, axis=1)[..., None]
    return vals.transpose(0, 1, 3, 2).reshape(g * 512, n)


def silu(v):
    return v / (1.0 + np.exp(-np.maximum(v, -700.0)))


K, T, E, C, N = 512, 768, 12, 128, 256


def by_expert(wq, xq):
    return np.concatenate([wq[e].T @ xq[:, e * C:(e + 1) * C] for e in range(E)], axis=1)


def setup_inputs():
    n = np.random.standard_normal
    s = mx_kscale(K)[:, None]
    first = np.random.permutation(np.repeat(np.arange(E), T // E))
    second = (first + 1 + np.random.permutation(np.repeat(np.arange(E - 1), -(-T // (E - 1)))[:T])) % E
    while np.bincount(second, minlength=E).max() != T // E:
        load = np.bincount(second, minlength=E); hi, lo = int(load.argmax()), int(load.argmin())
        t = np.flatnonzero((second == hi) & (first != lo))[0]; second[t] = lo
    slot_token = np.empty(E * C, np.int64); pos = np.empty((2, T), np.int64); fill = np.zeros(E, np.int64)
    place = np.stack([np.random.permutation(C) for _ in range(E)])
    for r, deal in enumerate((first, second)):
        for t in np.random.permutation(T):
            e = deal[t]; j = e * C + place[e, fill[e]]; fill[e] += 1; slot_token[j] = t; pos[r, t] = j
    g = np.random.uniform(0.2, 0.8, T)
    x = pack_weight(n((K, T)) * s, "e4m3")
    return {
        "x_words": x[0],
        "x_scales": x[1],
        "w": (n((E, K, N)) / np.sqrt(K) / s[None]).astype(np.float32),
        "b": (0.3 * n((N, E))).astype(np.float32),
        "gate": np.stack([np.tile(g, (N, 1)), np.tile(1.0 - g, (N, 1))]).astype(np.float32),
        "offs": striped(slot_token),
        "pos1": striped(pos[0]),
        "pos2": striped(pos[1]),
    }


def reference(x_words, x_scales, w, b, gate, offs, pos1, pos2):
    idx = unstriped(offs)
    xq = unpack_weight(x_words, x_scales, "e4m3")[:, idx]
    y = by_expert(mxq(f64(w), 1, "e4m3"), xq)
    y = silu(y + np.repeat(f64(b), C, axis=1))
    return f64(gate[0]) * y[:, unstriped(pos1)] + f64(gate[1]) * y[:, unstriped(pos2)]

@@ -1,0 +1,152 @@
+from contextlib import ExitStack
+
+import concourse.mybir as mybir
+
+K, T, E, C, N = 512, 768, 12, 128, 256
+S = E * C
+P = 128
+PACK = 4
+HALVES = N // P
+FLOPS = 2 * K * N * S
+
+F32 = mybir.dt.float32
+BF16 = mybir.dt.bfloat16
+I32 = mybir.dt.int32
+U32 = mybir.dt.uint32
+U16 = mybir.dt.uint16
+U8 = mybir.dt.uint8
+FP8X4 = mybir.dt.float8_e4m3fn_x4
+MULT = mybir.AluOpType.mult
+ADD = mybir.AluOpType.add
+SILU = mybir.ActivationFunctionType.Silu
+
+LIST_ROWS = 16
+WORD_EXPERTS = 4
+SCALE_EXPERTS = 2
+GATHER_STEPS = [("words", 0, 0), ("words", 1, 0), ("words", 2, 1), ("scales", 0, 2), ("scales", 1, 3), ("scales", 2, 4), ("scales", 3, 6), ("scales", 4, 8), ("scales", 5, 10)]
+VECTOR_COPIES = [(4, 0), (5, 0), (6, 0), (7, 0), (8, 0), (9, 0), (10, 0), (11, 0)]
+TOKEN_CUTS = [[0,768],[0,512,768]]
+SPLIT = 0
+LINE = 4
+UNITS = [[(0, 0)], [(0, 1), (1, 0)], [(1, 1), (2, 0)], [(2, 1), (3, 0)], [(3, 1), (4, 0)], [(4, 1), (5, 0)], [(5, 1), (6, 0)], [(6, 1), (7, 0)], [(7, 1), (8, 0)], [(8, 1), (9, 0)], [(9, 1), (10, 0)], [(10, 1)], [(11, 0)], [(11, 1)]]
+LOADS = [("offs",), ("words",), ("w", 0, 0, 256), ("scales",), ("w", 1, 0, 256), ("w", 2, 0, 256), ("bias",), ("w", 3, 0, 256), ("w", 4, 0, 256), ("w", 5, 0, 256), ("pos",), ("w", 6, 0, 256), ("w", 7, 0, 256), ("w", 8, 0, 256), ("w", 9, 0, 256), ("w", 10, 0, 256), ("w", 11, 0, 256), ("gate", 0, 0), ("gate", 1, 0), ("gate", 0, 1), ("gate", 1, 1)]
+
+
+def tile_moe_pkd_lin_silu_kernel(tc, x_words, x_scales, w, b, gate, offs, pos1, pos2, out):
+    nc = tc.nc
+    with ExitStack() as ctx:
+        keep = ctx.enter_context(tc.tile_pool(name="keep", bufs=1))
+        psum = ctx.enter_context(tc.psum_pool(name="psum", bufs=8))
+
+        offs_sb = keep.tile([P, S // LIST_ROWS], U16, name="offs_sb")
+        pos_sb = [keep.tile([P, T // LIST_ROWS], U16, name="pos%d_sb" % r) for r in range(2)]
+        token_words = keep.tile([P, T], I32, name="token_words", align_bytes=64)
+        token_scales = keep.tile([P, T], U8, name="token_scales", align_bytes=64)
+        slot_words = [keep.tile([P, WORD_EXPERTS * C], U32, name="slot_words%d" % g, align_bytes=64) for g in range(E // WORD_EXPERTS)]
+        slot_scales = [keep.tile([P, SCALE_EXPERTS * C], U8, name="slot_scales%d" % g, align_bytes=64) for g in range(E // SCALE_EXPERTS)]
+        bias = keep.tile([P, HALVES, E], F32, name="bias")
+        w_raw = [keep.tile([P, PACK, N], F32, name="w_raw%d" % e, align_bytes=64) for e in range(E)]
+        w_grouped = keep.tile([P, E * N, PACK], BF16, name="w_grouped", align_bytes=64)
+        w_words = keep.tile([P, E * N], U32, name="w_words", align_bytes=64)
+        w_scales = keep.tile([P, E * N], U8, name="w_scales", align_bytes=64)
+        gates = [[keep.tile([P, T], F32, name="gate%d_%d" % (r, h)) for r in range(2)] for h in range(HALVES)]
+        y = [keep.tile([P, S], F32, name="y%d" % h) for h in range(HALVES)]
+        terms = [[keep.tile([P, T], F32, name="term%d_%d" % (r, h)) for r in range(2)] for h in range(HALVES)]
+        result = [keep.tile([P, T], F32, name="result%d" % h) for h in range(HALVES)]
+
+        nc.gpsimd.memset(token_scales[:].bitcast(I32), 0)
+        warm = keep.tile([P, 2], F32, name="warm")
+        nc.gpsimd.memset(warm[:, 0:1], 0.0)
+        nc.scalar.activation(warm[:, 1:2], warm[:, 0:1], SILU)
+
+        for load in LOADS:
+            if load[0] == "offs":
+                nc.sync.dma_start(offs_sb[:], offs)
+            elif load[0] == "words":
+                nc.sync.dma_start(token_words[:], x_words[0].rearrange("p t r -> p (t r)").bitcast(I32))
+            elif load[0] == "scales":
+                for q in range(4):
+                    nc.sync.dma_start(token_scales[32 * q : 32 * q + 4, :].bitcast(I32), x_scales[0, 4 * q : 4 * q + 4, :].bitcast(I32))
+            elif load[0] == "bias":
+                nc.sync.dma_start(bias[:], b.rearrange("(h p) e -> p h e", p=P))
+            elif load[0] == "pos":
+                nc.sync.dma_start(pos_sb[0][:], pos1)
+                nc.sync.dma_start(pos_sb[1][:], pos2)
+            elif load[0] == "gate":
+                r, h = load[1], load[2]
+                nc.sync.dma_start(gates[h][r][:], gate[r, h * P : (h + 1) * P, :])
+            else:
+                e, cols = load[1], slice(load[2], load[3])
+                nc.sync.dma_start(w_raw[e][:, :, cols], w[e].rearrange("(p j) n -> p j n", j=PACK)[:, :, cols])
+
+        def gather(sort, g):
+            tile, window = (slot_words[g], token_words[:].bitcast(U32)) if sort == "words" else (slot_scales[g], token_scales[:])
+            per = tile.shape[1] // LIST_ROWS
+            nc.vector.tensor_copy(tile[:], window.indirect(offs_sb[:, g * per : (g + 1) * per]))
+
+        def regroup(copy, e, a, z):
+            copy(
+                w_grouped[:, e * N + a : e * N + z, :].rearrange("p (c i) j -> p c j i", i=LINE),
+                w_raw[e][:, :, a:z].rearrange("p j (c i) -> p c j i", i=LINE),
+            )
+
+        def quantize(a, z):
+            nc.vector.quantize_mx(
+                out=w_words[:, a:z].bitcast(FP8X4),
+                scales=w_scales[:, a:z],
+                in_=w_grouped[:, a:z, :].rearrange("p n j -> p (n j)"),
+            )
+
+        def expert(e, h):
+            cols = slice(e * N + h * P, e * N + (h + 1) * P)
+            gw, pw = divmod(e, WORD_EXPERTS)
+            gs, ps = divmod(e, SCALE_EXPERTS)
+            acc = psum.tile([P, C], F32, name="acc")
+            nc.tensor.matmul_mx(
+                out=acc[:],
+                lhsT=w_words[:, cols].bitcast(FP8X4),
+                lhsT_scale=w_scales[:, cols],
+                rhs=slot_words[gw][:, pw * C : (pw + 1) * C].bitcast(FP8X4),
+                rhs_scale=slot_scales[gs][:, ps * C : (ps + 1) * C],
+                start=True,
+                stop=True,
+            )
+            nc.scalar.activation(y[h][:, e * C : (e + 1) * C], acc[:], SILU, bias=bias[:, h, e : e + 1])
+
+        def combine(h):
+            cuts = TOKEN_CUTS[h]
+            for a, z in zip(cuts[:-1], cuts[1:]):
+                for r in range(2):
+                    entries = pos_sb[r][:, a // LIST_ROWS : z // LIST_ROWS]
+                    nc.vector.tensor_tensor(terms[h][r][:, a:z], y[h][:].indirect(entries), gates[h][r][:, a:z], MULT)
+                nc.vector.tensor_tensor(result[h][:, a:z], terms[h][0][:, a:z], terms[h][1][:, a:z], ADD)
+                nc.sync.dma_start(out[h * P : (h + 1) * P, a:z], result[h][:, a:z])
+
+        done = set()
+        waiting = []
+        copied = set()
+        for u, unit in enumerate(UNITS):
+            for sort, g, step in GATHER_STEPS:
+                if step == u:
+                    gather(sort, g)
+                    done.add((sort, g))
+            for e, h in unit:
+                if (e, h) in copied:
+                    continue
+                if (e, h) in VECTOR_COPIES:
+                    regroup(nc.vector.tensor_copy, e, h * P, (h + 1) * P)
+                elif h == 0 and e < E - SPLIT:
+                    regroup(nc.scalar.copy, e, 0, N)
+                    copied.add((e, 1))
+                else:
+                    regroup(nc.scalar.copy, e, h * P, (h + 1) * P)
+            first = unit[0][0] * N + unit[0][1] * P
+            quantize(first, first + len(unit) * P)
+            waiting += sorted(unit, key=lambda block: block[1])
+            ready = [blk for blk in waiting if ("words", blk[0] // WORD_EXPERTS) in done and ("scales", blk[0] // SCALE_EXPERTS) in done]
+            for e, h in ready:
+                expert(e, h)
+                waiting.remove((e, h))
+        assert not waiting
+        combine(0)
+        combine(1)

@@ -22,21 +22,17 @@ SILU = mybir.ActivationFunctionType.Silu
 
 LIST_ROWS = 16
 WORD_EXPERTS = 4
-SCALE_EXPERTS = 2
-GATHER_STEPS = [("words", 0, 0), ("words", 1, 0), ("words", 2, 1), ("scales", 0, 2), ("scales", 1, 3), ("scales", 2, 4), ("scales", 3, 6), ("scales", 4, 8), ("scales", 5, 10)]
-VECTOR_COPIES = [(4, 0), (5, 0), (6, 0), (7, 0), (8, 0), (9, 0), (10, 0), (11, 0)]
+SCALE_EXPERTS = 4
 TOKEN_CUTS = [[0,768],[0,512,768]]
-SPLIT = 0
 LINE = 4
-UNITS = [[(0, 0)], [(0, 1), (1, 0)], [(1, 1), (2, 0)], [(2, 1), (3, 0)], [(3, 1), (4, 0)], [(4, 1), (5, 0)], [(5, 1), (6, 0)], [(6, 1), (7, 0)], [(7, 1), (8, 0)], [(8, 1), (9, 0)], [(9, 1), (10, 0)], [(10, 1)], [(11, 0)], [(11, 1)]]
-LOADS = [("offs",), ("words",), ("w", 0, 0, 256), ("scales",), ("w", 1, 0, 256), ("w", 2, 0, 256), ("bias",), ("w", 3, 0, 256), ("w", 4, 0, 256), ("w", 5, 0, 256), ("pos",), ("w", 6, 0, 256), ("w", 7, 0, 256), ("w", 8, 0, 256), ("w", 9, 0, 256), ("w", 10, 0, 256), ("w", 11, 0, 256), ("gate", 0, 0), ("gate", 1, 0), ("gate", 0, 1), ("gate", 1, 1)]
+LOADS = [("offs",), ("words",), ("scales",), ("w", 0, 0, 256), ("w", 1, 0, 256), ("w", 2, 0, 256), ("w", 3, 0, 256), ("w", 4, 0, 256), ("w", 5, 0, 256), ("w", 6, 0, 256), ("w", 7, 0, 256), ("w", 8, 0, 256), ("w", 9, 0, 256), ("bias",), ("w", 10, 0, 128), ("w", 11, 0, 128), ("w", 10, 128, 256), ("w", 11, 128, 256), ("pos",), ("gate", 0, 0), ("gate", 1, 0), ("gate", 0, 1), ("gate", 1, 1)]
 
 
 def tile_moe_pkd_lin_silu_kernel(tc, x_words, x_scales, w, b, gate, offs, pos1, pos2, out):
     nc = tc.nc
     with ExitStack() as ctx:
         keep = ctx.enter_context(tc.tile_pool(name="keep", bufs=1))
-        psum = ctx.enter_context(tc.psum_pool(name="psum", bufs=8))
+        psum = ctx.enter_context(tc.psum_pool(name="psum", bufs=4))
 
         offs_sb = keep.tile([P, S // LIST_ROWS], U16, name="offs_sb")
         pos_sb = [keep.tile([P, T // LIST_ROWS], U16, name="pos%d_sb" % r) for r in range(2)]
@@ -122,31 +118,28 @@ def tile_moe_pkd_lin_silu_kernel(tc, x_words, x_scales, w, b, gate, offs, pos1, 
                 nc.vector.tensor_tensor(result[h][:, a:z], terms[h][0][:, a:z], terms[h][1][:, a:z], ADD)
                 nc.sync.dma_start(out[h * P : (h + 1) * P, a:z], result[h][:, a:z])
 
-        done = set()
-        waiting = []
-        copied = set()
-        for u, unit in enumerate(UNITS):
-            for sort, g, step in GATHER_STEPS:
-                if step == u:
-                    gather(sort, g)
-                    done.add((sort, g))
-            for e, h in unit:
-                if (e, h) in copied:
-                    continue
-                if (e, h) in VECTOR_COPIES:
-                    regroup(nc.vector.tensor_copy, e, h * P, (h + 1) * P)
-                elif h == 0 and e < E - SPLIT:
-                    regroup(nc.scalar.copy, e, 0, N)
-                    copied.add((e, 1))
-                else:
-                    regroup(nc.scalar.copy, e, h * P, (h + 1) * P)
-            first = unit[0][0] * N + unit[0][1] * P
-            quantize(first, first + len(unit) * P)
-            waiting += sorted(unit, key=lambda block: block[1])
-            ready = [blk for blk in waiting if ("words", blk[0] // WORD_EXPERTS) in done and ("scales", blk[0] // SCALE_EXPERTS) in done]
-            for e, h in ready:
-                expert(e, h)
-                waiting.remove((e, h))
-        assert not waiting
+        for g in range(E // WORD_EXPERTS):
+            gather("words", g)
+        for g in range(E // SCALE_EXPERTS):
+            gather("scales", g)
+        late = 2
+        first = 0
+        for e in range(E - late):
+            regroup(nc.vector.tensor_copy if e in (7, 9) else nc.scalar.copy, e, 0, N)
+            if e % 2 == 1 or e >= 6:
+                quantize(first * N, (e + 1) * N)
+                for d in range(first, e + 1):
+                    expert(d, 0)
+                first = e + 1
+        for e in range(E - late, E):
+            regroup(nc.vector.tensor_copy if e == E - 1 else nc.scalar.copy, e, 0, P)
+            quantize(e * N, e * N + P)
+            expert(e, 0)
+        for e in range(E - late):
+            expert(e, 1)
+        for e in range(E - late, E):
+            regroup(nc.vector.tensor_copy, e, P, N)
+            quantize(e * N + P, (e + 1) * N)
+            expert(e, 1)
         combine(0)
         combine(1)

@@ -1,6 +1,7 @@
 from contextlib import ExitStack
 
 import concourse.mybir as mybir
+from concourse.masks import make_identity
 
 K, T, E, C, N = 512, 768, 12, 128, 256
 S = E * C
@@ -21,11 +22,14 @@ ADD = mybir.AluOpType.add
 SILU = mybir.ActivationFunctionType.Silu
 
 LIST_ROWS = 16
-WORD_EXPERTS = 4
-SCALE_EXPERTS = 4
-TOKEN_CUTS = [[0,768],[0,512,768]]
+GATHER_EXPERTS = 4
 LINE = 4
-LOADS = [("offs",), ("words",), ("scales",), ("w", 0, 0, 256), ("w", 1, 0, 256), ("w", 2, 0, 256), ("w", 3, 0, 256), ("w", 4, 0, 256), ("w", 5, 0, 256), ("w", 6, 0, 256), ("w", 7, 0, 256), ("w", 8, 0, 256), ("w", 9, 0, 256), ("bias",), ("w", 10, 0, 128), ("w", 11, 0, 128), ("w", 10, 128, 256), ("w", 11, 128, 256), ("pos",), ("gate", 0, 0), ("gate", 1, 0), ("gate", 0, 1), ("gate", 1, 1)]
+LOAD_GROUPS = (1, 1, 2, 2, 2, 1, 1)
+LATE = 2
+EARLY = E - LATE
+VECTOR_EXPERTS = (7, 9)
+PAIRED = 6
+TOKEN_CUTS = ((0, 384, 768), (0, 576, 768))
 
 
 def tile_moe_pkd_lin_silu_kernel(tc, x_words, x_scales, w, b, gate, offs, pos1, pos2, out):
@@ -33,57 +37,68 @@ def tile_moe_pkd_lin_silu_kernel(tc, x_words, x_scales, w, b, gate, offs, pos1, 
     with ExitStack() as ctx:
         keep = ctx.enter_context(tc.tile_pool(name="keep", bufs=1))
         psum = ctx.enter_context(tc.psum_pool(name="psum", bufs=4))
+        psum_sum = ctx.enter_context(tc.psum_pool(name="psum_sum", bufs=2))
 
+        groups = E // GATHER_EXPERTS
         offs_sb = keep.tile([P, S // LIST_ROWS], U16, name="offs_sb")
         pos_sb = [keep.tile([P, T // LIST_ROWS], U16, name="pos%d_sb" % r) for r in range(2)]
         token_words = keep.tile([P, T], I32, name="token_words", align_bytes=64)
         token_scales = keep.tile([P, T], U8, name="token_scales", align_bytes=64)
-        slot_words = [keep.tile([P, WORD_EXPERTS * C], U32, name="slot_words%d" % g, align_bytes=64) for g in range(E // WORD_EXPERTS)]
-        slot_scales = [keep.tile([P, SCALE_EXPERTS * C], U8, name="slot_scales%d" % g, align_bytes=64) for g in range(E // SCALE_EXPERTS)]
+        slot_words = [keep.tile([P, GATHER_EXPERTS * C], U32, name="slot_words%d" % g, align_bytes=64) for g in range(groups)]
+        slot_scales = [keep.tile([P, GATHER_EXPERTS * C], U8, name="slot_scales%d" % g, align_bytes=64) for g in range(groups)]
         bias = keep.tile([P, HALVES, E], F32, name="bias")
-        w_raw = [keep.tile([P, PACK, N], F32, name="w_raw%d" % e, align_bytes=64) for e in range(E)]
+        w_raw = keep.tile([P, E, PACK, N], F32, name="w_raw", align_bytes=64)
         w_grouped = keep.tile([P, E * N, PACK], BF16, name="w_grouped", align_bytes=64)
         w_words = keep.tile([P, E * N], U32, name="w_words", align_bytes=64)
         w_scales = keep.tile([P, E * N], U8, name="w_scales", align_bytes=64)
-        gates = [[keep.tile([P, T], F32, name="gate%d_%d" % (r, h)) for r in range(2)] for h in range(HALVES)]
+        gates = [keep.tile([P, 2, T], F32, name="gates%d" % h) for h in range(HALVES)]
         y = [keep.tile([P, S], F32, name="y%d" % h) for h in range(HALVES)]
         terms = [[keep.tile([P, T], F32, name="term%d_%d" % (r, h)) for r in range(2)] for h in range(HALVES)]
         result = [keep.tile([P, T], F32, name="result%d" % h) for h in range(HALVES)]
+        turned = keep.tile([P, T], F32, name="turned")
+        identity = keep.tile([P, P], F32, name="identity")
 
         nc.gpsimd.memset(token_scales[:].bitcast(I32), 0)
         warm = keep.tile([P, 2], F32, name="warm")
         nc.gpsimd.memset(warm[:, 0:1], 0.0)
         nc.scalar.activation(warm[:, 1:2], warm[:, 0:1], SILU)
+        make_identity(nc, identity[:])
 
-        for load in LOADS:
-            if load[0] == "offs":
-                nc.sync.dma_start(offs_sb[:], offs)
-            elif load[0] == "words":
-                nc.sync.dma_start(token_words[:], x_words[0].rearrange("p t r -> p (t r)").bitcast(I32))
-            elif load[0] == "scales":
-                for q in range(4):
-                    nc.sync.dma_start(token_scales[32 * q : 32 * q + 4, :].bitcast(I32), x_scales[0, 4 * q : 4 * q + 4, :].bitcast(I32))
-            elif load[0] == "bias":
-                nc.sync.dma_start(bias[:], b.rearrange("(h p) e -> p h e", p=P))
-            elif load[0] == "pos":
-                nc.sync.dma_start(pos_sb[0][:], pos1)
-                nc.sync.dma_start(pos_sb[1][:], pos2)
-            elif load[0] == "gate":
-                r, h = load[1], load[2]
-                nc.sync.dma_start(gates[h][r][:], gate[r, h * P : (h + 1) * P, :])
-            else:
-                e, cols = load[1], slice(load[2], load[3])
-                nc.sync.dma_start(w_raw[e][:, :, cols], w[e].rearrange("(p j) n -> p j n", j=PACK)[:, :, cols])
+        def load_gate(r, h, a, z):
+            nc.sync.dma_start(gates[h][:, r, a:z], gate[r, h * P : (h + 1) * P, a:z])
 
-        def gather(sort, g):
-            tile, window = (slot_words[g], token_words[:].bitcast(U32)) if sort == "words" else (slot_scales[g], token_scales[:])
-            per = tile.shape[1] // LIST_ROWS
-            nc.vector.tensor_copy(tile[:], window.indirect(offs_sb[:, g * per : (g + 1) * per]))
+        nc.sync.dma_start(offs_sb[:], offs)
+        nc.sync.dma_start(token_words[:], x_words[0].rearrange("p t r -> p (t r)").bitcast(I32))
+        for q in range(4):
+            nc.sync.dma_start(token_scales[32 * q : 32 * q + 4, :].bitcast(I32), x_scales[0, 4 * q : 4 * q + 4, :].bitcast(I32))
+        first = 0
+        for count in LOAD_GROUPS:
+            experts = slice(first, first + count)
+            nc.sync.dma_start(
+                w_raw[:, experts, :, :].rearrange("p e j n -> p e (j n)"),
+                w[experts].rearrange("e (p j) n -> p e (j n)", j=PACK),
+            )
+            first += count
+        nc.sync.dma_start(bias[:], b.rearrange("(h p) e -> p h e", p=P))
+        for h in range(HALVES):
+            for e in range(EARLY, E):
+                cols = slice(h * P, (h + 1) * P)
+                nc.sync.dma_start(w_raw[:, e, :, cols], w[e].rearrange("(p j) n -> p j n", j=PACK)[:, :, cols])
+        for a, z in zip(TOKEN_CUTS[0][:-1], TOKEN_CUTS[0][1:]):
+            for r, pos in enumerate((pos1, pos2)):
+                if a == 0:
+                    nc.sync.dma_start(pos_sb[r][:], pos)
+                load_gate(r, 0, a, z)
+        nc.sync.dma_start(gates[1][:], gate[:, P:N, :].rearrange("r p t -> p r t"))
+
+        def entries(g):
+            per = GATHER_EXPERTS * C // LIST_ROWS
+            return offs_sb[:, g * per : (g + 1) * per]
 
         def regroup(copy, e, a, z):
             copy(
                 w_grouped[:, e * N + a : e * N + z, :].rearrange("p (c i) j -> p c j i", i=LINE),
-                w_raw[e][:, :, a:z].rearrange("p j (c i) -> p c j i", i=LINE),
+                w_raw[:, e, :, a:z].rearrange("p j (c i) -> p c j i", i=LINE),
             )
 
         def quantize(a, z):
@@ -95,51 +110,70 @@ def tile_moe_pkd_lin_silu_kernel(tc, x_words, x_scales, w, b, gate, offs, pos1, 
 
         def expert(e, h):
             cols = slice(e * N + h * P, e * N + (h + 1) * P)
-            gw, pw = divmod(e, WORD_EXPERTS)
-            gs, ps = divmod(e, SCALE_EXPERTS)
+            g, place = divmod(e, GATHER_EXPERTS)
+            slots = slice(place * C, (place + 1) * C)
             acc = psum.tile([P, C], F32, name="acc")
             nc.tensor.matmul_mx(
                 out=acc[:],
                 lhsT=w_words[:, cols].bitcast(FP8X4),
                 lhsT_scale=w_scales[:, cols],
-                rhs=slot_words[gw][:, pw * C : (pw + 1) * C].bitcast(FP8X4),
-                rhs_scale=slot_scales[gs][:, ps * C : (ps + 1) * C],
+                rhs=slot_words[g][:, slots].bitcast(FP8X4),
+                rhs_scale=slot_scales[g][:, slots],
                 start=True,
                 stop=True,
             )
             nc.scalar.activation(y[h][:, e * C : (e + 1) * C], acc[:], SILU, bias=bias[:, h, e : e + 1])
 
-        def combine(h):
-            cuts = TOKEN_CUTS[h]
-            for a, z in zip(cuts[:-1], cuts[1:]):
+        def add_on_vector(h, a, z):
+            nc.vector.tensor_tensor(result[h][:, a:z], terms[h][0][:, a:z], terms[h][1][:, a:z], ADD)
+
+        def add_by_transposes(h, a, z):
+            summed = psum_sum.tile([P, z - a], F32, name="summed")
+            for t in range(a, z, P):
+                for r in (1, 0):
+                    nc.tensor.matmul(
+                        summed[:, t - a : t - a + P],
+                        terms[h][r][:, t : t + P],
+                        identity[:],
+                        start=(r == 1),
+                        stop=(r == 0),
+                        is_transpose=True,
+                    )
+            nc.scalar.copy(turned[:, a:z], summed[:])
+            back = psum_sum.tile([P, z - a], F32, name="back")
+            for t in range(a, z, P):
+                nc.tensor.transpose(back[:, t - a : t - a + P], turned[:, t : t + P], identity[:])
+            nc.scalar.copy(result[h][:, a:z], back[:])
+
+        def combine(h, add):
+            for a, z in zip(TOKEN_CUTS[h][:-1], TOKEN_CUTS[h][1:]):
                 for r in range(2):
-                    entries = pos_sb[r][:, a // LIST_ROWS : z // LIST_ROWS]
-                    nc.vector.tensor_tensor(terms[h][r][:, a:z], y[h][:].indirect(entries), gates[h][r][:, a:z], MULT)
-                nc.vector.tensor_tensor(result[h][:, a:z], terms[h][0][:, a:z], terms[h][1][:, a:z], ADD)
+                    picked = y[h][:].indirect(pos_sb[r][:, a // LIST_ROWS : z // LIST_ROWS])
+                    nc.vector.tensor_tensor(terms[h][r][:, a:z], picked, gates[h][:, r, a:z], MULT)
+                add(h, a, z)
                 nc.sync.dma_start(out[h * P : (h + 1) * P, a:z], result[h][:, a:z])
 
-        for g in range(E // WORD_EXPERTS):
-            gather("words", g)
-        for g in range(E // SCALE_EXPERTS):
-            gather("scales", g)
-        late = 2
+        for g in range(groups):
+            nc.vector.tensor_copy(slot_words[g][:], token_words[:].bitcast(U32).indirect(entries(g)))
+        for g in range(groups):
+            nc.vector.tensor_copy(slot_scales[g][:], token_scales[:].indirect(entries(g)))
         first = 0
-        for e in range(E - late):
-            regroup(nc.vector.tensor_copy if e in (7, 9) else nc.scalar.copy, e, 0, N)
-            if e % 2 == 1 or e >= 6:
+        for e in range(EARLY):
+            regroup(nc.vector.tensor_copy if e in VECTOR_EXPERTS else nc.scalar.copy, e, 0, N)
+            if e % 2 == 1 or e >= PAIRED:
                 quantize(first * N, (e + 1) * N)
                 for d in range(first, e + 1):
                     expert(d, 0)
                 first = e + 1
-        for e in range(E - late, E):
+        for e in range(EARLY, E):
             regroup(nc.vector.tensor_copy if e == E - 1 else nc.scalar.copy, e, 0, P)
             quantize(e * N, e * N + P)
             expert(e, 0)
-        for e in range(E - late):
+        for e in range(EARLY):
             expert(e, 1)
-        for e in range(E - late, E):
+        for e in range(EARLY, E):
             regroup(nc.vector.tensor_copy, e, P, N)
             quantize(e * N + P, (e + 1) * N)
             expert(e, 1)
-        combine(0)
-        combine(1)
+        combine(0, add_by_transposes)
+        combine(1, add_on_vector)

@@ -24,20 +24,19 @@ SILU = mybir.ActivationFunctionType.Silu
 LIST_ROWS = 16
 GATHER_EXPERTS = 4
 LINE = 4
-LOAD_GROUPS = (1, 1, 2, 2, 2, 1, 1)
-LATE = 2
-EARLY = E - LATE
-VECTOR_EXPERTS = (7, 9)
+BANK = 512
 PAIRED = 6
-TOKEN_CUTS = ((0, 384, 768), (0, 576, 768))
+EARLY = 9
+BIAS_AFTER = 8
+ON_VECTOR = ((6, 0), (8, 0), (10, 0), (11, 0))
+CUTS = ((0, 256, 512, 768), (0, 256, 512, 768))
 
 
 def tile_moe_pkd_lin_silu_kernel(tc, x_words, x_scales, w, b, gate, offs, pos1, pos2, out):
     nc = tc.nc
     with ExitStack() as ctx:
         keep = ctx.enter_context(tc.tile_pool(name="keep", bufs=1))
-        psum = ctx.enter_context(tc.psum_pool(name="psum", bufs=4))
-        psum_sum = ctx.enter_context(tc.psum_pool(name="psum_sum", bufs=2))
+        psum = ctx.enter_context(tc.psum_pool(name="psum", bufs=1))
 
         groups = E // GATHER_EXPERTS
         offs_sb = keep.tile([P, S // LIST_ROWS], U16, name="offs_sb")
@@ -46,17 +45,31 @@ def tile_moe_pkd_lin_silu_kernel(tc, x_words, x_scales, w, b, gate, offs, pos1, 
         token_scales = keep.tile([P, T], U8, name="token_scales", align_bytes=64)
         slot_words = [keep.tile([P, GATHER_EXPERTS * C], U32, name="slot_words%d" % g, align_bytes=64) for g in range(groups)]
         slot_scales = [keep.tile([P, GATHER_EXPERTS * C], U8, name="slot_scales%d" % g, align_bytes=64) for g in range(groups)]
-        bias = keep.tile([P, HALVES, E], F32, name="bias")
-        w_raw = keep.tile([P, E, PACK, N], F32, name="w_raw", align_bytes=64)
-        w_grouped = keep.tile([P, E * N, PACK], BF16, name="w_grouped", align_bytes=64)
-        w_words = keep.tile([P, E * N], U32, name="w_words", align_bytes=64)
-        w_scales = keep.tile([P, E * N], U8, name="w_scales", align_bytes=64)
-        gates = [keep.tile([P, 2, T], F32, name="gates%d" % h) for h in range(HALVES)]
+        bias = [keep.tile([P, E], F32, name="bias%d" % h) for h in range(HALVES)]
+        gates = keep.tile([P, 2, T], F32, name="gates")
         y = [keep.tile([P, S], F32, name="y%d" % h) for h in range(HALVES)]
-        terms = [[keep.tile([P, T], F32, name="term%d_%d" % (r, h)) for r in range(2)] for h in range(HALVES)]
+        terms = {}
         result = [keep.tile([P, T], F32, name="result%d" % h) for h in range(HALVES)]
-        turned = keep.tile([P, T], F32, name="turned")
         identity = keep.tile([P, P], F32, name="identity")
+        banks = [psum.tile([P, BANK], F32, name="bank%d" % i) for i in range(8)]
+
+        units = [(e, 2, 0, N) for e in range(0, PAIRED, 2)] + [(e, 1, 0, N) for e in range(PAIRED, EARLY)]
+        units += [(e, 1, h * P, P) for h in range(HALVES) for e in range(EARLY, E)]
+        raw, grouped, words, scales = {}, {}, {}, {}
+        for u in units:
+            e, count, col, width = u
+            name = "%d_%d" % (e, col)
+            if count == 2 and e < 2:
+                for d in (e, e + 1):
+                    raw[d, col] = keep.tile([P, PACK, width], F32, name="raw%d_%d" % (d, col), align_bytes=64)[:]
+            else:
+                whole = keep.tile([P, count, PACK, width], F32, name="raw" + name, tag="raw" + name, align_bytes=64)
+                raw[u] = whole
+                for i in range(count):
+                    raw[e + i, col] = whole[:, i]
+            grouped[u] = keep.tile([P, count * width, PACK], BF16, name="grouped" + name, tag="grouped" + name, align_bytes=64)
+            words[u] = keep.tile([P, count * width], U32, name="words" + name, align_bytes=64)
+            scales[u] = keep.tile([P, count * width], U8, name="scales" + name, align_bytes=64)
 
         nc.gpsimd.memset(token_scales[:].bitcast(I32), 0)
         warm = keep.tile([P, 2], F32, name="warm")
@@ -64,116 +77,132 @@ def tile_moe_pkd_lin_silu_kernel(tc, x_words, x_scales, w, b, gate, offs, pos1, 
         nc.scalar.activation(warm[:, 1:2], warm[:, 0:1], SILU)
         make_identity(nc, identity[:])
 
-        def load_gate(r, h, a, z):
-            nc.sync.dma_start(gates[h][:, r, a:z], gate[r, h * P : (h + 1) * P, a:z])
+        def load(u):
+            e, count, col, width = u
+            if width < N:
+                nc.sync.dma_start(raw[e, col], w[e].rearrange("(p j) n -> p j n", j=PACK)[:, :, col : col + width])
+            elif u in raw:
+                nc.sync.dma_start(
+                    raw[u][:].rearrange("p e j n -> p e (j n)"),
+                    w[e : e + count].rearrange("e (p j) n -> p e (j n)", j=PACK),
+                )
+            else:
+                for d in range(e, e + count):
+                    nc.sync.dma_start(raw[d, col].rearrange("p j n -> p (j n)"), w[d].rearrange("(p j) n -> p (j n)", j=PACK))
+
+        def load_bias(h):
+            nc.sync.dma_start(bias[h][:], b[h * P : (h + 1) * P, :])
+
+        def load_gates(a, z):
+            nc.sync.dma_start(gates[:, :, a:z], gate[:, 0:P, a:z].rearrange("r p t -> p r t"))
 
         nc.sync.dma_start(offs_sb[:], offs)
         nc.sync.dma_start(token_words[:], x_words[0].rearrange("p t r -> p (t r)").bitcast(I32))
-        for q in range(4):
-            nc.sync.dma_start(token_scales[32 * q : 32 * q + 4, :].bitcast(I32), x_scales[0, 4 * q : 4 * q + 4, :].bitcast(I32))
-        first = 0
-        for count in LOAD_GROUPS:
-            experts = slice(first, first + count)
-            nc.sync.dma_start(
-                w_raw[:, experts, :, :].rearrange("p e j n -> p e (j n)"),
-                w[experts].rearrange("e (p j) n -> p e (j n)", j=PACK),
-            )
-            first += count
-        nc.sync.dma_start(bias[:], b.rearrange("(h p) e -> p h e", p=P))
-        for h in range(HALVES):
-            for e in range(EARLY, E):
-                cols = slice(h * P, (h + 1) * P)
-                nc.sync.dma_start(w_raw[:, e, :, cols], w[e].rearrange("(p j) n -> p j n", j=PACK)[:, :, cols])
-        for a, z in zip(TOKEN_CUTS[0][:-1], TOKEN_CUTS[0][1:]):
-            for r, pos in enumerate((pos1, pos2)):
-                if a == 0:
-                    nc.sync.dma_start(pos_sb[r][:], pos)
-                load_gate(r, 0, a, z)
-        nc.sync.dma_start(gates[1][:], gate[:, P:N, :].rearrange("r p t -> p r t"))
+        scale_rows = x_scales[0].rearrange("(q r) t -> r q t", r=4)
+        for u in units:
+            load(u)
+            e, count, col, width = u
+            if e == 0:
+                for r in range(4):
+                    nc.sync.dma_start(token_scales[r:P:32, :].bitcast(I32), scale_rows[r].bitcast(I32))
+            if e == 2:
+                nc.sync.dma_start(pos_sb[0][:], pos1)
+            if e == 4:
+                nc.sync.dma_start(pos_sb[1][:], pos2)
+            if e == BIAS_AFTER and col == 0:
+                load_bias(0)
+            if (e, col) == (11, 0):
+                load_gates(0, 512)
+            if (e, col) == (11, 0):
+                load_bias(1)
+        load_gates(512, T)
 
         def entries(g):
             per = GATHER_EXPERTS * C // LIST_ROWS
             return offs_sb[:, g * per : (g + 1) * per]
 
-        def regroup(copy, e, a, z):
-            copy(
-                w_grouped[:, e * N + a : e * N + z, :].rearrange("p (c i) j -> p c j i", i=LINE),
-                w_raw[:, e, :, a:z].rearrange("p j (c i) -> p c j i", i=LINE),
-            )
+        def regroup(u):
+            e, count, col, width = u
+            for i in range(count):
+                copy = nc.vector.tensor_copy if (e + i, col) in ON_VECTOR else nc.scalar.copy
+                copy(
+                    grouped[u][:, i * width : (i + 1) * width, :].rearrange("p (c i) j -> p c j i", i=LINE),
+                    raw[e + i, col].rearrange("p j (c i) -> p c j i", i=LINE),
+                )
 
-        def quantize(a, z):
+        def quantize(u):
             nc.vector.quantize_mx(
-                out=w_words[:, a:z].bitcast(FP8X4),
-                scales=w_scales[:, a:z],
-                in_=w_grouped[:, a:z, :].rearrange("p n j -> p (n j)"),
+                out=words[u][:].bitcast(FP8X4),
+                scales=scales[u][:],
+                in_=grouped[u][:].rearrange("p n j -> p (n j)"),
             )
 
-        def expert(e, h):
-            cols = slice(e * N + h * P, e * N + (h + 1) * P)
-            g, place = divmod(e, GATHER_EXPERTS)
-            slots = slice(place * C, (place + 1) * C)
-            acc = psum.tile([P, C], F32, name="acc")
+        def multiply(e, h, acc):
+            u = [v for v in units if v[0] <= e < v[0] + v[1] and v[2] <= h * P < v[2] + v[3]][0]
+            first = (e - u[0]) * u[3] + h * P - u[2]
+            cols = slice(first, first + P)
+            g, at = divmod(e, GATHER_EXPERTS)
+            slots = slice(at * C, (at + 1) * C)
             nc.tensor.matmul_mx(
-                out=acc[:],
-                lhsT=w_words[:, cols].bitcast(FP8X4),
-                lhsT_scale=w_scales[:, cols],
+                out=acc,
+                lhsT=words[u][:, cols].bitcast(FP8X4),
+                lhsT_scale=scales[u][:, cols],
                 rhs=slot_words[g][:, slots].bitcast(FP8X4),
                 rhs_scale=slot_scales[g][:, slots],
                 start=True,
                 stop=True,
             )
-            nc.scalar.activation(y[h][:, e * C : (e + 1) * C], acc[:], SILU, bias=bias[:, h, e : e + 1])
 
-        def add_on_vector(h, a, z):
-            nc.vector.tensor_tensor(result[h][:, a:z], terms[h][0][:, a:z], terms[h][1][:, a:z], ADD)
+        def experts(first, last, h, bank):
+            for e in range(first, last):
+                multiply(e, h, bank[:, (e - first) * C : (e - first + 1) * C])
+            for e in range(first, last):
+                nc.scalar.activation(
+                    y[h][:, e * C : (e + 1) * C], bank[:, (e - first) * C : (e - first + 1) * C], SILU, bias=bias[h][:, e : e + 1]
+                )
 
-        def add_by_transposes(h, a, z):
-            summed = psum_sum.tile([P, z - a], F32, name="summed")
+        def pick(h, a, z):
+            name = "terms%d_%d" % (h, a)
+            held = h == 0 and z == T
+            terms[h, a] = keep.tile([P, 2, z - a], F32, name=name, tag="raw%d_%d" % (E - 1, P) if held else name, align_bytes=64)
+            for r in range(2):
+                picked = y[h][:].indirect(pos_sb[r][:, a // LIST_ROWS : z // LIST_ROWS])
+                nc.vector.tensor_tensor(terms[h, a][:, r, :], picked, gates[:, r, a:z], MULT)
+
+        def add_by_transposes(h, a, z, summed, turned, back):
             for t in range(a, z, P):
-                for r in (1, 0):
-                    nc.tensor.matmul(
-                        summed[:, t - a : t - a + P],
-                        terms[h][r][:, t : t + P],
-                        identity[:],
-                        start=(r == 1),
-                        stop=(r == 0),
-                        is_transpose=True,
-                    )
-            nc.scalar.copy(turned[:, a:z], summed[:])
-            back = psum_sum.tile([P, z - a], F32, name="back")
-            for t in range(a, z, P):
-                nc.tensor.transpose(back[:, t - a : t - a + P], turned[:, t : t + P], identity[:])
-            nc.scalar.copy(result[h][:, a:z], back[:])
-
-        def combine(h, add):
-            for a, z in zip(TOKEN_CUTS[h][:-1], TOKEN_CUTS[h][1:]):
                 for r in range(2):
-                    picked = y[h][:].indirect(pos_sb[r][:, a // LIST_ROWS : z // LIST_ROWS])
-                    nc.vector.tensor_tensor(terms[h][r][:, a:z], picked, gates[h][:, r, a:z], MULT)
-                add(h, a, z)
-                nc.sync.dma_start(out[h * P : (h + 1) * P, a:z], result[h][:, a:z])
+                    nc.tensor.matmul(
+                        summed[:, t - a : t - a + P], terms[h, a][:, r, t - a : t - a + P], identity[:], start=(r == 0), stop=(r == 1), is_transpose=True
+                    )
+            nc.scalar.copy(turned, summed[:, 0 : z - a])
+            for t in range(a, z, P):
+                nc.tensor.transpose(back[:, t - a : t - a + P], turned[:, t - a : t - a + P], identity[:])
+            nc.scalar.copy(result[h][:, a:z], back[:, 0 : z - a])
+            nc.scalar.dma_start(out[h * P : (h + 1) * P, a:z], result[h][:, a:z])
 
         for g in range(groups):
             nc.vector.tensor_copy(slot_words[g][:], token_words[:].bitcast(U32).indirect(entries(g)))
         for g in range(groups):
             nc.vector.tensor_copy(slot_scales[g][:], token_scales[:].indirect(entries(g)))
-        first = 0
-        for e in range(EARLY):
-            regroup(nc.vector.tensor_copy if e in VECTOR_EXPERTS else nc.scalar.copy, e, 0, N)
-            if e % 2 == 1 or e >= PAIRED:
-                quantize(first * N, (e + 1) * N)
-                for d in range(first, e + 1):
-                    expert(d, 0)
-                first = e + 1
-        for e in range(EARLY, E):
-            regroup(nc.vector.tensor_copy if e == E - 1 else nc.scalar.copy, e, 0, P)
-            quantize(e * N, e * N + P)
-            expert(e, 0)
-        for e in range(EARLY):
-            expert(e, 1)
-        for e in range(EARLY, E):
-            regroup(nc.vector.tensor_copy, e, P, N)
-            quantize(e * N + P, (e + 1) * N)
-            expert(e, 1)
-        combine(0, add_by_transposes)
-        combine(1, add_on_vector)
+        for u in units:
+            regroup(u)
+            quantize(u)
+        ring = [(0, 4)] + [(e, e + 1) for e in range(4, E)]
+        for i, (first, last) in enumerate(ring):
+            experts(first, last, 0, banks[i % 3])
+        for first, last, bank in ((0, 4, 3), (4, 8, 4), (8, 9, 5), (9, 10, 0), (10, 11, 1), (11, 12, 2)):
+            experts(first, last, 1, banks[bank])
+        for i, (a, z) in enumerate(zip(CUTS[0][:-1], CUTS[0][1:])):
+            pick(0, a, z)
+        turned = keep.tile([P, T], F32, name="turned", tag="grouped%d_%d" % (E - 1, P), align_bytes=64)
+        for i, (a, z) in enumerate(zip(CUTS[0][:-1], CUTS[0][1:])):
+            add_by_transposes(0, a, z, banks[(6, 7, 2)[i]], turned[:, a:z], banks[3 + i])
+        for i, (a, z) in enumerate(zip(CUTS[1][:-1], CUTS[1][1:])):
+            pick(1, a, z)
+            if i < 1:
+                turned = keep.tile([P, z - a], F32, name="turned_last%d" % i)
+                add_by_transposes(1, a, z, banks[6 * i], turned[:], banks[1 + 6 * i])
+            else:
+                nc.vector.tensor_tensor(result[1][:, a:z], terms[1, a][:, 0, :], terms[1, a][:, 1, :], ADD)
+                nc.sync.dma_start(out[P:N, a:z], result[1][:, a:z])

@@ -25,11 +25,11 @@ LIST_ROWS = 16
 GATHER_EXPERTS = 4
 LINE = 4
 BANK = 512
-PAIRED = 6
-EARLY = 9
+PAIRED = 10
+EARLY = 8
 BIAS_AFTER = 8
-ON_VECTOR = ((6, 0), (8, 0), (10, 0), (11, 0))
-CUTS = ((0, 256, 512, 768), (0, 256, 512, 768))
+ON_VECTOR = ((8, 0), (9, 0), (10, 0), (11, 0))
+CUTS = ((0, 256, 512, 768), (0, 384, 640, 768))
 
 
 def tile_moe_pkd_lin_silu_kernel(tc, x_words, x_scales, w, b, gate, offs, pos1, pos2, out):
@@ -53,23 +53,20 @@ def tile_moe_pkd_lin_silu_kernel(tc, x_words, x_scales, w, b, gate, offs, pos1, 
         identity = keep.tile([P, P], F32, name="identity")
         banks = [psum.tile([P, BANK], F32, name="bank%d" % i) for i in range(8)]
 
-        units = [(e, 2, 0, N) for e in range(0, PAIRED, 2)] + [(e, 1, 0, N) for e in range(PAIRED, EARLY)]
-        units += [(e, 1, h * P, P) for h in range(HALVES) for e in range(EARLY, E)]
-        raw, grouped, words, scales = {}, {}, {}, {}
+        units = [(e, 2, 0, P) for e in range(0, PAIRED, 2)] + [(e, 1, 0, P) for e in range(PAIRED, E)]
+        held = [(0, 4, P, P), (4, 4, P, P)]
+        units += held + [(e, 1, P, P) for e in range(EARLY, E)]
+        loads = [(e, 0, N) for e in range(EARLY)] + [(e, h * P, P) for h in range(HALVES) for e in range(EARLY, E)]
+        landed, raw, grouped, words, scales = {}, {}, {}, {}, {}
+        for e, col, width in loads:
+            name = "raw%d_%d" % (e, col)
+            landed[e, col] = keep.tile([P, PACK, width], F32, name=name, tag=name, align_bytes=64)
+            for c in range(0, width, P):
+                raw[e, col + c] = landed[e, col][:, :, c : c + P]
         for u in units:
             e, count, col, width = u
-            name = "%d_%d" % (e, col)
-            if count == 2 and e < 2:
-                for d in (e, e + 1):
-                    raw[d, col] = keep.tile([P, PACK, width], F32, name="raw%d_%d" % (d, col), align_bytes=64)[:]
-            else:
-                whole = keep.tile([P, count, PACK, width], F32, name="raw" + name, tag="raw" + name, align_bytes=64)
-                raw[u] = whole
-                for i in range(count):
-                    raw[e + i, col] = whole[:, i]
-            grouped[u] = keep.tile([P, count * width, PACK], BF16, name="grouped" + name, tag="grouped" + name, align_bytes=64)
-            words[u] = keep.tile([P, count * width], U32, name="words" + name, align_bytes=64)
-            scales[u] = keep.tile([P, count * width], U8, name="scales" + name, align_bytes=64)
+            name = "grouped%d_%d" % (e, col)
+            grouped[u] = keep.tile([P, count * width, PACK], BF16, name=name, tag=name, align_bytes=64)
 
         nc.gpsimd.memset(token_scales[:].bitcast(I32), 0)
         warm = keep.tile([P, 2], F32, name="warm")
@@ -77,18 +74,12 @@ def tile_moe_pkd_lin_silu_kernel(tc, x_words, x_scales, w, b, gate, offs, pos1, 
         nc.scalar.activation(warm[:, 1:2], warm[:, 0:1], SILU)
         make_identity(nc, identity[:])
 
-        def load(u):
-            e, count, col, width = u
-            if width < N:
-                nc.sync.dma_start(raw[e, col], w[e].rearrange("(p j) n -> p j n", j=PACK)[:, :, col : col + width])
-            elif u in raw:
-                nc.sync.dma_start(
-                    raw[u][:].rearrange("p e j n -> p e (j n)"),
-                    w[e : e + count].rearrange("e (p j) n -> p e (j n)", j=PACK),
-                )
+        def load(e, col, width):
+            rows = w[e].rearrange("(p j) n -> p j n", j=PACK)
+            if width == N:
+                nc.sync.dma_start(landed[e, col][:].rearrange("p j n -> p (j n)"), rows.rearrange("p j n -> p (j n)"))
             else:
-                for d in range(e, e + count):
-                    nc.sync.dma_start(raw[d, col].rearrange("p j n -> p (j n)"), w[d].rearrange("(p j) n -> p (j n)", j=PACK))
+                nc.sync.dma_start(landed[e, col][:], rows[:, :, col : col + width])
 
         def load_bias(h):
             nc.sync.dma_start(bias[h][:], b[h * P : (h + 1) * P, :])
@@ -99,10 +90,9 @@ def tile_moe_pkd_lin_silu_kernel(tc, x_words, x_scales, w, b, gate, offs, pos1, 
         nc.sync.dma_start(offs_sb[:], offs)
         nc.sync.dma_start(token_words[:], x_words[0].rearrange("p t r -> p (t r)").bitcast(I32))
         scale_rows = x_scales[0].rearrange("(q r) t -> r q t", r=4)
-        for u in units:
-            load(u)
-            e, count, col, width = u
-            if e == 0:
+        for e, col, width in loads:
+            load(e, col, width)
+            if e == 1:
                 for r in range(4):
                     nc.sync.dma_start(token_scales[r:P:32, :].bitcast(I32), scale_rows[r].bitcast(I32))
             if e == 2:
@@ -113,7 +103,7 @@ def tile_moe_pkd_lin_silu_kernel(tc, x_words, x_scales, w, b, gate, offs, pos1, 
                 load_bias(0)
             if (e, col) == (11, 0):
                 load_gates(0, 512)
-            if (e, col) == (11, 0):
+            if (e, col) == (9, 128):
                 load_bias(1)
         load_gates(512, T)
 
@@ -131,6 +121,13 @@ def tile_moe_pkd_lin_silu_kernel(tc, x_words, x_scales, w, b, gate, offs, pos1, 
                 )
 
         def quantize(u):
+            e, count, col, width = u
+            name = "%d_%d" % (e, col)
+            tags = ["words" + name, "scales" + name]
+            if u in held:
+                tags[0] = ("words0_128", "raw11_0")[held.index(u)]
+            words[u] = keep.tile([P, count * width], U32, name="words" + name, tag=tags[0], align_bytes=64)
+            scales[u] = keep.tile([P, count * width], U8, name="scales" + name, tag=tags[1], align_bytes=64)
             nc.vector.quantize_mx(
                 out=words[u][:].bitcast(FP8X4),
                 scales=scales[u][:],
@@ -188,21 +185,20 @@ def tile_moe_pkd_lin_silu_kernel(tc, x_words, x_scales, w, b, gate, offs, pos1, 
         for u in units:
             regroup(u)
             quantize(u)
-        ring = [(0, 4)] + [(e, e + 1) for e in range(4, E)]
-        for i, (first, last) in enumerate(ring):
-            experts(first, last, 0, banks[i % 3])
+        for first, last, bank in ((0, 4, 0), (4, 6, 1), (6, 8, 2), (8, 10, 5), (10, 11, 6), (11, 12, 7)):
+            experts(first, last, 0, banks[bank])
         for first, last, bank in ((0, 4, 3), (4, 8, 4), (8, 9, 5), (9, 10, 0), (10, 11, 1), (11, 12, 2)):
             experts(first, last, 1, banks[bank])
         for i, (a, z) in enumerate(zip(CUTS[0][:-1], CUTS[0][1:])):
             pick(0, a, z)
         turned = keep.tile([P, T], F32, name="turned", tag="grouped%d_%d" % (E - 1, P), align_bytes=64)
         for i, (a, z) in enumerate(zip(CUTS[0][:-1], CUTS[0][1:])):
-            add_by_transposes(0, a, z, banks[(6, 7, 2)[i]], turned[:, a:z], banks[3 + i])
+            add_by_transposes(0, a, z, banks[(1, 2, 6)[i]], turned[:, a:z], banks[3 + i])
         for i, (a, z) in enumerate(zip(CUTS[1][:-1], CUTS[1][1:])):
             pick(1, a, z)
-            if i < 1:
+            if i < 0:
                 turned = keep.tile([P, z - a], F32, name="turned_last%d" % i)
-                add_by_transposes(1, a, z, banks[6 * i], turned[:], banks[1 + 6 * i])
+                add_by_transposes(1, a, z, banks[2 * i], turned[:], banks[1 + 2 * i])
             else:
                 nc.vector.tensor_tensor(result[1][:, a:z], terms[1, a][:, 0, :], terms[1, a][:, 1, :], ADD)
                 nc.sync.dma_start(out[P:N, a:z], result[1][:, a:z])

@@ -19,16 +19,19 @@ U8 = mybir.dt.uint8
 FP8X4 = mybir.dt.float8_e4m3fn_x4
 MULT = mybir.AluOpType.mult
 ADD = mybir.AluOpType.add
+COPY = mybir.ActivationFunctionType.Copy
 SILU = mybir.ActivationFunctionType.Silu
 
 LIST_ROWS = 16
 GATHER_EXPERTS = 4
 LINE = 4
 BANK = 512
+BLOCKS = T // P
 PAIRED = 10
-EARLY = 8
-BIAS_AFTER = 8
-ON_VECTOR = ((8, 0), (9, 0), (10, 0), (11, 0))
+PAIR_TO = 6
+EARLY = 6
+BIAS_AFTER = 7
+ON_VECTOR = ((7, 0), (8, 0), (9, 0), (10, 0), (11, 0), (5, 128), (6, 128), (7, 128), (11, 128))
 CUTS = ((0, 256, 512, 768), (0, 384, 640, 768))
 
 
@@ -45,8 +48,10 @@ def tile_moe_pkd_lin_silu_kernel(tc, x_words, x_scales, w, b, gate, offs, pos1, 
         token_scales = keep.tile([P, T], U8, name="token_scales", align_bytes=64)
         slot_words = [keep.tile([P, GATHER_EXPERTS * C], U32, name="slot_words%d" % g, align_bytes=64) for g in range(groups)]
         slot_scales = [keep.tile([P, GATHER_EXPERTS * C], U8, name="slot_scales%d" % g, align_bytes=64) for g in range(groups)]
-        bias = [keep.tile([P, E], F32, name="bias%d" % h) for h in range(HALVES)]
+        bias = {}
         gates = keep.tile([P, 2, T], F32, name="gates")
+        gate_rows = keep.tile([P, 2, P], F32, name="gate_rows")
+        gate_cols = keep.tile([P, 2, BLOCKS], F32, name="gate_cols")
         y = [keep.tile([P, S], F32, name="y%d" % h) for h in range(HALVES)]
         terms = {}
         result = [keep.tile([P, T], F32, name="result%d" % h) for h in range(HALVES)]
@@ -54,13 +59,19 @@ def tile_moe_pkd_lin_silu_kernel(tc, x_words, x_scales, w, b, gate, offs, pos1, 
         banks = [psum.tile([P, BANK], F32, name="bank%d" % i) for i in range(8)]
 
         units = [(e, 2, 0, P) for e in range(0, PAIRED, 2)] + [(e, 1, 0, P) for e in range(PAIRED, E)]
-        held = [(0, 4, P, P), (4, 4, P, P)]
+        held = [(0, 4, P, P), (4, 2, P, P)]
         units += held + [(e, 1, P, P) for e in range(EARLY, E)]
         loads = [(e, 0, N) for e in range(EARLY)] + [(e, h * P, P) for h in range(HALVES) for e in range(EARLY, E)]
+        both = {}
         landed, raw, grouped, words, scales = {}, {}, {}, {}, {}
         for e, col, width in loads:
             name = "raw%d_%d" % (e, col)
-            landed[e, col] = keep.tile([P, PACK, width], F32, name=name, tag=name, align_bytes=64)
+            if 2 <= e < PAIR_TO:
+                if e % 2 == 0:
+                    both[e] = keep.tile([P, 2, PACK, width], F32, name=name, align_bytes=64)
+                landed[e, col] = both[e - e % 2][:, e % 2]
+            else:
+                landed[e, col] = keep.tile([P, PACK, width], F32, name=name, tag=name, align_bytes=64)[:]
             for c in range(0, width, P):
                 raw[e, col + c] = landed[e, col][:, :, c : c + P]
         for u in units:
@@ -73,39 +84,51 @@ def tile_moe_pkd_lin_silu_kernel(tc, x_words, x_scales, w, b, gate, offs, pos1, 
         nc.gpsimd.memset(warm[:, 0:1], 0.0)
         nc.scalar.activation(warm[:, 1:2], warm[:, 0:1], SILU)
         make_identity(nc, identity[:])
+        nc.gpsimd.memset(gate_rows[:], 0.0)
 
         def load(e, col, width):
             rows = w[e].rearrange("(p j) n -> p j n", j=PACK)
-            if width == N:
-                nc.sync.dma_start(landed[e, col][:].rearrange("p j n -> p (j n)"), rows.rearrange("p j n -> p (j n)"))
+            if 2 <= e < PAIR_TO:
+                if e % 2 == 0:
+                    nc.sync.dma_start(
+                        both[e][:].rearrange("p e j n -> p e (j n)"),
+                        w[e : e + 2].rearrange("e (p j) n -> p e (j n)", j=PACK),
+                    )
+            elif width == N:
+                nc.sync.dma_start(landed[e, col].rearrange("p j n -> p (j n)"), rows.rearrange("p j n -> p (j n)"))
             else:
-                nc.sync.dma_start(landed[e, col][:], rows[:, :, col : col + width])
+                nc.sync.dma_start(landed[e, col], rows[:, :, col : col + width])
 
-        def load_bias(h):
-            nc.sync.dma_start(bias[h][:], b[h * P : (h + 1) * P, :])
+        def load_bias(h, first, last):
+            for e in range(first, last):
+                bias[h, e] = (first, keep.tile([P, last - first], F32, name="bias%d_%d" % (h, first))) if e == first else bias[h, first]
+            nc.sync.dma_start(bias[h, first][1][:], b[h * P : (h + 1) * P, first:last])
 
         def load_gates(a, z):
             nc.sync.dma_start(gates[:, :, a:z], gate[:, 0:P, a:z].rearrange("r p t -> p r t"))
 
-        nc.sync.dma_start(offs_sb[:], offs)
         nc.sync.dma_start(token_words[:], x_words[0].rearrange("p t r -> p (t r)").bitcast(I32))
+        nc.sync.dma_start(offs_sb[:], offs)
         scale_rows = x_scales[0].rearrange("(q r) t -> r q t", r=4)
         for e, col, width in loads:
             load(e, col, width)
             if e == 1:
                 for r in range(4):
                     nc.sync.dma_start(token_scales[r:P:32, :].bitcast(I32), scale_rows[r].bitcast(I32))
-            if e == 2:
-                nc.sync.dma_start(pos_sb[0][:], pos1)
-            if e == 4:
-                nc.sync.dma_start(pos_sb[1][:], pos2)
             if e == BIAS_AFTER and col == 0:
-                load_bias(0)
-            if (e, col) == (11, 0):
-                load_gates(0, 512)
-            if (e, col) == (9, 128):
-                load_bias(1)
-        load_gates(512, T)
+                load_bias(0, 0, E)
+            if (e, col) == (2, 0):
+                nc.sync.dma_start(pos_sb[0][:], pos1)
+            if (e, col) == (3, 0):
+                nc.sync.dma_start(pos_sb[1][:], pos2)
+            if (e, col) == (7, 0):
+                load_bias(1, 0, EARLY)
+            if (e, col) == (0, 0):
+                nc.sync.dma_start(gate_rows[0:BLOCKS, :, :], gate[:, 0, :].rearrange("r (j p) -> j r p", p=P))
+            if (e, col) == (10, 128):
+                load_bias(1, EARLY, E)
+        for a, z in ((0, 384), (384, 768)):
+            load_gates(a, z)
 
         def entries(g):
             per = GATHER_EXPERTS * C // LIST_ROWS
@@ -125,7 +148,7 @@ def tile_moe_pkd_lin_silu_kernel(tc, x_words, x_scales, w, b, gate, offs, pos1, 
             name = "%d_%d" % (e, col)
             tags = ["words" + name, "scales" + name]
             if u in held:
-                tags[0] = ("words0_128", "raw11_0")[held.index(u)]
+                tags[0] = ("h0", "raw11_0")[held.index(u)]
             words[u] = keep.tile([P, count * width], U32, name="words" + name, tag=tags[0], align_bytes=64)
             scales[u] = keep.tile([P, count * width], U8, name="scales" + name, tag=tags[1], align_bytes=64)
             nc.vector.quantize_mx(
@@ -155,7 +178,7 @@ def tile_moe_pkd_lin_silu_kernel(tc, x_words, x_scales, w, b, gate, offs, pos1, 
                 multiply(e, h, bank[:, (e - first) * C : (e - first + 1) * C])
             for e in range(first, last):
                 nc.scalar.activation(
-                    y[h][:, e * C : (e + 1) * C], bank[:, (e - first) * C : (e - first + 1) * C], SILU, bias=bias[h][:, e : e + 1]
+                    y[h][:, e * C : (e + 1) * C], bank[:, (e - first) * C : (e - first + 1) * C], SILU, bias=bias[h, e][1][:, e - bias[h, e][0] : e - bias[h, e][0] + 1]
                 )
 
         def pick(h, a, z):
@@ -164,7 +187,10 @@ def tile_moe_pkd_lin_silu_kernel(tc, x_words, x_scales, w, b, gate, offs, pos1, 
             terms[h, a] = keep.tile([P, 2, z - a], F32, name=name, tag="raw%d_%d" % (E - 1, P) if held else name, align_bytes=64)
             for r in range(2):
                 picked = y[h][:].indirect(pos_sb[r][:, a // LIST_ROWS : z // LIST_ROWS])
-                nc.vector.tensor_tensor(terms[h, a][:, r, :], picked, gates[:, r, a:z], MULT)
+                if h == 0:
+                    nc.vector.tensor_copy(terms[h, a][:, r, :], picked)
+                else:
+                    nc.vector.tensor_tensor(terms[h, a][:, r, :], picked, gates[:, r, a:z], MULT)
 
         def add_by_transposes(h, a, z, summed, turned, back):
             for t in range(a, z, P):
@@ -178,6 +204,28 @@ def tile_moe_pkd_lin_silu_kernel(tc, x_words, x_scales, w, b, gate, offs, pos1, 
             nc.scalar.copy(result[h][:, a:z], back[:, 0 : z - a])
             nc.scalar.dma_start(out[h * P : (h + 1) * P, a:z], result[h][:, a:z])
 
+        def weigh_turned(a, z, turned, scaled, back):
+            width = z - a
+            for r in range(2):
+                for t in range(0, width, P):
+                    nc.tensor.transpose(turned[:, r * width + t : r * width + t + P], terms[0, a][:, r, t : t + P], identity[:])
+            for t in range(0, width, P):
+                for r in range(2):
+                    j = (a + t) // P
+                    nc.scalar.activation(
+                        scaled[:, r, a + t : a + t + P], turned[:, r * width + t : r * width + t + P], COPY, scale=gate_cols[:, r, j : j + 1]
+                    )
+            for t in range(0, width, P):
+                for r in range(2):
+                    nc.tensor.matmul(
+                        back[:, t : t + P], scaled[:, r, a + t : a + t + P], identity[:], start=(r == 0), stop=(r == 1), is_transpose=True
+                    )
+            nc.scalar.copy(result[0][:, a:z], back[:, 0:width])
+            nc.scalar.dma_start(out[0:P, a:z], result[0][:, a:z])
+
+        for r in range(2):
+            nc.tensor.transpose(banks[7][:, r * P : (r + 1) * P], gate_rows[:, r, :], identity[:])
+        nc.scalar.copy(gate_cols[:], banks[7][:, 0 : 2 * P].rearrange("p (r q) -> p r q", r=2)[:, :, 0:BLOCKS])
         for g in range(groups):
             nc.vector.tensor_copy(slot_words[g][:], token_words[:].bitcast(U32).indirect(entries(g)))
         for g in range(groups):
@@ -187,13 +235,13 @@ def tile_moe_pkd_lin_silu_kernel(tc, x_words, x_scales, w, b, gate, offs, pos1, 
             quantize(u)
         for first, last, bank in ((0, 4, 0), (4, 6, 1), (6, 8, 2), (8, 10, 5), (10, 11, 6), (11, 12, 7)):
             experts(first, last, 0, banks[bank])
-        for first, last, bank in ((0, 4, 3), (4, 8, 4), (8, 9, 5), (9, 10, 0), (10, 11, 1), (11, 12, 2)):
+        for first, last, bank in ((0, 4, 3), (4, 6, 4), (6, 8, 0), (8, 9, 1), (9, 10, 2), (10, 11, 5), (11, 12, 0)):
             experts(first, last, 1, banks[bank])
         for i, (a, z) in enumerate(zip(CUTS[0][:-1], CUTS[0][1:])):
             pick(0, a, z)
-        turned = keep.tile([P, T], F32, name="turned", tag="grouped%d_%d" % (E - 1, P), align_bytes=64)
+        scaled = keep.tile([P, 2, T], F32, name="scaled", tag="words%d_%d" % (E - 1, P), align_bytes=64)
         for i, (a, z) in enumerate(zip(CUTS[0][:-1], CUTS[0][1:])):
-            add_by_transposes(0, a, z, banks[(1, 2, 6)[i]], turned[:, a:z], banks[3 + i])
+            weigh_turned(a, z, banks[(6, 7, 1)[i]], scaled, banks[(3, 4, 2)[i]])
         for i, (a, z) in enumerate(zip(CUTS[1][:-1], CUTS[1][1:])):
             pick(1, a, z)
             if i < 0:

@@ -27,12 +27,13 @@ GATHER_EXPERTS = 4
 LINE = 4
 BANK = 512
 BLOCKS = T // P
-PAIRED = 10
-PAIR_TO = 6
+LAST = E - 1
 EARLY = 6
-BIAS_AFTER = 7
-ON_VECTOR = ((7, 0), (8, 0), (9, 0), (10, 0), (11, 0), (5, 128), (6, 128), (7, 128), (11, 128))
-CUTS = ((0, 256, 512, 768), (0, 384, 640, 768))
+SINGLE = 2
+VECTOR_SECOND = 2
+BIAS_AFTER = EARLY + 1
+FIRST_PIECE = 2 * P
+SECOND_CUTS = (0, 3 * P, 5 * P, T)
 
 
 def tile_moe_pkd_lin_silu_kernel(tc, x_words, x_scales, w, b, gate, offs, pos1, pos2, out):
@@ -48,36 +49,32 @@ def tile_moe_pkd_lin_silu_kernel(tc, x_words, x_scales, w, b, gate, offs, pos1, 
         token_scales = keep.tile([P, T], U8, name="token_scales", align_bytes=64)
         slot_words = [keep.tile([P, GATHER_EXPERTS * C], U32, name="slot_words%d" % g, align_bytes=64) for g in range(groups)]
         slot_scales = [keep.tile([P, GATHER_EXPERTS * C], U8, name="slot_scales%d" % g, align_bytes=64) for g in range(groups)]
-        bias = {}
         gates = keep.tile([P, 2, T], F32, name="gates")
         gate_rows = keep.tile([P, 2, P], F32, name="gate_rows")
         gate_cols = keep.tile([P, 2, BLOCKS], F32, name="gate_cols")
         y = [keep.tile([P, S], F32, name="y%d" % h) for h in range(HALVES)]
-        terms = {}
         result = [keep.tile([P, T], F32, name="result%d" % h) for h in range(HALVES)]
         identity = keep.tile([P, P], F32, name="identity")
         banks = [psum.tile([P, BANK], F32, name="bank%d" % i) for i in range(8)]
 
-        units = [(e, 2, 0, P) for e in range(0, PAIRED, 2)] + [(e, 1, 0, P) for e in range(PAIRED, E)]
-        held = [(0, 4, P, P), (4, 2, P, P)]
-        units += held + [(e, 1, P, P) for e in range(EARLY, E)]
-        loads = [(e, 0, N) for e in range(EARLY)] + [(e, h * P, P) for h in range(HALVES) for e in range(EARLY, E)]
-        both = {}
-        landed, raw, grouped, words, scales = {}, {}, {}, {}, {}
-        for e, col, width in loads:
-            name = "raw%d_%d" % (e, col)
-            if 2 <= e < PAIR_TO:
-                if e % 2 == 0:
-                    both[e] = keep.tile([P, 2, PACK, width], F32, name=name, align_bytes=64)
-                landed[e, col] = both[e - e % 2][:, e % 2]
-            else:
-                landed[e, col] = keep.tile([P, PACK, width], F32, name=name, tag=name, align_bytes=64)[:]
-            for c in range(0, width, P):
-                raw[e, col + c] = landed[e, col][:, :, c : c + P]
-        for u in units:
-            e, count, col, width = u
-            name = "grouped%d_%d" % (e, col)
-            grouped[u] = keep.tile([P, count * width, PACK], BF16, name=name, tag=name, align_bytes=64)
+        first_units = [(e, 2, 0) for e in range(0, E - 2, 2)] + [(e, 1, 0) for e in range(E - 2, E)]
+        filler_unit = (GATHER_EXPERTS, EARLY - GATHER_EXPERTS, 1)
+        second_units = [(0, GATHER_EXPERTS, 1), filler_unit] + [(e, 1, 1) for e in range(EARLY, E)]
+        units = first_units + second_units
+        loads = [(e, 1, None) for e in range(SINGLE)] + [(e, 2, None) for e in range(SINGLE, EARLY, 2)]
+        loads += [(e, 1, h) for h in range(HALVES) for e in range(EARLY, E)]
+
+        landed, raw, grouped, words, scales, bias = {}, {}, {}, {}, {}, {}
+        for e, count, h in loads:
+            name = "raw%d_%s" % (e, h)
+            landed[e, h] = keep.tile([P, count, PACK, N if h is None else P], F32, name=name, tag=name, align_bytes=64)
+            for i in range(count):
+                for half in range(HALVES) if h is None else (h,):
+                    first = half * P if h is None else 0
+                    raw[e + i, half] = landed[e, h][:, i, :, first : first + P]
+        for unit in units:
+            e, count, h = unit
+            grouped[unit] = keep.tile([P, count * P, PACK], BF16, name="grouped%d_%d" % (e, h), align_bytes=64)
 
         nc.gpsimd.memset(token_scales[:].bitcast(I32), 0)
         warm = keep.tile([P, 2], F32, name="warm")
@@ -86,167 +83,144 @@ def tile_moe_pkd_lin_silu_kernel(tc, x_words, x_scales, w, b, gate, offs, pos1, 
         make_identity(nc, identity[:])
         nc.gpsimd.memset(gate_rows[:], 0.0)
 
-        def load(e, col, width):
-            rows = w[e].rearrange("(p j) n -> p j n", j=PACK)
-            if 2 <= e < PAIR_TO:
-                if e % 2 == 0:
-                    nc.sync.dma_start(
-                        both[e][:].rearrange("p e j n -> p e (j n)"),
-                        w[e : e + 2].rearrange("e (p j) n -> p e (j n)", j=PACK),
-                    )
-            elif width == N:
-                nc.sync.dma_start(landed[e, col].rearrange("p j n -> p (j n)"), rows.rearrange("p j n -> p (j n)"))
+        def load_weights(e, count, h):
+            if h is None:
+                nc.sync.dma_start(
+                    landed[e, h][:].rearrange("p e j n -> p e (j n)"),
+                    w[e : e + count].rearrange("e (p j) n -> p e (j n)", j=PACK),
+                )
             else:
-                nc.sync.dma_start(landed[e, col], rows[:, :, col : col + width])
+                nc.sync.dma_start(landed[e, h][:, 0], w[e].rearrange("(p j) n -> p j n", j=PACK)[:, :, h * P : (h + 1) * P])
 
         def load_bias(h, first, last):
+            columns = keep.tile([P, last - first], F32, name="bias%d_%d" % (h, first))
+            nc.sync.dma_start(columns[:], b[h * P : (h + 1) * P, first:last])
             for e in range(first, last):
-                bias[h, e] = (first, keep.tile([P, last - first], F32, name="bias%d_%d" % (h, first))) if e == first else bias[h, first]
-            nc.sync.dma_start(bias[h, first][1][:], b[h * P : (h + 1) * P, first:last])
-
-        def load_gates(a, z):
-            nc.sync.dma_start(gates[:, :, a:z], gate[:, 0:P, a:z].rearrange("r p t -> p r t"))
+                bias[e, h] = columns[:, e - first : e - first + 1]
 
         nc.sync.dma_start(token_words[:], x_words[0].rearrange("p t r -> p (t r)").bitcast(I32))
         nc.sync.dma_start(offs_sb[:], offs)
         scale_rows = x_scales[0].rearrange("(q r) t -> r q t", r=4)
-        for e, col, width in loads:
-            load(e, col, width)
-            if e == 1:
+        for e, count, h in loads:
+            load_weights(e, count, h)
+            if e == 0:
+                nc.sync.dma_start(gate_rows[0:BLOCKS, :, :], gate[:, 0, :].rearrange("r (j p) -> j r p", p=P))
+            if e == SINGLE - 1:
                 for r in range(4):
                     nc.sync.dma_start(token_scales[r:P:32, :].bitcast(I32), scale_rows[r].bitcast(I32))
-            if e == BIAS_AFTER and col == 0:
-                load_bias(0, 0, E)
-            if (e, col) == (2, 0):
+            if e == SINGLE:
                 nc.sync.dma_start(pos_sb[0][:], pos1)
-            if (e, col) == (3, 0):
                 nc.sync.dma_start(pos_sb[1][:], pos2)
-            if (e, col) == (7, 0):
+            if (e, h) == (BIAS_AFTER, 0):
+                load_bias(0, 0, E)
                 load_bias(1, 0, EARLY)
-            if (e, col) == (0, 0):
-                nc.sync.dma_start(gate_rows[0:BLOCKS, :, :], gate[:, 0, :].rearrange("r (j p) -> j r p", p=P))
-            if (e, col) == (10, 128):
-                load_bias(1, EARLY, E)
-        for a, z in ((0, 384), (384, 768)):
-            load_gates(a, z)
+        load_bias(1, EARLY, E)
+        for a, z in ((0, SECOND_CUTS[1]), (SECOND_CUTS[1], T)):
+            nc.sync.dma_start(gates[:, :, a:z], gate[:, 0:P, a:z].rearrange("r p t -> p r t"))
 
         def entries(g):
             per = GATHER_EXPERTS * C // LIST_ROWS
             return offs_sb[:, g * per : (g + 1) * per]
 
-        def regroup(u):
-            e, count, col, width = u
+        def regroup(unit):
+            first, count, h = unit
             for i in range(count):
-                copy = nc.vector.tensor_copy if (e + i, col) in ON_VECTOR else nc.scalar.copy
+                e = first + i
+                on_vector = EARLY <= e < (E if h == 0 else EARLY + VECTOR_SECOND)
+                copy = nc.vector.tensor_copy if on_vector else nc.scalar.copy
                 copy(
-                    grouped[u][:, i * width : (i + 1) * width, :].rearrange("p (c i) j -> p c j i", i=LINE),
-                    raw[e + i, col].rearrange("p j (c i) -> p c j i", i=LINE),
+                    grouped[unit][:, i * P : (i + 1) * P, :].rearrange("p (c i) j -> p c j i", i=LINE),
+                    raw[e, h].rearrange("p j (c i) -> p c j i", i=LINE),
                 )
 
-        def quantize(u):
-            e, count, col, width = u
-            name = "%d_%d" % (e, col)
-            tags = ["words" + name, "scales" + name]
-            if u in held:
-                tags[0] = ("h0", "raw11_0")[held.index(u)]
-            words[u] = keep.tile([P, count * width], U32, name="words" + name, tag=tags[0], align_bytes=64)
-            scales[u] = keep.tile([P, count * width], U8, name="scales" + name, tag=tags[1], align_bytes=64)
+        def quantize(unit):
+            first, count, h = unit
+            tag = "raw%d_0" % LAST if unit == filler_unit else "words%d_%d" % (first, h)
+            words[unit] = keep.tile([P, count * P], U32, name="words%d_%d" % (first, h), tag=tag, align_bytes=64)
+            scales[unit] = keep.tile([P, count * P], U8, name="scales%d_%d" % (first, h), align_bytes=64)
             nc.vector.quantize_mx(
-                out=words[u][:].bitcast(FP8X4),
-                scales=scales[u][:],
-                in_=grouped[u][:].rearrange("p n j -> p (n j)"),
+                out=words[unit][:].bitcast(FP8X4),
+                scales=scales[unit][:],
+                in_=grouped[unit][:].rearrange("p n j -> p (n j)"),
             )
 
         def multiply(e, h, acc):
-            u = [v for v in units if v[0] <= e < v[0] + v[1] and v[2] <= h * P < v[2] + v[3]][0]
-            first = (e - u[0]) * u[3] + h * P - u[2]
-            cols = slice(first, first + P)
-            g, at = divmod(e, GATHER_EXPERTS)
-            slots = slice(at * C, (at + 1) * C)
+            unit = [u for u in units if u[2] == h and u[0] <= e < u[0] + u[1]][0]
+            cols = slice((e - unit[0]) * P, (e - unit[0] + 1) * P)
+            g, place = divmod(e, GATHER_EXPERTS)
+            slots = slice(place * C, (place + 1) * C)
             nc.tensor.matmul_mx(
                 out=acc,
-                lhsT=words[u][:, cols].bitcast(FP8X4),
-                lhsT_scale=scales[u][:, cols],
+                lhsT=words[unit][:, cols].bitcast(FP8X4),
+                lhsT_scale=scales[unit][:, cols],
                 rhs=slot_words[g][:, slots].bitcast(FP8X4),
                 rhs_scale=slot_scales[g][:, slots],
                 start=True,
                 stop=True,
             )
 
-        def experts(first, last, h, bank):
-            for e in range(first, last):
-                multiply(e, h, bank[:, (e - first) * C : (e - first + 1) * C])
-            for e in range(first, last):
-                nc.scalar.activation(
-                    y[h][:, e * C : (e + 1) * C], bank[:, (e - first) * C : (e - first + 1) * C], SILU, bias=bias[h, e][1][:, e - bias[h, e][0] : e - bias[h, e][0] + 1]
-                )
+        def experts(first, count, h, bank):
+            for i in range(count):
+                multiply(first + i, h, bank[:, i * C : (i + 1) * C])
+            for i in range(count):
+                e = first + i
+                nc.scalar.activation(y[h][:, e * C : (e + 1) * C], bank[:, i * C : (i + 1) * C], SILU, bias=bias[e, h])
 
-        def pick(h, a, z):
-            name = "terms%d_%d" % (h, a)
-            held = h == 0 and z == T
-            terms[h, a] = keep.tile([P, 2, z - a], F32, name=name, tag="raw%d_%d" % (E - 1, P) if held else name, align_bytes=64)
+        def fetched(h, r, a, z):
+            return y[h][:].indirect(pos_sb[r][:, a // LIST_ROWS : z // LIST_ROWS])
+
+        def weigh_turned(values, a, turned, scaled, back):
+            starts = range(0, FIRST_PIECE, P)
             for r in range(2):
-                picked = y[h][:].indirect(pos_sb[r][:, a // LIST_ROWS : z // LIST_ROWS])
-                if h == 0:
-                    nc.vector.tensor_copy(terms[h, a][:, r, :], picked)
-                else:
-                    nc.vector.tensor_tensor(terms[h, a][:, r, :], picked, gates[:, r, a:z], MULT)
-
-        def add_by_transposes(h, a, z, summed, turned, back):
-            for t in range(a, z, P):
+                for t in starts:
+                    at = r * FIRST_PIECE + t
+                    nc.tensor.transpose(turned[:, at : at + P], values[:, r, t : t + P], identity[:])
+            for t in starts:
                 for r in range(2):
-                    nc.tensor.matmul(
-                        summed[:, t - a : t - a + P], terms[h, a][:, r, t - a : t - a + P], identity[:], start=(r == 0), stop=(r == 1), is_transpose=True
-                    )
-            nc.scalar.copy(turned, summed[:, 0 : z - a])
-            for t in range(a, z, P):
-                nc.tensor.transpose(back[:, t - a : t - a + P], turned[:, t - a : t - a + P], identity[:])
-            nc.scalar.copy(result[h][:, a:z], back[:, 0 : z - a])
-            nc.scalar.dma_start(out[h * P : (h + 1) * P, a:z], result[h][:, a:z])
-
-        def weigh_turned(a, z, turned, scaled, back):
-            width = z - a
-            for r in range(2):
-                for t in range(0, width, P):
-                    nc.tensor.transpose(turned[:, r * width + t : r * width + t + P], terms[0, a][:, r, t : t + P], identity[:])
-            for t in range(0, width, P):
-                for r in range(2):
+                    at = r * FIRST_PIECE + t
                     j = (a + t) // P
-                    nc.scalar.activation(
-                        scaled[:, r, a + t : a + t + P], turned[:, r * width + t : r * width + t + P], COPY, scale=gate_cols[:, r, j : j + 1]
-                    )
-            for t in range(0, width, P):
+                    nc.scalar.activation(scaled[:, r, a + t : a + t + P], turned[:, at : at + P], COPY, scale=gate_cols[:, r, j : j + 1])
+            for t in starts:
                 for r in range(2):
                     nc.tensor.matmul(
                         back[:, t : t + P], scaled[:, r, a + t : a + t + P], identity[:], start=(r == 0), stop=(r == 1), is_transpose=True
                     )
-            nc.scalar.copy(result[0][:, a:z], back[:, 0:width])
-            nc.scalar.dma_start(out[0:P, a:z], result[0][:, a:z])
+            nc.scalar.copy(result[0][:, a : a + FIRST_PIECE], back[:, 0:FIRST_PIECE])
+            nc.scalar.dma_start(out[0:P, a : a + FIRST_PIECE], result[0][:, a : a + FIRST_PIECE])
 
         for r in range(2):
             nc.tensor.transpose(banks[7][:, r * P : (r + 1) * P], gate_rows[:, r, :], identity[:])
         nc.scalar.copy(gate_cols[:], banks[7][:, 0 : 2 * P].rearrange("p (r q) -> p r q", r=2)[:, :, 0:BLOCKS])
+
         for g in range(groups):
             nc.vector.tensor_copy(slot_words[g][:], token_words[:].bitcast(U32).indirect(entries(g)))
         for g in range(groups):
             nc.vector.tensor_copy(slot_scales[g][:], token_scales[:].indirect(entries(g)))
-        for u in units:
-            regroup(u)
-            quantize(u)
-        for first, last, bank in ((0, 4, 0), (4, 6, 1), (6, 8, 2), (8, 10, 5), (10, 11, 6), (11, 12, 7)):
-            experts(first, last, 0, banks[bank])
-        for first, last, bank in ((0, 4, 3), (4, 6, 4), (6, 8, 0), (8, 9, 1), (9, 10, 2), (10, 11, 5), (11, 12, 0)):
-            experts(first, last, 1, banks[bank])
-        for i, (a, z) in enumerate(zip(CUTS[0][:-1], CUTS[0][1:])):
-            pick(0, a, z)
-        scaled = keep.tile([P, 2, T], F32, name="scaled", tag="words%d_%d" % (E - 1, P), align_bytes=64)
-        for i, (a, z) in enumerate(zip(CUTS[0][:-1], CUTS[0][1:])):
-            weigh_turned(a, z, banks[(6, 7, 1)[i]], scaled, banks[(3, 4, 2)[i]])
-        for i, (a, z) in enumerate(zip(CUTS[1][:-1], CUTS[1][1:])):
-            pick(1, a, z)
-            if i < 0:
-                turned = keep.tile([P, z - a], F32, name="turned_last%d" % i)
-                add_by_transposes(1, a, z, banks[2 * i], turned[:], banks[1 + 2 * i])
-            else:
-                nc.vector.tensor_tensor(result[1][:, a:z], terms[1, a][:, 0, :], terms[1, a][:, 1, :], ADD)
-                nc.sync.dma_start(out[P:N, a:z], result[1][:, a:z])
+        for unit in units:
+            regroup(unit)
+            quantize(unit)
+
+        first_runs = [(0, GATHER_EXPERTS)] + [u[:2] for u in first_units[GATHER_EXPERTS // 2 :]]
+        for (first, count), bank in zip(first_runs, (0, 1, 2, 5, 6, 7)):
+            experts(first, count, 0, banks[bank])
+        second_runs = [u[:2] for u in second_units[:2]] + [(EARLY, VECTOR_SECOND)] + [(e, 1) for e in range(EARLY + VECTOR_SECOND, E)]
+        for (first, count), bank in zip(second_runs, (3, 4, 0, 1, 2, 5, 0)):
+            experts(first, count, 1, banks[bank])
+
+        pieces = []
+        for a in range(0, T, FIRST_PIECE):
+            tag = "raw%d_1" % LAST if a + FIRST_PIECE == T else "values%d" % a
+            values = keep.tile([P, 2, FIRST_PIECE], F32, name="values%d" % a, tag=tag, align_bytes=64)
+            for r in range(2):
+                nc.vector.tensor_copy(values[:, r, :], fetched(0, r, a, a + FIRST_PIECE))
+            pieces.append((values, a))
+        scaled = keep.tile([P, 2, T], F32, name="scaled", tag="words%d_1" % LAST, align_bytes=64)
+        for (values, a), turned, back in zip(pieces, (6, 7, 1), (3, 4, 2)):
+            weigh_turned(values, a, banks[turned], scaled, banks[back])
+
+        for a, z in zip(SECOND_CUTS[:-1], SECOND_CUTS[1:]):
+            terms = keep.tile([P, 2, z - a], F32, name="terms%d" % a, align_bytes=64)
+            for r in range(2):
+                nc.vector.tensor_tensor(terms[:, r, :], fetched(1, r, a, z), gates[:, r, a:z], MULT)
+            nc.vector.tensor_tensor(result[1][:, a:z], terms[:, 0, :], terms[:, 1, :], ADD)
+            nc.sync.dma_start(out[P:N, a:z], result[1][:, a:z])

@@ -31,6 +31,23 @@ LAST = E - 1
 EARLY = 6
 SINGLE = 2
 VECTOR_SECOND = 2
+VECTOR_LAST = 0
+POS_AT = (SINGLE, None)
+ONE_BIAS = 0
+HOLD = 2
+HOLD_TAG0 = "same"
+HOLD_TAG = "raw11_1"
+TURNED = (6, 5, 0)
+BACK = (3, 4, 7)
+SBANKS = (3, 4, 0, 1, 2, 5, 0, 1)
+GATE_AT = 0
+EARLY_LOADS = ((0, 1), (1, 1), (2, 2), (4, 2))
+SCALES_AT = 1
+Q_HOLD = 8
+BSPLIT = 6
+EXTRA_V = ()
+Q_TAG = "words8_1"
+SCALED_TAG = "words11_1"
 BIAS_AFTER = EARLY + 1
 FIRST_PIECE = 2 * P
 SECOND_CUTS = (0, 3 * P, 5 * P, T)
@@ -58,10 +75,10 @@ def tile_moe_pkd_lin_silu_kernel(tc, x_words, x_scales, w, b, gate, offs, pos1, 
         banks = [psum.tile([P, BANK], F32, name="bank%d" % i) for i in range(8)]
 
         first_units = [(e, 2, 0) for e in range(0, E - 2, 2)] + [(e, 1, 0) for e in range(E - 2, E)]
-        filler_unit = (GATHER_EXPERTS, EARLY - GATHER_EXPERTS, 1)
-        second_units = [(0, GATHER_EXPERTS, 1), filler_unit] + [(e, 1, 1) for e in range(EARLY, E)]
+        filler_unit = (GATHER_EXPERTS, 2, 1)
+        second_units = [(0, GATHER_EXPERTS, 1), filler_unit] + [(e, 1, 1) for e in range(6, E)]
         units = first_units + second_units
-        loads = [(e, 1, None) for e in range(SINGLE)] + [(e, 2, None) for e in range(SINGLE, EARLY, 2)]
+        loads = [(e, c, None) for e, c in EARLY_LOADS]
         loads += [(e, 1, h) for h in range(HALVES) for e in range(EARLY, E)]
 
         landed, raw, grouped, words, scales, bias = {}, {}, {}, {}, {}, {}
@@ -103,18 +120,26 @@ def tile_moe_pkd_lin_silu_kernel(tc, x_words, x_scales, w, b, gate, offs, pos1, 
         scale_rows = x_scales[0].rearrange("(q r) t -> r q t", r=4)
         for e, count, h in loads:
             load_weights(e, count, h)
-            if e == 0:
+            if e == GATE_AT:
                 nc.sync.dma_start(gate_rows[0:BLOCKS, :, :], gate[:, 0, :].rearrange("r (j p) -> j r p", p=P))
-            if e == SINGLE - 1:
+            if e == SCALES_AT:
                 for r in range(4):
                     nc.sync.dma_start(token_scales[r:P:32, :].bitcast(I32), scale_rows[r].bitcast(I32))
-            if e == SINGLE:
+            if (e, h) == POS_AT:
                 nc.sync.dma_start(pos_sb[0][:], pos1)
                 nc.sync.dma_start(pos_sb[1][:], pos2)
             if (e, h) == (BIAS_AFTER, 0):
-                load_bias(0, 0, E)
-                load_bias(1, 0, EARLY)
-        load_bias(1, EARLY, E)
+                if ONE_BIAS:
+                    both = keep.tile([P, 2, E], F32, name="both")
+                    nc.sync.dma_start(both[:], b.rearrange("(h p) e -> p h e", p=P))
+                    for hh in range(2):
+                        for ee in range(E):
+                            bias[ee, hh] = both[:, hh, ee : ee + 1]
+                else:
+                    load_bias(0, 0, E)
+                    load_bias(1, 0, BSPLIT)
+        if not ONE_BIAS:
+            load_bias(1, BSPLIT, E)
         for a, z in ((0, SECOND_CUTS[1]), (SECOND_CUTS[1], T)):
             nc.sync.dma_start(gates[:, :, a:z], gate[:, 0:P, a:z].rearrange("r p t -> p r t"))
 
@@ -126,7 +151,7 @@ def tile_moe_pkd_lin_silu_kernel(tc, x_words, x_scales, w, b, gate, offs, pos1, 
             first, count, h = unit
             for i in range(count):
                 e = first + i
-                on_vector = EARLY <= e < (E if h == 0 else EARLY + VECTOR_SECOND)
+                on_vector = EARLY <= e < (E if h == 0 else EARLY + VECTOR_SECOND) or e >= E - VECTOR_LAST or (e, h) in EXTRA_V
                 copy = nc.vector.tensor_copy if on_vector else nc.scalar.copy
                 copy(
                     grouped[unit][:, i * P : (i + 1) * P, :].rearrange("p (c i) j -> p c j i", i=LINE),
@@ -135,7 +160,7 @@ def tile_moe_pkd_lin_silu_kernel(tc, x_words, x_scales, w, b, gate, offs, pos1, 
 
         def quantize(unit):
             first, count, h = unit
-            tag = "raw%d_0" % LAST if unit == filler_unit else "words%d_%d" % (first, h)
+            tag = "raw%d_0" % LAST if unit == filler_unit else Q_TAG if unit == (Q_HOLD, 1, 1) else "words%d_%d" % (first, h)
             words[unit] = keep.tile([P, count * P], U32, name="words%d_%d" % (first, h), tag=tag, align_bytes=64)
             scales[unit] = keep.tile([P, count * P], U8, name="scales%d_%d" % (first, h), align_bytes=64)
             nc.vector.quantize_mx(
@@ -169,12 +194,28 @@ def tile_moe_pkd_lin_silu_kernel(tc, x_words, x_scales, w, b, gate, offs, pos1, 
         def fetched(h, r, a, z):
             return y[h][:].indirect(pos_sb[r][:, a // LIST_ROWS : z // LIST_ROWS])
 
-        def weigh_turned(values, a, turned, scaled, back):
-            starts = range(0, FIRST_PIECE, P)
+        def turn(values, turned):
             for r in range(2):
-                for t in starts:
+                for t in range(0, FIRST_PIECE, P):
                     at = r * FIRST_PIECE + t
-                    nc.tensor.transpose(turned[:, at : at + P], values[:, r, t : t + P], identity[:])
+                    nc.tensor.transpose(turned[:, at : at + P], values[r][:, t : t + P], identity[:])
+
+        def fetch_first(a):
+            values = []
+            if a + FIRST_PIECE == T and HOLD_TAG0 == "same":
+                pair = keep.tile([P, 2, FIRST_PIECE], F32, name="values%d" % a, tag=HOLD_TAG, align_bytes=64)
+                for r in range(2):
+                    nc.vector.tensor_copy(pair[:, r, :], fetched(0, r, a, a + FIRST_PIECE))
+                return [pair[:, 0, :], pair[:, 1, :]]
+            for r in range(2):
+                held = a + FIRST_PIECE == T and r >= 2 - HOLD
+                tag = (HOLD_TAG if r == 1 else HOLD_TAG0) if held else "values%d_%d" % (a, r)
+                values.append(keep.tile([P, FIRST_PIECE], F32, name="values%d_%d" % (a, r), tag=tag, align_bytes=64))
+                nc.vector.tensor_copy(values[r][:], fetched(0, r, a, a + FIRST_PIECE))
+            return values
+
+        def weigh_turned(a, turned, scaled, back):
+            starts = range(0, FIRST_PIECE, P)
             for t in starts:
                 for r in range(2):
                     at = r * FIRST_PIECE + t
@@ -198,25 +239,27 @@ def tile_moe_pkd_lin_silu_kernel(tc, x_words, x_scales, w, b, gate, offs, pos1, 
             nc.vector.tensor_copy(slot_scales[g][:], token_scales[:].indirect(entries(g)))
         for unit in units:
             regroup(unit)
-            quantize(unit)
+            if unit[2] == 0 or unit[0] < Q_HOLD:
+                quantize(unit)
 
         first_runs = [(0, GATHER_EXPERTS)] + [u[:2] for u in first_units[GATHER_EXPERTS // 2 :]]
         for (first, count), bank in zip(first_runs, (0, 1, 2, 5, 6, 7)):
             experts(first, count, 0, banks[bank])
-        second_runs = [u[:2] for u in second_units[:2]] + [(EARLY, VECTOR_SECOND)] + [(e, 1) for e in range(EARLY + VECTOR_SECOND, E)]
-        for (first, count), bank in zip(second_runs, (3, 4, 0, 1, 2, 5, 0)):
+        second_runs = [u[:2] for u in second_units[:2]] + [(6, 2)] + [(e, 1) for e in range(8, E)]
+        values0 = fetch_first(0)
+        turn(values0, banks[TURNED[0]])
+        values1 = fetch_first(FIRST_PIECE)
+        for unit in units:
+            if unit[2] == 1 and unit[0] >= Q_HOLD:
+                quantize(unit)
+        for (first, count), bank in zip(second_runs, SBANKS):
             experts(first, count, 1, banks[bank])
-
-        pieces = []
-        for a in range(0, T, FIRST_PIECE):
-            tag = "raw%d_1" % LAST if a + FIRST_PIECE == T else "values%d" % a
-            values = keep.tile([P, 2, FIRST_PIECE], F32, name="values%d" % a, tag=tag, align_bytes=64)
-            for r in range(2):
-                nc.vector.tensor_copy(values[:, r, :], fetched(0, r, a, a + FIRST_PIECE))
-            pieces.append((values, a))
-        scaled = keep.tile([P, 2, T], F32, name="scaled", tag="words%d_1" % LAST, align_bytes=64)
-        for (values, a), turned, back in zip(pieces, (6, 7, 1), (3, 4, 2)):
-            weigh_turned(values, a, banks[turned], scaled, banks[back])
+        values2 = fetch_first(2 * FIRST_PIECE)
+        turn(values1, banks[TURNED[1]])
+        turn(values2, banks[TURNED[2]])
+        scaled = keep.tile([P, 2, T], F32, name="scaled", tag=SCALED_TAG, align_bytes=64)
+        for a, turned, back in zip(range(0, T, FIRST_PIECE), TURNED, BACK):
+            weigh_turned(a, banks[turned], scaled, banks[back])
 
         for a, z in zip(SECOND_CUTS[:-1], SECOND_CUTS[1:]):
             terms = keep.tile([P, 2, z - a], F32, name="terms%d" % a, align_bytes=64)

@@ -37,18 +37,24 @@ ONE_BIAS = 0
 HOLD = 2
 HOLD_TAG0 = "same"
 HOLD_TAG = "raw11_1"
-TURNED = (6, 5, 0)
-BACK = (3, 4, 7)
-SBANKS = (3, 4, 0, 1, 2, 5, 0, 1)
-GATE_AT = 0
+TURNED = (6,5,7)
+BACK = (3,4,0)
+SBANKS = (3,4,0,1,2,5,7)
+GATE_AT = (0, None)
+GATE_BANK = 7
 EARLY_LOADS = ((0, 1), (1, 1), (2, 2), (4, 2))
 SCALES_AT = 1
 Q_HOLD = 8
+ON_POOL = ()
+NOT_V = ((6,0),)
+FIRST_TAG = "values0_0"
+HEAD_ACT = 0
+HEAD_POOL = 0
 BSPLIT = 6
 EXTRA_V = ()
-Q_TAG = "words8_1"
+Q_TAG = "wordsq"
 SCALED_TAG = "words11_1"
-BIAS_AFTER = EARLY + 1
+BIAS_AFTER = 8
 FIRST_PIECE = 2 * P
 SECOND_CUTS = (0, 3 * P, 5 * P, T)
 
@@ -93,12 +99,37 @@ def tile_moe_pkd_lin_silu_kernel(tc, x_words, x_scales, w, b, gate, offs, pos1, 
             e, count, h = unit
             grouped[unit] = keep.tile([P, count * P, PACK], BF16, name="grouped%d_%d" % (e, h), align_bytes=64)
 
-        nc.gpsimd.memset(token_scales[:].bitcast(I32), 0)
         warm = keep.tile([P, 2], F32, name="warm")
-        nc.gpsimd.memset(warm[:, 0:1], 0.0)
+        if HEAD_POOL:
+            nc.vector.memset(warm[:, 0:1], 0.0)
+        scale_rows = x_scales[0].rearrange("(q r) t -> r q t", r=4)
+        if HEAD_ACT:
+            nc.vector.memset(token_scales[:].bitcast(I32), 0)
+            for r in range(4):
+                nc.scalar.dma_start(token_scales[r:P:32, :].bitcast(I32), scale_rows[r].bitcast(I32))
+            if HEAD_ACT == 2:
+                nc.gpsimd.memset(gate_rows[:], 0.0)
+                nc.scalar.dma_start(gate_rows[0:BLOCKS, :, :], gate[:, 0, :].rearrange("r (j p) -> j r p", p=P))
+            make_identity(nc, identity[:])
+        else:
+            if HEAD_POOL:
+                nc.vector.memset(token_scales[:].bitcast(I32), 0)
+                nc.vector.memset(gate_rows[:], 0.0)
+                make_identity(nc, identity[:])
+            else:
+                nc.gpsimd.memset(token_scales[:].bitcast(I32), 0)
+            if HEAD_POOL:
+                for r in range(4):
+                    nc.gpsimd.dma_start(token_scales[r:P:32, :].bitcast(I32), scale_rows[r].bitcast(I32))
+        if not HEAD_POOL:
+            nc.gpsimd.memset(warm[:, 0:1], 0.0)
         nc.scalar.activation(warm[:, 1:2], warm[:, 0:1], SILU)
-        make_identity(nc, identity[:])
-        nc.gpsimd.memset(gate_rows[:], 0.0)
+        if not HEAD_ACT and not HEAD_POOL:
+            make_identity(nc, identity[:])
+        if HEAD_ACT != 2 and not HEAD_POOL:
+            nc.gpsimd.memset(gate_rows[:], 0.0)
+        if HEAD_POOL == 2:
+            nc.gpsimd.dma_start(gate_rows[0:BLOCKS, :, :], gate[:, 0, :].rearrange("r (j p) -> j r p", p=P))
 
         def load_weights(e, count, h):
             if h is None:
@@ -117,12 +148,11 @@ def tile_moe_pkd_lin_silu_kernel(tc, x_words, x_scales, w, b, gate, offs, pos1, 
 
         nc.sync.dma_start(token_words[:], x_words[0].rearrange("p t r -> p (t r)").bitcast(I32))
         nc.sync.dma_start(offs_sb[:], offs)
-        scale_rows = x_scales[0].rearrange("(q r) t -> r q t", r=4)
         for e, count, h in loads:
             load_weights(e, count, h)
-            if e == GATE_AT:
+            if (e, h) == GATE_AT and HEAD_ACT != 2 and HEAD_POOL != 2:
                 nc.sync.dma_start(gate_rows[0:BLOCKS, :, :], gate[:, 0, :].rearrange("r (j p) -> j r p", p=P))
-            if e == SCALES_AT:
+            if e == SCALES_AT and not HEAD_ACT and not HEAD_POOL:
                 for r in range(4):
                     nc.sync.dma_start(token_scales[r:P:32, :].bitcast(I32), scale_rows[r].bitcast(I32))
             if (e, h) == POS_AT:
@@ -147,12 +177,18 @@ def tile_moe_pkd_lin_silu_kernel(tc, x_words, x_scales, w, b, gate, offs, pos1, 
             per = GATHER_EXPERTS * C // LIST_ROWS
             return offs_sb[:, g * per : (g + 1) * per]
 
+        def pool_copy(dst, src):
+            nc.gpsimd.tensor_scalar(dst, src, 1.0, 0.0, MULT, ADD)
+
         def regroup(unit):
             first, count, h = unit
             for i in range(count):
                 e = first + i
                 on_vector = EARLY <= e < (E if h == 0 else EARLY + VECTOR_SECOND) or e >= E - VECTOR_LAST or (e, h) in EXTRA_V
+                on_vector = on_vector and (e, h) not in NOT_V
                 copy = nc.vector.tensor_copy if on_vector else nc.scalar.copy
+                if (e, h) in ON_POOL:
+                    copy = pool_copy
                 copy(
                     grouped[unit][:, i * P : (i + 1) * P, :].rearrange("p (c i) j -> p c j i", i=LINE),
                     raw[e, h].rearrange("p j (c i) -> p c j i", i=LINE),
@@ -209,7 +245,7 @@ def tile_moe_pkd_lin_silu_kernel(tc, x_words, x_scales, w, b, gate, offs, pos1, 
                 return [pair[:, 0, :], pair[:, 1, :]]
             for r in range(2):
                 held = a + FIRST_PIECE == T and r >= 2 - HOLD
-                tag = (HOLD_TAG if r == 1 else HOLD_TAG0) if held else "values%d_%d" % (a, r)
+                tag = (HOLD_TAG if r == 1 else HOLD_TAG0) if held else FIRST_TAG if (a, r) == (0, 0) else "values%d_%d" % (a, r)
                 values.append(keep.tile([P, FIRST_PIECE], F32, name="values%d_%d" % (a, r), tag=tag, align_bytes=64))
                 nc.vector.tensor_copy(values[r][:], fetched(0, r, a, a + FIRST_PIECE))
             return values
@@ -229,10 +265,13 @@ def tile_moe_pkd_lin_silu_kernel(tc, x_words, x_scales, w, b, gate, offs, pos1, 
             nc.scalar.copy(result[0][:, a : a + FIRST_PIECE], back[:, 0:FIRST_PIECE])
             nc.scalar.dma_start(out[0:P, a : a + FIRST_PIECE], result[0][:, a : a + FIRST_PIECE])
 
-        for r in range(2):
-            nc.tensor.transpose(banks[7][:, r * P : (r + 1) * P], gate_rows[:, r, :], identity[:])
-        nc.scalar.copy(gate_cols[:], banks[7][:, 0 : 2 * P].rearrange("p (r q) -> p r q", r=2)[:, :, 0:BLOCKS])
+        def turn_gates():
+            for r in range(2):
+                nc.tensor.transpose(banks[GATE_BANK][:, r * P : (r + 1) * P], gate_rows[:, r, :], identity[:])
+            nc.scalar.copy(gate_cols[:], banks[GATE_BANK][:, 0 : 2 * P].rearrange("p (r q) -> p r q", r=2)[:, :, 0:BLOCKS])
 
+        if GATE_AT[1] is None:
+            turn_gates()
         for g in range(groups):
             nc.vector.tensor_copy(slot_words[g][:], token_words[:].bitcast(U32).indirect(entries(g)))
         for g in range(groups):
@@ -246,6 +285,8 @@ def tile_moe_pkd_lin_silu_kernel(tc, x_words, x_scales, w, b, gate, offs, pos1, 
         for (first, count), bank in zip(first_runs, (0, 1, 2, 5, 6, 7)):
             experts(first, count, 0, banks[bank])
         second_runs = [u[:2] for u in second_units[:2]] + [(6, 2)] + [(e, 1) for e in range(8, E)]
+        if GATE_AT[1] is not None:
+            turn_gates()
         values0 = fetch_first(0)
         turn(values0, banks[TURNED[0]])
         values1 = fetch_first(FIRST_PIECE)

@@ -28,35 +28,20 @@ LINE = 4
 BANK = 512
 BLOCKS = T // P
 LAST = E - 1
-EARLY = 6
-SINGLE = 2
-VECTOR_SECOND = 2
-VECTOR_LAST = 0
-POS_AT = (SINGLE, None)
-ONE_BIAS = 0
-HOLD = 2
-HOLD_TAG0 = "same"
-HOLD_TAG = "raw11_1"
-TURNED = (6,5,7)
-BACK = (3,4,0)
-SBANKS = (3,4,0,1,2,5,7)
-GATE_AT = (0, None)
-GATE_BANK = 7
-EARLY_LOADS = ((0, 1), (1, 1), (2, 2), (4, 2))
-SCALES_AT = 1
-Q_HOLD = 8
-ON_POOL = ()
-NOT_V = ((6,0),)
-FIRST_TAG = "values0_0"
-HEAD_ACT = 0
-HEAD_POOL = 0
-BSPLIT = 6
-EXTRA_V = ()
-Q_TAG = "wordsq"
-SCALED_TAG = "words11_1"
-BIAS_AFTER = 8
-FIRST_PIECE = 2 * P
-SECOND_CUTS = (0, 3 * P, 5 * P, T)
+LOADS = ((0,1,0,2,),(1,1,0,2,),(2,1,0,2,),(3,1,0,2,),(4,1,0,2,),(5,1,0,2,),(6,1,0,2,),(7,1,0,2,),(8,1,0,2,),(9,1,0,2,),(10,1,0,2,),(11,1,0,2,),)
+UNITS = ((0,1,0,2,),(1,2,0,2,),(3,2,0,2,),(5,1,0,2,),(6,1,0,2,),(7,1,0,2,),(8,1,0,2,),(9,1,0,2,),(10,1,0,2,),(11,1,0,1,),(11,1,1,1,),)
+ON_VECTOR = ((5,0,),(7,0,),(9,0,),(10,0,),(11,0,),)
+LATE_UNITS = 0
+POS_AFTER = (9,0,)
+BIAS_AFTER = (7,0,)
+GATE_AFTER = (0,0,)
+VECTOR_CUTS = ((0,256,512,),(0,256,384,),)
+SCALAR_CUTS = ((512,768,),(384,640,768,),)
+VECTOR_TOKENS = max(cuts[-1] for cuts in VECTOR_CUTS)
+FIRST_TURNED = min(cuts[0] for cuts in SCALAR_CUTS)
+TURNED_BLOCKS = (T - FIRST_TURNED) // P
+GATE_LOADS = ((11,0,0,256,),(11,0,256,512,),)
+TAGS = {}
 
 
 def tile_moe_pkd_lin_silu_kernel(tc, x_words, x_scales, w, b, gate, offs, pos1, pos2, out):
@@ -72,239 +57,163 @@ def tile_moe_pkd_lin_silu_kernel(tc, x_words, x_scales, w, b, gate, offs, pos1, 
         token_scales = keep.tile([P, T], U8, name="token_scales", align_bytes=64)
         slot_words = [keep.tile([P, GATHER_EXPERTS * C], U32, name="slot_words%d" % g, align_bytes=64) for g in range(groups)]
         slot_scales = [keep.tile([P, GATHER_EXPERTS * C], U8, name="slot_scales%d" % g, align_bytes=64) for g in range(groups)]
-        gates = keep.tile([P, 2, T], F32, name="gates")
-        gate_rows = keep.tile([P, 2, P], F32, name="gate_rows")
-        gate_cols = keep.tile([P, 2, BLOCKS], F32, name="gate_cols")
+        gates = keep.tile([P, 2, VECTOR_TOKENS], F32, name="gates")
+        gate_rows = keep.tile([P, T - FIRST_TURNED], F32, name="gate_rows")
+        gate_cols = keep.tile([P, TURNED_BLOCKS, 2], F32, name="gate_cols")
+        bias = keep.tile([P, HALVES, E], F32, name="bias")
         y = [keep.tile([P, S], F32, name="y%d" % h) for h in range(HALVES)]
-        result = [keep.tile([P, T], F32, name="result%d" % h) for h in range(HALVES)]
         identity = keep.tile([P, P], F32, name="identity")
         banks = [psum.tile([P, BANK], F32, name="bank%d" % i) for i in range(8)]
 
-        first_units = [(e, 2, 0) for e in range(0, E - 2, 2)] + [(e, 1, 0) for e in range(E - 2, E)]
-        filler_unit = (GATHER_EXPERTS, 2, 1)
-        second_units = [(0, GATHER_EXPERTS, 1), filler_unit] + [(e, 1, 1) for e in range(6, E)]
-        units = first_units + second_units
-        loads = [(e, c, None) for e, c in EARLY_LOADS]
-        loads += [(e, 1, h) for h in range(HALVES) for e in range(EARLY, E)]
+        units = list(UNITS)
+        loads = list(LOADS)
 
-        landed, raw, grouped, words, scales, bias = {}, {}, {}, {}, {}, {}
-        for e, count, h in loads:
-            name = "raw%d_%s" % (e, h)
-            landed[e, h] = keep.tile([P, count, PACK, N if h is None else P], F32, name=name, tag=name, align_bytes=64)
+        landed, raw = {}, {}
+        for load in loads:
+            e, count, h, halves = load
+            landed[load] = keep.tile([P, count, PACK, halves * P], F32, name="raw%d_%d" % (e, h), tag="raw%d_%d" % (e, h), align_bytes=64)
             for i in range(count):
-                for half in range(HALVES) if h is None else (h,):
-                    first = half * P if h is None else 0
-                    raw[e + i, half] = landed[e, h][:, i, :, first : first + P]
-        for unit in units:
-            e, count, h = unit
-            grouped[unit] = keep.tile([P, count * P, PACK], BF16, name="grouped%d_%d" % (e, h), align_bytes=64)
+                raw[e + i, h, halves] = landed[load][:, i]
+                for d in range(halves):
+                    raw[e + i, h + d, 1] = landed[load][:, i, :, d * P : (d + 1) * P]
 
         warm = keep.tile([P, 2], F32, name="warm")
-        if HEAD_POOL:
-            nc.vector.memset(warm[:, 0:1], 0.0)
-        scale_rows = x_scales[0].rearrange("(q r) t -> r q t", r=4)
-        if HEAD_ACT:
-            nc.vector.memset(token_scales[:].bitcast(I32), 0)
-            for r in range(4):
-                nc.scalar.dma_start(token_scales[r:P:32, :].bitcast(I32), scale_rows[r].bitcast(I32))
-            if HEAD_ACT == 2:
-                nc.gpsimd.memset(gate_rows[:], 0.0)
-                nc.scalar.dma_start(gate_rows[0:BLOCKS, :, :], gate[:, 0, :].rearrange("r (j p) -> j r p", p=P))
-            make_identity(nc, identity[:])
-        else:
-            if HEAD_POOL:
-                nc.vector.memset(token_scales[:].bitcast(I32), 0)
-                nc.vector.memset(gate_rows[:], 0.0)
-                make_identity(nc, identity[:])
-            else:
-                nc.gpsimd.memset(token_scales[:].bitcast(I32), 0)
-            if HEAD_POOL:
-                for r in range(4):
-                    nc.gpsimd.dma_start(token_scales[r:P:32, :].bitcast(I32), scale_rows[r].bitcast(I32))
-        if not HEAD_POOL:
-            nc.gpsimd.memset(warm[:, 0:1], 0.0)
+        nc.vector.memset(token_scales[:].bitcast(I32), 0)
+        nc.gpsimd.memset(warm[:, 0:1], 0.0)
         nc.scalar.activation(warm[:, 1:2], warm[:, 0:1], SILU)
-        if not HEAD_ACT and not HEAD_POOL:
-            make_identity(nc, identity[:])
-        if HEAD_ACT != 2 and not HEAD_POOL:
-            nc.gpsimd.memset(gate_rows[:], 0.0)
-        if HEAD_POOL == 2:
-            nc.gpsimd.dma_start(gate_rows[0:BLOCKS, :, :], gate[:, 0, :].rearrange("r (j p) -> j r p", p=P))
+        make_identity(nc, identity[:])
+        nc.vector.memset(gate_rows[:], 0.0)
 
-        def load_weights(e, count, h):
-            if h is None:
+        scale_rows = x_scales[0].rearrange("(q r) t -> r q t", r=4)
+        nc.sync.dma_start(token_words[:], x_words[0].rearrange("p t r -> p (t r)").bitcast(I32))
+        nc.sync.dma_start(offs_sb[:], offs)
+        for load in loads:
+            e, count, h, halves = load
+            if halves == HALVES:
                 nc.sync.dma_start(
-                    landed[e, h][:].rearrange("p e j n -> p e (j n)"),
+                    landed[load][:].rearrange("p e j n -> p e (j n)"),
                     w[e : e + count].rearrange("e (p j) n -> p e (j n)", j=PACK),
                 )
             else:
-                nc.sync.dma_start(landed[e, h][:, 0], w[e].rearrange("(p j) n -> p j n", j=PACK)[:, :, h * P : (h + 1) * P])
-
-        def load_bias(h, first, last):
-            columns = keep.tile([P, last - first], F32, name="bias%d_%d" % (h, first))
-            nc.sync.dma_start(columns[:], b[h * P : (h + 1) * P, first:last])
-            for e in range(first, last):
-                bias[e, h] = columns[:, e - first : e - first + 1]
-
-        nc.sync.dma_start(token_words[:], x_words[0].rearrange("p t r -> p (t r)").bitcast(I32))
-        nc.sync.dma_start(offs_sb[:], offs)
-        for e, count, h in loads:
-            load_weights(e, count, h)
-            if (e, h) == GATE_AT and HEAD_ACT != 2 and HEAD_POOL != 2:
-                nc.sync.dma_start(gate_rows[0:BLOCKS, :, :], gate[:, 0, :].rearrange("r (j p) -> j r p", p=P))
-            if e == SCALES_AT and not HEAD_ACT and not HEAD_POOL:
+                nc.sync.dma_start(landed[load][:, 0], w[e].rearrange("(p j) n -> p j n", j=PACK)[:, :, h * P : (h + 1) * P])
+            if (e, h) == GATE_AFTER:
+                nc.sync.dma_start(gate_rows[0:2, :], gate[:, 0, FIRST_TURNED:T])
+            if (e, h) == (1, 0):
                 for r in range(4):
                     nc.sync.dma_start(token_scales[r:P:32, :].bitcast(I32), scale_rows[r].bitcast(I32))
-            if (e, h) == POS_AT:
+            if (e, h) == POS_AFTER:
                 nc.sync.dma_start(pos_sb[0][:], pos1)
                 nc.sync.dma_start(pos_sb[1][:], pos2)
-            if (e, h) == (BIAS_AFTER, 0):
-                if ONE_BIAS:
-                    both = keep.tile([P, 2, E], F32, name="both")
-                    nc.sync.dma_start(both[:], b.rearrange("(h p) e -> p h e", p=P))
-                    for hh in range(2):
-                        for ee in range(E):
-                            bias[ee, hh] = both[:, hh, ee : ee + 1]
-                else:
-                    load_bias(0, 0, E)
-                    load_bias(1, 0, BSPLIT)
-        if not ONE_BIAS:
-            load_bias(1, BSPLIT, E)
-        for a, z in ((0, SECOND_CUTS[1]), (SECOND_CUTS[1], T)):
-            nc.sync.dma_start(gates[:, :, a:z], gate[:, 0:P, a:z].rearrange("r p t -> p r t"))
+            for after_e, after_h, a, z in GATE_LOADS:
+                if (e, h) == (after_e, after_h):
+                    nc.sync.dma_start(gates[:, :, a:z], gate[:, 0:P, a:z].rearrange("r p t -> p r t"))
+            if (e, h) == BIAS_AFTER:
+                nc.sync.dma_start(bias[:], b.rearrange("(h p) e -> p h e", p=P))
 
-        def entries(g):
-            per = GATHER_EXPERTS * C // LIST_ROWS
-            return offs_sb[:, g * per : (g + 1) * per]
+        for j in range(TURNED_BLOCKS):
+            nc.tensor.transpose(banks[7][:, j * P : (j + 1) * P], gate_rows[:, j * P : (j + 1) * P], identity[:])
+        nc.scalar.copy(gate_cols[:], banks[7][:, 0 : TURNED_BLOCKS * P].rearrange("p (j q) -> p j q", q=P)[:, :, 0:2])
 
-        def pool_copy(dst, src):
-            nc.gpsimd.tensor_scalar(dst, src, 1.0, 0.0, MULT, ADD)
+        per = GATHER_EXPERTS * C // LIST_ROWS
+        for g in range(groups):
+            nc.vector.tensor_copy(slot_words[g][:], token_words[:].bitcast(U32).indirect(offs_sb[:, g * per : (g + 1) * per]))
+        for g in range(groups):
+            nc.vector.tensor_copy(slot_scales[g][:], token_scales[:].indirect(offs_sb[:, g * per : (g + 1) * per]))
 
-        def regroup(unit):
-            first, count, h = unit
+        words, scales = {}, {}
+
+        def prepare(unit):
+            first, count, h, halves = unit
+            width = halves * P
+            name = "%d_%d" % (first, h)
+            grouped = keep.tile([P, count * width, PACK], BF16, name="grouped" + name, tag=TAGS.get("grouped" + name, "grouped" + name), align_bytes=64)
             for i in range(count):
-                e = first + i
-                on_vector = EARLY <= e < (E if h == 0 else EARLY + VECTOR_SECOND) or e >= E - VECTOR_LAST or (e, h) in EXTRA_V
-                on_vector = on_vector and (e, h) not in NOT_V
-                copy = nc.vector.tensor_copy if on_vector else nc.scalar.copy
-                if (e, h) in ON_POOL:
-                    copy = pool_copy
+                copy = nc.vector.tensor_copy if (first + i, h) in ON_VECTOR else nc.scalar.copy
                 copy(
-                    grouped[unit][:, i * P : (i + 1) * P, :].rearrange("p (c i) j -> p c j i", i=LINE),
-                    raw[e, h].rearrange("p j (c i) -> p c j i", i=LINE),
+                    grouped[:, i * width : (i + 1) * width, :].rearrange("p (c i) j -> p c j i", i=LINE),
+                    raw[first + i, h, halves].rearrange("p j (c i) -> p c j i", i=LINE),
                 )
+            words[unit] = keep.tile([P, count * width], U32, name="words" + name, tag="words" + name, align_bytes=64)
+            scales[unit] = keep.tile([P, count * width], U8, name="scales" + name, align_bytes=64)
+            nc.vector.quantize_mx(out=words[unit][:].bitcast(FP8X4), scales=scales[unit][:], in_=grouped[:].rearrange("p n j -> p (n j)"))
 
-        def quantize(unit):
-            first, count, h = unit
-            tag = "raw%d_0" % LAST if unit == filler_unit else Q_TAG if unit == (Q_HOLD, 1, 1) else "words%d_%d" % (first, h)
-            words[unit] = keep.tile([P, count * P], U32, name="words%d_%d" % (first, h), tag=tag, align_bytes=64)
-            scales[unit] = keep.tile([P, count * P], U8, name="scales%d_%d" % (first, h), align_bytes=64)
-            nc.vector.quantize_mx(
-                out=words[unit][:].bitcast(FP8X4),
-                scales=scales[unit][:],
-                in_=grouped[unit][:].rearrange("p n j -> p (n j)"),
-            )
-
-        def multiply(e, h, acc):
-            unit = [u for u in units if u[2] == h and u[0] <= e < u[0] + u[1]][0]
-            cols = slice((e - unit[0]) * P, (e - unit[0] + 1) * P)
-            g, place = divmod(e, GATHER_EXPERTS)
-            slots = slice(place * C, (place + 1) * C)
-            nc.tensor.matmul_mx(
-                out=acc,
-                lhsT=words[unit][:, cols].bitcast(FP8X4),
-                lhsT_scale=scales[unit][:, cols],
-                rhs=slot_words[g][:, slots].bitcast(FP8X4),
-                rhs_scale=slot_scales[g][:, slots],
-                start=True,
-                stop=True,
-            )
-
-        def experts(first, count, h, bank):
-            for i in range(count):
-                multiply(first + i, h, bank[:, i * C : (i + 1) * C])
-            for i in range(count):
-                e = first + i
-                nc.scalar.activation(y[h][:, e * C : (e + 1) * C], bank[:, i * C : (i + 1) * C], SILU, bias=bias[e, h])
+        def multiply(unit, bank):
+            first, count, h, halves = unit
+            parts = [(first + i, h + d) for i in range(count) for d in range(halves)]
+            for at, (e, half) in enumerate(parts):
+                cols = slice(at * P, (at + 1) * P)
+                g, place = divmod(e, GATHER_EXPERTS)
+                slots = slice(place * C, (place + 1) * C)
+                nc.tensor.matmul_mx(
+                    out=bank[:, cols],
+                    lhsT=words[unit][:, cols].bitcast(FP8X4),
+                    lhsT_scale=scales[unit][:, cols],
+                    rhs=slot_words[g][:, slots].bitcast(FP8X4),
+                    rhs_scale=slot_scales[g][:, slots],
+                    start=True,
+                    stop=True,
+                )
+            for at, (e, half) in enumerate(parts):
+                nc.scalar.activation(y[half][:, e * C : (e + 1) * C], bank[:, at * P : (at + 1) * P], SILU, bias=bias[:, half, e : e + 1])
 
         def fetched(h, r, a, z):
             return y[h][:].indirect(pos_sb[r][:, a // LIST_ROWS : z // LIST_ROWS])
 
-        def turn(values, turned):
-            for r in range(2):
-                for t in range(0, FIRST_PIECE, P):
-                    at = r * FIRST_PIECE + t
-                    nc.tensor.transpose(turned[:, at : at + P], values[r][:, t : t + P], identity[:])
-
-        def fetch_first(a):
-            values = []
-            if a + FIRST_PIECE == T and HOLD_TAG0 == "same":
-                pair = keep.tile([P, 2, FIRST_PIECE], F32, name="values%d" % a, tag=HOLD_TAG, align_bytes=64)
+        def combine_on_vector(h):
+            cuts = VECTOR_CUTS[h]
+            for a, z in zip(cuts[:-1], cuts[1:]):
+                names = ["terms%d_%d_%d" % (h, a, r) for r in range(2)]
+                terms = [keep.tile([P, z - a], F32, name=names[r], tag=TAGS.get(names[r], names[r]), align_bytes=64) for r in range(2)]
+                result = keep.tile([P, z - a], F32, name="result%d_%d" % (h, a))
                 for r in range(2):
-                    nc.vector.tensor_copy(pair[:, r, :], fetched(0, r, a, a + FIRST_PIECE))
-                return [pair[:, 0, :], pair[:, 1, :]]
-            for r in range(2):
-                held = a + FIRST_PIECE == T and r >= 2 - HOLD
-                tag = (HOLD_TAG if r == 1 else HOLD_TAG0) if held else FIRST_TAG if (a, r) == (0, 0) else "values%d_%d" % (a, r)
-                values.append(keep.tile([P, FIRST_PIECE], F32, name="values%d_%d" % (a, r), tag=tag, align_bytes=64))
-                nc.vector.tensor_copy(values[r][:], fetched(0, r, a, a + FIRST_PIECE))
-            return values
+                    nc.vector.tensor_tensor(terms[r][:], fetched(h, r, a, z), gates[:, r, a:z], MULT)
+                nc.vector.tensor_tensor(result[:], terms[0][:], terms[1][:], ADD)
+                nc.sync.dma_start(out[h * P : (h + 1) * P, a:z], result[:])
 
-        def weigh_turned(a, turned, scaled, back):
-            starts = range(0, FIRST_PIECE, P)
-            for t in starts:
+        def fetch_and_turn(h, a, z, turned):
+            name = "values%d_%d" % (h, a)
+            values = keep.tile([P, 2, z - a], F32, name=name, tag=TAGS.get(name, name), align_bytes=64)
+            for r in range(2):
+                nc.scalar.activation(values[:, r, :], fetched(h, r, a, z), COPY)
+            for t in range(0, z - a, P):
                 for r in range(2):
-                    at = r * FIRST_PIECE + t
-                    j = (a + t) // P
-                    nc.scalar.activation(scaled[:, r, a + t : a + t + P], turned[:, at : at + P], COPY, scale=gate_cols[:, r, j : j + 1])
-            for t in starts:
+                    at = 2 * t + r * P
+                    nc.tensor.transpose(turned[:, at : at + P], values[:, r, t : t + P], identity[:])
+
+        def weigh_and_turn_back(h, a, z, turned, back):
+            scaled = keep.tile([P, 2, z - a], F32, name="scaled%d_%d" % (h, a))
+            for t in range(0, z - a, P):
                 for r in range(2):
-                    nc.tensor.matmul(
-                        back[:, t : t + P], scaled[:, r, a + t : a + t + P], identity[:], start=(r == 0), stop=(r == 1), is_transpose=True
-                    )
-            nc.scalar.copy(result[0][:, a : a + FIRST_PIECE], back[:, 0:FIRST_PIECE])
-            nc.scalar.dma_start(out[0:P, a : a + FIRST_PIECE], result[0][:, a : a + FIRST_PIECE])
+                    at = 2 * t + r * P
+                    j = (a + t - FIRST_TURNED) // P
+                    nc.scalar.activation(scaled[:, r, t : t + P], turned[:, at : at + P], COPY, scale=gate_cols[:, j, r : r + 1])
+            for t in range(0, z - a, P):
+                for r in range(2):
+                    nc.tensor.matmul(back[:, t : t + P], scaled[:, r, t : t + P], identity[:], start=(r == 0), stop=(r == 1), is_transpose=True)
 
-        def turn_gates():
-            for r in range(2):
-                nc.tensor.transpose(banks[GATE_BANK][:, r * P : (r + 1) * P], gate_rows[:, r, :], identity[:])
-            nc.scalar.copy(gate_cols[:], banks[GATE_BANK][:, 0 : 2 * P].rearrange("p (r q) -> p r q", r=2)[:, :, 0:BLOCKS])
+        def store_turned(h, a, z, back):
+            result = keep.tile([P, z - a], F32, name="turned_result%d_%d" % (h, a))
+            nc.scalar.copy(result[:], back[:, 0 : z - a])
+            nc.scalar.dma_start(out[h * P : (h + 1) * P, a:z], result[:])
 
-        if GATE_AT[1] is None:
-            turn_gates()
-        for g in range(groups):
-            nc.vector.tensor_copy(slot_words[g][:], token_words[:].bitcast(U32).indirect(entries(g)))
-        for g in range(groups):
-            nc.vector.tensor_copy(slot_scales[g][:], token_scales[:].indirect(entries(g)))
-        for unit in units:
-            regroup(unit)
-            if unit[2] == 0 or unit[0] < Q_HOLD:
-                quantize(unit)
-
-        first_runs = [(0, GATHER_EXPERTS)] + [u[:2] for u in first_units[GATHER_EXPERTS // 2 :]]
-        for (first, count), bank in zip(first_runs, (0, 1, 2, 5, 6, 7)):
-            experts(first, count, 0, banks[bank])
-        second_runs = [u[:2] for u in second_units[:2]] + [(6, 2)] + [(e, 1) for e in range(8, E)]
-        if GATE_AT[1] is not None:
-            turn_gates()
-        values0 = fetch_first(0)
-        turn(values0, banks[TURNED[0]])
-        values1 = fetch_first(FIRST_PIECE)
-        for unit in units:
-            if unit[2] == 1 and unit[0] >= Q_HOLD:
-                quantize(unit)
-        for (first, count), bank in zip(second_runs, SBANKS):
-            experts(first, count, 1, banks[bank])
-        values2 = fetch_first(2 * FIRST_PIECE)
-        turn(values1, banks[TURNED[1]])
-        turn(values2, banks[TURNED[2]])
-        scaled = keep.tile([P, 2, T], F32, name="scaled", tag=SCALED_TAG, align_bytes=64)
-        for a, turned, back in zip(range(0, T, FIRST_PIECE), TURNED, BACK):
-            weigh_turned(a, banks[turned], scaled, banks[back])
-
-        for a, z in zip(SECOND_CUTS[:-1], SECOND_CUTS[1:]):
-            terms = keep.tile([P, 2, z - a], F32, name="terms%d" % a, align_bytes=64)
-            for r in range(2):
-                nc.vector.tensor_tensor(terms[:, r, :], fetched(1, r, a, z), gates[:, r, a:z], MULT)
-            nc.vector.tensor_tensor(result[1][:, a:z], terms[:, 0, :], terms[:, 1, :], ADD)
-            nc.sync.dma_start(out[P:N, a:z], result[1][:, a:z])
+        late = len(units) - LATE_UNITS
+        for unit in units[:late]:
+            prepare(unit)
+        for at, unit in enumerate(units[:late]):
+            multiply(unit, banks[at % 8])
+        for unit in units[late:]:
+            prepare(unit)
+        for unit in units[late:]:
+            multiply(unit, banks[units.index(unit) % 8])
+        pieces = [(h, a, z) for h in range(HALVES) for a, z in zip(SCALAR_CUTS[h][:-1], SCALAR_CUTS[h][1:])]
+        last_bank = len(units) - 1
+        turned = [banks[(last_bank + i) % 8] for i in range(len(pieces))]
+        back = [banks[(last_bank + len(pieces) + i) % 8] for i in range(len(pieces))]
+        for h in range(HALVES):
+            combine_on_vector(h)
+        for i, piece in enumerate(pieces):
+            fetch_and_turn(*piece, turned[i])
+        for i, piece in enumerate(pieces):
+            weigh_and_turn_back(*piece, turned[i], back[i])
+        for i, piece in enumerate(pieces):
+            store_turned(*piece, back[i])

@@ -35,13 +35,13 @@ LATE_UNITS = 0
 POS_AFTER = (9,0,)
 BIAS_AFTER = (7,0,)
 GATE_AFTER = (0,0,)
-VECTOR_CUTS = ((0,256,512,),(0,256,384,),)
-SCALAR_CUTS = ((512,768,),(384,640,768,),)
+VECTOR_CUTS = ((0,256,512,),(0,256,384,512,),)
+SCALAR_CUTS = ((512,768,),(512,768,),)
 VECTOR_TOKENS = max(cuts[-1] for cuts in VECTOR_CUTS)
 FIRST_TURNED = min(cuts[0] for cuts in SCALAR_CUTS)
 TURNED_BLOCKS = (T - FIRST_TURNED) // P
 GATE_LOADS = ((11,0,0,256,),(11,0,256,512,),)
-TAGS = {}
+TAGS = {"terms1_384_1": "terms1_0_0"}
 
 
 def tile_moe_pkd_lin_silu_kernel(tc, x_words, x_scales, w, b, gate, offs, pos1, pos2, out):

@@ -28,11 +28,11 @@ LINE = 4
 BANK = 512
 BLOCKS = T // P
 LAST = E - 1
-LOADS = ((0,1,0,2,),(1,1,0,2,),(2,1,0,2,),(3,1,0,2,),(4,1,0,2,),(5,1,0,2,),(6,1,0,2,),(7,1,0,2,),(8,1,0,2,),(9,1,0,2,),(10,1,0,2,),(11,1,0,2,),)
+LOADS = ((0,1,0,2,),(1,1,0,2,),(2,1,0,2,),(3,1,0,2,),(4,1,0,2,),(5,1,0,2,),(6,1,0,2,),(7,1,0,2,),(8,1,0,2,),(9,1,0,2,),(10,1,0,2,),(11,1,0,1,),(11,1,1,1,),)
 UNITS = ((0,1,0,2,),(1,2,0,2,),(3,2,0,2,),(5,1,0,2,),(6,1,0,2,),(7,1,0,2,),(8,1,0,2,),(9,1,0,2,),(10,1,0,2,),(11,1,0,1,),(11,1,1,1,),)
-ON_VECTOR = ((5,0,),(7,0,),(9,0,),(10,0,),(11,0,),)
+ON_VECTOR = ((7,0,),(9,0,),(10,0,),(11,0,),)
 LATE_UNITS = 0
-POS_AFTER = (9,0,)
+POS_AFTER = (11,1,)
 BIAS_AFTER = (7,0,)
 GATE_AFTER = (0,0,)
 VECTOR_CUTS = ((0,256,512,),(0,256,384,512,),)
@@ -40,8 +40,9 @@ SCALAR_CUTS = ((512,768,),(512,768,),)
 VECTOR_TOKENS = max(cuts[-1] for cuts in VECTOR_CUTS)
 FIRST_TURNED = min(cuts[0] for cuts in SCALAR_CUTS)
 TURNED_BLOCKS = (T - FIRST_TURNED) // P
-GATE_LOADS = ((11,0,0,256,),(11,0,256,512,),)
-TAGS = {"terms1_384_1": "terms1_0_0"}
+GATE_LOADS = ((11,1,0,256,),(11,1,256,512,),)
+ON_GPSIMD = ()
+TAGS = {"terms1_256_1": "terms1_0_0"}
 
 
 def tile_moe_pkd_lin_silu_kernel(tc, x_words, x_scales, w, b, gate, offs, pos1, pos2, out):
@@ -128,6 +129,11 @@ def tile_moe_pkd_lin_silu_kernel(tc, x_words, x_scales, w, b, gate, offs, pos1, 
             name = "%d_%d" % (first, h)
             grouped = keep.tile([P, count * width, PACK], BF16, name="grouped" + name, tag=TAGS.get("grouped" + name, "grouped" + name), align_bytes=64)
             for i in range(count):
+                if (first + i, h) in ON_GPSIMD:
+                    nc.gpsimd.tensor_scalar(
+                        grouped[:, i * width : (i + 1) * width, :], raw[first + i, h, halves].rearrange("p j n -> p n j"), 1.0, 0.0, MULT, ADD
+                    )
+                    continue
                 copy = nc.vector.tensor_copy if (first + i, h) in ON_VECTOR else nc.scalar.copy
                 copy(
                     grouped[:, i * width : (i + 1) * width, :].rearrange("p (c i) j -> p c j i", i=LINE),
@@ -137,15 +143,22 @@ def tile_moe_pkd_lin_silu_kernel(tc, x_words, x_scales, w, b, gate, offs, pos1, 
             scales[unit] = keep.tile([P, count * width], U8, name="scales" + name, align_bytes=64)
             nc.vector.quantize_mx(out=words[unit][:].bitcast(FP8X4), scales=scales[unit][:], in_=grouped[:].rearrange("p n j -> p (n j)"))
 
-        def multiply(unit, bank):
+        used = []
+
+        def multiply(unit):
             first, count, h, halves = unit
             parts = [(first + i, h + d) for i in range(count) for d in range(halves)]
+            for start in range(0, len(parts), BANK // C):
+                multiply_parts(unit, start, parts[start : start + BANK // C], banks[len(used) % 8])
+                used.append(unit)
+
+        def multiply_parts(unit, start, parts, bank):
             for at, (e, half) in enumerate(parts):
-                cols = slice(at * P, (at + 1) * P)
+                cols = slice((start + at) * P, (start + at + 1) * P)
                 g, place = divmod(e, GATHER_EXPERTS)
                 slots = slice(place * C, (place + 1) * C)
                 nc.tensor.matmul_mx(
-                    out=bank[:, cols],
+                    out=bank[:, at * C : (at + 1) * C],
                     lhsT=words[unit][:, cols].bitcast(FP8X4),
                     lhsT_scale=scales[unit][:, cols],
                     rhs=slot_words[g][:, slots].bitcast(FP8X4),
@@ -171,14 +184,14 @@ def tile_moe_pkd_lin_silu_kernel(tc, x_words, x_scales, w, b, gate, offs, pos1, 
                 nc.sync.dma_start(out[h * P : (h + 1) * P, a:z], result[:])
 
         def fetch_and_turn(h, a, z, turned):
-            name = "values%d_%d" % (h, a)
-            values = keep.tile([P, 2, z - a], F32, name=name, tag=TAGS.get(name, name), align_bytes=64)
+            names = ["values%d_%d_%d" % (h, a, r) for r in range(2)]
+            values = [keep.tile([P, z - a], F32, name=names[r], tag=TAGS.get(names[r], names[r]), align_bytes=64) for r in range(2)]
             for r in range(2):
-                nc.scalar.activation(values[:, r, :], fetched(h, r, a, z), COPY)
+                nc.scalar.activation(values[r][:], fetched(h, r, a, z), COPY)
             for t in range(0, z - a, P):
                 for r in range(2):
                     at = 2 * t + r * P
-                    nc.tensor.transpose(turned[:, at : at + P], values[:, r, t : t + P], identity[:])
+                    nc.tensor.transpose(turned[:, at : at + P], values[r][:, t : t + P], identity[:])
 
         def weigh_and_turn_back(h, a, z, turned, back):
             scaled = keep.tile([P, 2, z - a], F32, name="scaled%d_%d" % (h, a))
@@ -199,14 +212,14 @@ def tile_moe_pkd_lin_silu_kernel(tc, x_words, x_scales, w, b, gate, offs, pos1, 
         late = len(units) - LATE_UNITS
         for unit in units[:late]:
             prepare(unit)
-        for at, unit in enumerate(units[:late]):
-            multiply(unit, banks[at % 8])
+        for unit in units[:late]:
+            multiply(unit)
         for unit in units[late:]:
             prepare(unit)
         for unit in units[late:]:
-            multiply(unit, banks[units.index(unit) % 8])
+            multiply(unit)
         pieces = [(h, a, z) for h in range(HALVES) for a, z in zip(SCALAR_CUTS[h][:-1], SCALAR_CUTS[h][1:])]
-        last_bank = len(units) - 1
+        last_bank = len(used) - 1
         turned = [banks[(last_bank + i) % 8] for i in range(len(pieces))]
         back = [banks[(last_bank + len(pieces) + i) % 8] for i in range(len(pieces))]
         for h in range(HALVES):

@@ -8,6 +8,7 @@ S = E * C
 P = 128
 PACK = 4
 HALVES = N // P
+LISTS = 2
 FLOPS = 2 * K * N * S
 
 F32 = mybir.dt.float32
@@ -26,23 +27,15 @@ LIST_ROWS = 16
 GATHER_EXPERTS = 4
 LINE = 4
 BANK = 512
-BLOCKS = T // P
+BANKS = 8
 LAST = E - 1
-LOADS = ((0,1,0,2,),(1,1,0,2,),(2,1,0,2,),(3,1,0,2,),(4,1,0,2,),(5,1,0,2,),(6,1,0,2,),(7,1,0,2,),(8,1,0,2,),(9,1,0,2,),(10,1,0,2,),(11,1,0,1,),(11,1,1,1,),)
-UNITS = ((0,1,0,2,),(1,2,0,2,),(3,2,0,2,),(5,1,0,2,),(6,1,0,2,),(7,1,0,2,),(8,1,0,2,),(9,1,0,2,),(10,1,0,2,),(11,1,0,1,),(11,1,1,1,),)
-ON_VECTOR = ((7,0,),(9,0,),(10,0,),(11,0,),)
-LATE_UNITS = 0
-POS_AFTER = (11,1,)
-BIAS_AFTER = (7,0,)
-GATE_AFTER = (0,0,)
-VECTOR_CUTS = ((0,256,512,),(0,256,384,512,),)
-SCALAR_CUTS = ((512,768,),(512,768,),)
-VECTOR_TOKENS = max(cuts[-1] for cuts in VECTOR_CUTS)
-FIRST_TURNED = min(cuts[0] for cuts in SCALAR_CUTS)
-TURNED_BLOCKS = (T - FIRST_TURNED) // P
-GATE_LOADS = ((11,1,0,256,),(11,1,256,512,),)
-ON_GPSIMD = ()
-TAGS = {"terms1_256_1": "terms1_0_0"}
+VECTOR_FROM = 7
+HALVES_FROM = 9
+PAIRED_UP_TO = 5
+VECTOR_TOKENS = 4 * P
+TURNED = T - VECTOR_TOKENS
+GATE_CUT = 2 * P
+CUTS = ((0, GATE_CUT, VECTOR_TOKENS), (0, GATE_CUT, 3 * P, VECTOR_TOKENS))
 
 
 def tile_moe_pkd_lin_silu_kernel(tc, x_words, x_scales, w, b, gate, offs, pos1, pos2, out):
@@ -53,30 +46,31 @@ def tile_moe_pkd_lin_silu_kernel(tc, x_words, x_scales, w, b, gate, offs, pos1, 
 
         groups = E // GATHER_EXPERTS
         offs_sb = keep.tile([P, S // LIST_ROWS], U16, name="offs_sb")
-        pos_sb = [keep.tile([P, T // LIST_ROWS], U16, name="pos%d_sb" % r) for r in range(2)]
+        pos_sb = [keep.tile([P, T // LIST_ROWS], U16, name="pos%d_sb" % r) for r in range(LISTS)]
         token_words = keep.tile([P, T], I32, name="token_words", align_bytes=64)
         token_scales = keep.tile([P, T], U8, name="token_scales", align_bytes=64)
         slot_words = [keep.tile([P, GATHER_EXPERTS * C], U32, name="slot_words%d" % g, align_bytes=64) for g in range(groups)]
         slot_scales = [keep.tile([P, GATHER_EXPERTS * C], U8, name="slot_scales%d" % g, align_bytes=64) for g in range(groups)]
-        gates = keep.tile([P, 2, VECTOR_TOKENS], F32, name="gates")
-        gate_rows = keep.tile([P, T - FIRST_TURNED], F32, name="gate_rows")
-        gate_cols = keep.tile([P, TURNED_BLOCKS, 2], F32, name="gate_cols")
+        gates = keep.tile([P, LISTS, VECTOR_TOKENS], F32, name="gates")
+        gate_rows = keep.tile([P, TURNED], F32, name="gate_rows")
+        gate_cols = keep.tile([P, TURNED // P, LISTS], F32, name="gate_cols")
         bias = keep.tile([P, HALVES, E], F32, name="bias")
         y = [keep.tile([P, S], F32, name="y%d" % h) for h in range(HALVES)]
         identity = keep.tile([P, P], F32, name="identity")
-        banks = [psum.tile([P, BANK], F32, name="bank%d" % i) for i in range(8)]
+        banks = [psum.tile([P, BANK], F32, name="bank%d" % i) for i in range(BANKS)]
 
-        units = list(UNITS)
-        loads = list(LOADS)
+        loads = [(e, 0, HALVES) for e in range(LAST)] + [(LAST, h, 1) for h in range(HALVES)]
+        last_first = (LAST, 1, 0, 1)
+        middle_seconds = (HALVES_FROM, LAST - HALVES_FROM, 1, 1)
+        last_second = (LAST, 1, 1, 1)
+        units = [(0, 1, 0, HALVES)] + [(e, 2, 0, HALVES) for e in range(1, PAIRED_UP_TO, 2)]
+        units = units + [(e, 1, 0, HALVES) for e in range(PAIRED_UP_TO, HALVES_FROM)]
+        units = units + [(e, 1, 0, 1) for e in range(HALVES_FROM, E)] + [middle_seconds, last_second]
 
-        landed, raw = {}, {}
-        for load in loads:
-            e, count, h, halves = load
-            landed[load] = keep.tile([P, count, PACK, halves * P], F32, name="raw%d_%d" % (e, h), tag="raw%d_%d" % (e, h), align_bytes=64)
-            for i in range(count):
-                raw[e + i, h, halves] = landed[load][:, i]
-                for d in range(halves):
-                    raw[e + i, h + d, 1] = landed[load][:, i, :, d * P : (d + 1) * P]
+        landed = {}
+        for e, h, halves in loads:
+            name = "landed%d_%d" % (e, h)
+            landed[e, h] = keep.tile([P, PACK, halves * P], F32, name=name, tag=name, align_bytes=64)
 
         warm = keep.tile([P, 2], F32, name="warm")
         nc.vector.memset(token_scales[:].bitcast(I32), 0)
@@ -88,145 +82,134 @@ def tile_moe_pkd_lin_silu_kernel(tc, x_words, x_scales, w, b, gate, offs, pos1, 
         scale_rows = x_scales[0].rearrange("(q r) t -> r q t", r=4)
         nc.sync.dma_start(token_words[:], x_words[0].rearrange("p t r -> p (t r)").bitcast(I32))
         nc.sync.dma_start(offs_sb[:], offs)
-        for load in loads:
-            e, count, h, halves = load
+        for e, h, halves in loads:
             if halves == HALVES:
-                nc.sync.dma_start(
-                    landed[load][:].rearrange("p e j n -> p e (j n)"),
-                    w[e : e + count].rearrange("e (p j) n -> p e (j n)", j=PACK),
-                )
+                nc.sync.dma_start(landed[e, h][:].rearrange("p j n -> p (j n)"), w[e].rearrange("(p j) n -> p (j n)", j=PACK))
             else:
-                nc.sync.dma_start(landed[load][:, 0], w[e].rearrange("(p j) n -> p j n", j=PACK)[:, :, h * P : (h + 1) * P])
-            if (e, h) == GATE_AFTER:
-                nc.sync.dma_start(gate_rows[0:2, :], gate[:, 0, FIRST_TURNED:T])
-            if (e, h) == (1, 0):
+                nc.sync.dma_start(landed[e, h][:], w[e].rearrange("(p j) n -> p j n", j=PACK)[:, :, h * P : (h + 1) * P])
+            if e == 0:
+                nc.sync.dma_start(gate_rows[0:LISTS, :], gate[:, 0, VECTOR_TOKENS:T])
+            if e == 1:
                 for r in range(4):
                     nc.sync.dma_start(token_scales[r:P:32, :].bitcast(I32), scale_rows[r].bitcast(I32))
-            if (e, h) == POS_AFTER:
-                nc.sync.dma_start(pos_sb[0][:], pos1)
-                nc.sync.dma_start(pos_sb[1][:], pos2)
-            for after_e, after_h, a, z in GATE_LOADS:
-                if (e, h) == (after_e, after_h):
-                    nc.sync.dma_start(gates[:, :, a:z], gate[:, 0:P, a:z].rearrange("r p t -> p r t"))
-            if (e, h) == BIAS_AFTER:
+            if e == VECTOR_FROM:
                 nc.sync.dma_start(bias[:], b.rearrange("(h p) e -> p h e", p=P))
+        nc.sync.dma_start(pos_sb[0][:], pos1)
+        nc.sync.dma_start(pos_sb[1][:], pos2)
+        for a, z in ((0, GATE_CUT), (GATE_CUT, VECTOR_TOKENS)):
+            nc.sync.dma_start(gates[:, :, a:z], gate[:, 0:P, a:z].rearrange("r p t -> p r t"))
 
-        for j in range(TURNED_BLOCKS):
-            nc.tensor.transpose(banks[7][:, j * P : (j + 1) * P], gate_rows[:, j * P : (j + 1) * P], identity[:])
-        nc.scalar.copy(gate_cols[:], banks[7][:, 0 : TURNED_BLOCKS * P].rearrange("p (j q) -> p j q", q=P)[:, :, 0:2])
+        for t in range(0, TURNED, P):
+            nc.tensor.transpose(banks[-1][:, t : t + P], gate_rows[:, t : t + P], identity[:])
+        nc.scalar.copy(gate_cols[:], banks[-1][:, 0:TURNED].rearrange("p (j q) -> p j q", q=P)[:, :, 0:LISTS])
 
-        per = GATHER_EXPERTS * C // LIST_ROWS
+        columns = GATHER_EXPERTS * C // LIST_ROWS
         for g in range(groups):
-            nc.vector.tensor_copy(slot_words[g][:], token_words[:].bitcast(U32).indirect(offs_sb[:, g * per : (g + 1) * per]))
+            nc.vector.tensor_copy(slot_words[g][:], token_words[:].bitcast(U32).indirect(offs_sb[:, g * columns : (g + 1) * columns]))
         for g in range(groups):
-            nc.vector.tensor_copy(slot_scales[g][:], token_scales[:].indirect(offs_sb[:, g * per : (g + 1) * per]))
+            nc.vector.tensor_copy(slot_scales[g][:], token_scales[:].indirect(offs_sb[:, g * columns : (g + 1) * columns]))
 
         words, scales = {}, {}
 
-        def prepare(unit):
+        def tag_of(kind, unit):
+            return "%s%d_%d" % (kind, unit[0], unit[2])
+
+        def quantize(unit):
             first, count, h, halves = unit
             width = halves * P
-            name = "%d_%d" % (first, h)
-            grouped = keep.tile([P, count * width, PACK], BF16, name="grouped" + name, tag=TAGS.get("grouped" + name, "grouped" + name), align_bytes=64)
+            grouped_tag = tag_of("grouped", last_first if unit == last_second else unit)
+            words_tag = tag_of("landed", last_second) if unit == middle_seconds else tag_of("words", unit)
+            grouped = keep.tile([P, count * width, PACK], BF16, name=tag_of("grouped", unit), tag=grouped_tag, align_bytes=64)
             for i in range(count):
-                if (first + i, h) in ON_GPSIMD:
-                    nc.gpsimd.tensor_scalar(
-                        grouped[:, i * width : (i + 1) * width, :], raw[first + i, h, halves].rearrange("p j n -> p n j"), 1.0, 0.0, MULT, ADD
-                    )
-                    continue
-                copy = nc.vector.tensor_copy if (first + i, h) in ON_VECTOR else nc.scalar.copy
+                e = first + i
+                source = landed[e, h][:] if e == LAST else landed[e, 0][:, :, h * P : h * P + width]
+                copy = nc.scalar.copy if e < VECTOR_FROM or unit == middle_seconds else nc.vector.tensor_copy
                 copy(
                     grouped[:, i * width : (i + 1) * width, :].rearrange("p (c i) j -> p c j i", i=LINE),
-                    raw[first + i, h, halves].rearrange("p j (c i) -> p c j i", i=LINE),
+                    source.rearrange("p j (c i) -> p c j i", i=LINE),
                 )
-            words[unit] = keep.tile([P, count * width], U32, name="words" + name, tag="words" + name, align_bytes=64)
-            scales[unit] = keep.tile([P, count * width], U8, name="scales" + name, align_bytes=64)
+            words[unit] = keep.tile([P, count * width], U32, name=tag_of("words", unit), tag=words_tag, align_bytes=64)
+            scales[unit] = keep.tile([P, count * width], U8, name=tag_of("scales", unit), align_bytes=64)
             nc.vector.quantize_mx(out=words[unit][:].bitcast(FP8X4), scales=scales[unit][:], in_=grouped[:].rearrange("p n j -> p (n j)"))
 
-        used = []
-
-        def multiply(unit):
+        def multiply(unit, bank):
             first, count, h, halves = unit
             parts = [(first + i, h + d) for i in range(count) for d in range(halves)]
-            for start in range(0, len(parts), BANK // C):
-                multiply_parts(unit, start, parts[start : start + BANK // C], banks[len(used) % 8])
-                used.append(unit)
-
-        def multiply_parts(unit, start, parts, bank):
             for at, (e, half) in enumerate(parts):
-                cols = slice((start + at) * P, (start + at + 1) * P)
-                g, place = divmod(e, GATHER_EXPERTS)
-                slots = slice(place * C, (place + 1) * C)
+                features = slice(at * P, (at + 1) * P)
+                g, member = divmod(e, GATHER_EXPERTS)
+                slots = slice(member * C, (member + 1) * C)
                 nc.tensor.matmul_mx(
                     out=bank[:, at * C : (at + 1) * C],
-                    lhsT=words[unit][:, cols].bitcast(FP8X4),
-                    lhsT_scale=scales[unit][:, cols],
+                    lhsT=words[unit][:, features].bitcast(FP8X4),
+                    lhsT_scale=scales[unit][:, features],
                     rhs=slot_words[g][:, slots].bitcast(FP8X4),
                     rhs_scale=slot_scales[g][:, slots],
                     start=True,
                     stop=True,
                 )
             for at, (e, half) in enumerate(parts):
-                nc.scalar.activation(y[half][:, e * C : (e + 1) * C], bank[:, at * P : (at + 1) * P], SILU, bias=bias[:, half, e : e + 1])
+                nc.scalar.activation(y[half][:, e * C : (e + 1) * C], bank[:, at * C : (at + 1) * C], SILU, bias=bias[:, half, e : e + 1])
 
         def fetched(h, r, a, z):
             return y[h][:].indirect(pos_sb[r][:, a // LIST_ROWS : z // LIST_ROWS])
 
         def combine_on_vector(h):
-            cuts = VECTOR_CUTS[h]
-            for a, z in zip(cuts[:-1], cuts[1:]):
-                names = ["terms%d_%d_%d" % (h, a, r) for r in range(2)]
-                terms = [keep.tile([P, z - a], F32, name=names[r], tag=TAGS.get(names[r], names[r]), align_bytes=64) for r in range(2)]
+            for a, z in zip(CUTS[h][:-1], CUTS[h][1:]):
+                names = ["terms%d_%d_%d" % (h, a, r) for r in range(LISTS)]
+                tags = list(names)
+                if (h, a) == (1, GATE_CUT):
+                    tags = [names[0], "terms1_0_0"]
+                terms = [keep.tile([P, z - a], F32, name=names[r], tag=tags[r], align_bytes=64) for r in range(LISTS)]
                 result = keep.tile([P, z - a], F32, name="result%d_%d" % (h, a))
-                for r in range(2):
+                for r in range(LISTS):
                     nc.vector.tensor_tensor(terms[r][:], fetched(h, r, a, z), gates[:, r, a:z], MULT)
                 nc.vector.tensor_tensor(result[:], terms[0][:], terms[1][:], ADD)
                 nc.sync.dma_start(out[h * P : (h + 1) * P, a:z], result[:])
 
-        def fetch_and_turn(h, a, z, turned):
-            names = ["values%d_%d_%d" % (h, a, r) for r in range(2)]
-            values = [keep.tile([P, z - a], F32, name=names[r], tag=TAGS.get(names[r], names[r]), align_bytes=64) for r in range(2)]
-            for r in range(2):
-                nc.scalar.activation(values[r][:], fetched(h, r, a, z), COPY)
-            for t in range(0, z - a, P):
-                for r in range(2):
-                    at = 2 * t + r * P
-                    nc.tensor.transpose(turned[:, at : at + P], values[r][:, t : t + P], identity[:])
+        def place(t, r):
+            return slice(LISTS * t + r * P, LISTS * t + (r + 1) * P)
 
-        def weigh_and_turn_back(h, a, z, turned, back):
-            scaled = keep.tile([P, 2, z - a], F32, name="scaled%d_%d" % (h, a))
-            for t in range(0, z - a, P):
-                for r in range(2):
-                    at = 2 * t + r * P
-                    j = (a + t - FIRST_TURNED) // P
-                    nc.scalar.activation(scaled[:, r, t : t + P], turned[:, at : at + P], COPY, scale=gate_cols[:, j, r : r + 1])
-            for t in range(0, z - a, P):
-                for r in range(2):
-                    nc.tensor.matmul(back[:, t : t + P], scaled[:, r, t : t + P], identity[:], start=(r == 0), stop=(r == 1), is_transpose=True)
+        def fetch_and_turn(h, turned):
+            names = ["values%d_%d" % (h, r) for r in range(LISTS)]
+            tags = list(names)
+            if h == 0:
+                tags = [names[0], tag_of("words", last_second)]
+            values = [keep.tile([P, TURNED], F32, name=names[r], tag=tags[r], align_bytes=64) for r in range(LISTS)]
+            for r in range(LISTS):
+                nc.scalar.activation(values[r][:], fetched(h, r, VECTOR_TOKENS, T), COPY)
+            for r in range(LISTS):
+                for t in range(0, TURNED, P):
+                    nc.tensor.transpose(turned[:, place(t, r)], values[r][:, t : t + P], identity[:])
 
-        def store_turned(h, a, z, back):
-            result = keep.tile([P, z - a], F32, name="turned_result%d_%d" % (h, a))
-            nc.scalar.copy(result[:], back[:, 0 : z - a])
-            nc.scalar.dma_start(out[h * P : (h + 1) * P, a:z], result[:])
+        def weigh_and_turn_back(h, turned, back):
+            scaled = keep.tile([P, LISTS, TURNED], F32, name="scaled%d" % h)
+            for t in range(0, TURNED, P):
+                for r in range(LISTS):
+                    nc.scalar.activation(scaled[:, r, t : t + P], turned[:, place(t, r)], COPY, scale=gate_cols[:, t // P, r : r + 1])
+            for t in range(0, TURNED, P):
+                for r in range(LISTS):
+                    nc.tensor.matmul(
+                        back[:, t : t + P], scaled[:, r, t : t + P], identity[:], start=(r == 0), stop=(r == LISTS - 1), is_transpose=True
+                    )
 
-        late = len(units) - LATE_UNITS
-        for unit in units[:late]:
-            prepare(unit)
-        for unit in units[:late]:
-            multiply(unit)
-        for unit in units[late:]:
-            prepare(unit)
-        for unit in units[late:]:
-            multiply(unit)
-        pieces = [(h, a, z) for h in range(HALVES) for a, z in zip(SCALAR_CUTS[h][:-1], SCALAR_CUTS[h][1:])]
-        last_bank = len(used) - 1
-        turned = [banks[(last_bank + i) % 8] for i in range(len(pieces))]
-        back = [banks[(last_bank + len(pieces) + i) % 8] for i in range(len(pieces))]
+        def store_turned(h, back):
+            result = keep.tile([P, TURNED], F32, name="turned_result%d" % h)
+            nc.scalar.copy(result[:], back[:, 0:TURNED])
+            nc.scalar.dma_start(out[h * P : (h + 1) * P, VECTOR_TOKENS:T], result[:])
+
+        for unit in units:
+            quantize(unit)
+        for i, unit in enumerate(units):
+            multiply(unit, banks[i % BANKS])
+        last_bank = len(units) - 1
+        turned = [banks[(last_bank + h) % BANKS] for h in range(HALVES)]
+        back = [banks[(last_bank + HALVES + h) % BANKS] for h in range(HALVES)]
         for h in range(HALVES):
             combine_on_vector(h)
-        for i, piece in enumerate(pieces):
-            fetch_and_turn(*piece, turned[i])
-        for i, piece in enumerate(pieces):
-            weigh_and_turn_back(*piece, turned[i], back[i])
-        for i, piece in enumerate(pieces):
-            store_turned(*piece, back[i])
+        for h in range(HALVES):
+            fetch_and_turn(h, turned[h])
+        for h in range(HALVES):
+            weigh_and_turn_back(h, turned[h], back[h])
+        for h in range(HALVES):
+            store_turned(h, back[h])

@@ -26,6 +26,8 @@ SILU = mybir.ActivationFunctionType.Silu
 LIST_ROWS = 16
 GATHER_EXPERTS = 4
 LINE = 4
+ALIGN = 256
+BIAS_ROW = 16
 BANK = 512
 BANKS = 8
 LAST = E - 1
@@ -47,14 +49,14 @@ def tile_moe_pkd_lin_silu_kernel(tc, x_words, x_scales, w, b, gate, offs, pos1, 
         groups = E // GATHER_EXPERTS
         offs_sb = keep.tile([P, S // LIST_ROWS], U16, name="offs_sb")
         pos_sb = [keep.tile([P, T // LIST_ROWS], U16, name="pos%d_sb" % r) for r in range(LISTS)]
-        token_words = keep.tile([P, T], I32, name="token_words", align_bytes=64)
-        token_scales = keep.tile([P, T], U8, name="token_scales", align_bytes=64)
-        slot_words = [keep.tile([P, GATHER_EXPERTS * C], U32, name="slot_words%d" % g, align_bytes=64) for g in range(groups)]
-        slot_scales = [keep.tile([P, GATHER_EXPERTS * C], U8, name="slot_scales%d" % g, align_bytes=64) for g in range(groups)]
-        gates = keep.tile([P, LISTS, VECTOR_TOKENS], F32, name="gates")
+        token_words = keep.tile([P, T], I32, name="token_words", align_bytes=ALIGN)
+        token_scales = keep.tile([P, T], U8, name="token_scales", align_bytes=ALIGN)
+        slot_words = [keep.tile([P, GATHER_EXPERTS * C], U32, name="slot_words%d" % g, align_bytes=ALIGN) for g in range(groups)]
+        slot_scales = [keep.tile([P, GATHER_EXPERTS * C], U8, name="slot_scales%d" % g, align_bytes=ALIGN) for g in range(groups)]
+        gates = keep.tile([P, LISTS, VECTOR_TOKENS], F32, name="gates", align_bytes=ALIGN)
         gate_rows = keep.tile([P, TURNED], F32, name="gate_rows")
         gate_cols = keep.tile([P, TURNED // P, LISTS], F32, name="gate_cols")
-        bias = keep.tile([P, HALVES, E], F32, name="bias")
+        bias = keep.tile([P, HALVES, BIAS_ROW], F32, name="bias")
         y = [keep.tile([P, S], F32, name="y%d" % h) for h in range(HALVES)]
         identity = keep.tile([P, P], F32, name="identity")
         banks = [psum.tile([P, BANK], F32, name="bank%d" % i) for i in range(BANKS)]
@@ -70,7 +72,7 @@ def tile_moe_pkd_lin_silu_kernel(tc, x_words, x_scales, w, b, gate, offs, pos1, 
         landed = {}
         for e, h, halves in loads:
             name = "landed%d_%d" % (e, h)
-            landed[e, h] = keep.tile([P, PACK, halves * P], F32, name=name, tag=name, align_bytes=64)
+            landed[e, h] = keep.tile([P, PACK, halves * P], F32, name=name, tag=name, align_bytes=ALIGN)
 
         warm = keep.tile([P, 2], F32, name="warm")
         nc.vector.memset(token_scales[:].bitcast(I32), 0)
@@ -93,7 +95,7 @@ def tile_moe_pkd_lin_silu_kernel(tc, x_words, x_scales, w, b, gate, offs, pos1, 
                 for r in range(4):
                     nc.sync.dma_start(token_scales[r:P:32, :].bitcast(I32), scale_rows[r].bitcast(I32))
             if e == VECTOR_FROM:
-                nc.sync.dma_start(bias[:], b.rearrange("(h p) e -> p h e", p=P))
+                nc.sync.dma_start(bias[:, :, 0:E], b.rearrange("(h p) e -> p h e", p=P))
         nc.sync.dma_start(pos_sb[0][:], pos1)
         nc.sync.dma_start(pos_sb[1][:], pos2)
         for a, z in ((0, GATE_CUT), (GATE_CUT, VECTOR_TOKENS)):
@@ -119,7 +121,7 @@ def tile_moe_pkd_lin_silu_kernel(tc, x_words, x_scales, w, b, gate, offs, pos1, 
             width = halves * P
             grouped_tag = tag_of("grouped", last_first if unit == last_second else unit)
             words_tag = tag_of("landed", last_second) if unit == middle_seconds else tag_of("words", unit)
-            grouped = keep.tile([P, count * width, PACK], BF16, name=tag_of("grouped", unit), tag=grouped_tag, align_bytes=64)
+            grouped = keep.tile([P, count * width, PACK], BF16, name=tag_of("grouped", unit), tag=grouped_tag, align_bytes=ALIGN)
             for i in range(count):
                 e = first + i
                 source = landed[e, h][:] if e == LAST else landed[e, 0][:, :, h * P : h * P + width]
@@ -128,8 +130,8 @@ def tile_moe_pkd_lin_silu_kernel(tc, x_words, x_scales, w, b, gate, offs, pos1, 
                     grouped[:, i * width : (i + 1) * width, :].rearrange("p (c i) j -> p c j i", i=LINE),
                     source.rearrange("p j (c i) -> p c j i", i=LINE),
                 )
-            words[unit] = keep.tile([P, count * width], U32, name=tag_of("words", unit), tag=words_tag, align_bytes=64)
-            scales[unit] = keep.tile([P, count * width], U8, name=tag_of("scales", unit), align_bytes=64)
+            words[unit] = keep.tile([P, count * width], U32, name=tag_of("words", unit), tag=words_tag, align_bytes=ALIGN)
+            scales[unit] = keep.tile([P, count * width], U8, name=tag_of("scales", unit), align_bytes=ALIGN)
             nc.vector.quantize_mx(out=words[unit][:].bitcast(FP8X4), scales=scales[unit][:], in_=grouped[:].rearrange("p n j -> p (n j)"))
 
         def multiply(unit, bank):
@@ -160,8 +162,8 @@ def tile_moe_pkd_lin_silu_kernel(tc, x_words, x_scales, w, b, gate, offs, pos1, 
                 tags = list(names)
                 if (h, a) == (1, GATE_CUT):
                     tags = [names[0], "terms1_0_0"]
-                terms = [keep.tile([P, z - a], F32, name=names[r], tag=tags[r], align_bytes=64) for r in range(LISTS)]
-                result = keep.tile([P, z - a], F32, name="result%d_%d" % (h, a))
+                terms = [keep.tile([P, z - a], F32, name=names[r], tag=tags[r], align_bytes=ALIGN) for r in range(LISTS)]
+                result = keep.tile([P, z - a], F32, name="result%d_%d" % (h, a), align_bytes=ALIGN)
                 for r in range(LISTS):
                     nc.vector.tensor_tensor(terms[r][:], fetched(h, r, a, z), gates[:, r, a:z], MULT)
                 nc.vector.tensor_tensor(result[:], terms[0][:], terms[1][:], ADD)
@@ -175,7 +177,7 @@ def tile_moe_pkd_lin_silu_kernel(tc, x_words, x_scales, w, b, gate, offs, pos1, 
             tags = list(names)
             if h == 0:
                 tags = [names[0], tag_of("words", last_second)]
-            values = [keep.tile([P, TURNED], F32, name=names[r], tag=tags[r], align_bytes=64) for r in range(LISTS)]
+            values = [keep.tile([P, TURNED], F32, name=names[r], tag=tags[r], align_bytes=ALIGN) for r in range(LISTS)]
             for r in range(LISTS):
                 nc.scalar.activation(values[r][:], fetched(h, r, VECTOR_TOKENS, T), COPY)
             for r in range(LISTS):
@@ -194,7 +196,7 @@ def tile_moe_pkd_lin_silu_kernel(tc, x_words, x_scales, w, b, gate, offs, pos1, 
                     )
 
         def store_turned(h, back):
-            result = keep.tile([P, TURNED], F32, name="turned_result%d" % h)
+            result = keep.tile([P, TURNED], F32, name="turned_result%d" % h, align_bytes=ALIGN)
             nc.scalar.copy(result[:], back[:, 0:TURNED])
             nc.scalar.dma_start(out[h * P : (h + 1) * P, VECTOR_TOKENS:T], result[:])
 

@@ -63,8 +63,8 @@ def tile_moe_pkd_lin_silu_kernel(tc, x_words, x_scales, w, b, gate, offs, pos1, 
 
         loads = [(e, 0, HALVES) for e in range(LAST)] + [(LAST, h, 1) for h in range(HALVES)]
         last_first = (LAST, 1, 0, 1)
-        middle_seconds = (HALVES_FROM, LAST - HALVES_FROM, 1, 1)
-        last_second = (LAST, 1, 1, 1)
+        middle_seconds = (HALVES_FROM, LAST - 1 - HALVES_FROM, 1, 1)
+        last_second = (LAST - 1, 2, 1, 1)
         units = [(0, 1, 0, HALVES)] + [(e, 2, 0, HALVES) for e in range(1, PAIRED_UP_TO, 2)]
         units = units + [(e, 1, 0, HALVES) for e in range(PAIRED_UP_TO, HALVES_FROM)]
         units = units + [(e, 1, 0, 1) for e in range(HALVES_FROM, E)] + [middle_seconds, last_second]
@@ -120,19 +120,32 @@ def tile_moe_pkd_lin_silu_kernel(tc, x_words, x_scales, w, b, gate, offs, pos1, 
             first, count, h, halves = unit
             width = halves * P
             grouped_tag = tag_of("grouped", last_first if unit == last_second else unit)
-            words_tag = tag_of("landed", last_second) if unit == middle_seconds else tag_of("words", unit)
+            words_tag = tag_of("landed", last_first) if unit == middle_seconds else tag_of("words", unit)
             grouped = keep.tile([P, count * width, PACK], BF16, name=tag_of("grouped", unit), tag=grouped_tag, align_bytes=ALIGN)
+            on_scalar = first < VECTOR_FROM or unit == middle_seconds
+            if on_scalar or unit == last_second:
+                cuts = [0, width]
+            else:
+                cuts = [0, width // 2, width]
             for i in range(count):
                 e = first + i
                 source = landed[e, h][:] if e == LAST else landed[e, 0][:, :, h * P : h * P + width]
-                copy = nc.scalar.copy if e < VECTOR_FROM or unit == middle_seconds else nc.vector.tensor_copy
-                copy(
-                    grouped[:, i * width : (i + 1) * width, :].rearrange("p (c i) j -> p c j i", i=LINE),
-                    source.rearrange("p j (c i) -> p c j i", i=LINE),
-                )
+                for a, z in zip(cuts[:-1], cuts[1:]):
+                    copy = nc.scalar.copy if on_scalar else nc.vector.tensor_copy
+                    copy(
+                        grouped[:, i * width + a : i * width + z, :].rearrange("p (c i) j -> p c j i", i=LINE),
+                        source[:, :, a:z].rearrange("p j (c i) -> p c j i", i=LINE),
+                    )
             words[unit] = keep.tile([P, count * width], U32, name=tag_of("words", unit), tag=words_tag, align_bytes=ALIGN)
             scales[unit] = keep.tile([P, count * width], U8, name=tag_of("scales", unit), align_bytes=ALIGN)
-            nc.vector.quantize_mx(out=words[unit][:].bitcast(FP8X4), scales=scales[unit][:], in_=grouped[:].rearrange("p n j -> p (n j)"))
+            if on_scalar:
+                cuts = [0, count * width]
+            elif unit == last_second:
+                cuts = [0, width, count * width]
+            for a, z in zip(cuts[:-1], cuts[1:]):
+                nc.vector.quantize_mx(
+                    out=words[unit][:, a:z].bitcast(FP8X4), scales=scales[unit][:, a:z], in_=grouped[:, a:z, :].rearrange("p n j -> p (n j)")
+                )
 
         def multiply(unit, bank):
             first, count, h, halves = unit

@@ -33,6 +33,8 @@ BANKS = 8
 LAST = E - 1
 VECTOR_FROM = 7
 HALVES_FROM = 9
+SHARED = HALVES_FROM - 1
+SHARED_CUT = 3 * N // 4
 PAIRED_UP_TO = 5
 VECTOR_TOKENS = 4 * P
 TURNED = T - VECTOR_TOKENS
@@ -125,13 +127,15 @@ def tile_moe_pkd_lin_silu_kernel(tc, x_words, x_scales, w, b, gate, offs, pos1, 
             on_scalar = first < VECTOR_FROM or unit == middle_seconds
             if on_scalar or unit == last_second:
                 cuts = [0, width]
+            elif first == SHARED:
+                cuts = [0, P, SHARED_CUT, N]
             else:
                 cuts = [0, width // 2, width]
             for i in range(count):
                 e = first + i
                 source = landed[e, h][:] if e == LAST else landed[e, 0][:, :, h * P : h * P + width]
                 for a, z in zip(cuts[:-1], cuts[1:]):
-                    copy = nc.scalar.copy if on_scalar else nc.vector.tensor_copy
+                    copy = nc.scalar.copy if on_scalar or (e == SHARED and a == SHARED_CUT) else nc.vector.tensor_copy
                     copy(
                         grouped[:, i * width + a : i * width + z, :].rearrange("p (c i) j -> p c j i", i=LINE),
                         source[:, :, a:z].rearrange("p j (c i) -> p c j i", i=LINE),

@@ -36,10 +36,14 @@ HALVES_FROM = 9
 SHARED = HALVES_FROM - 1
 SHARED_CUT = 3 * N // 4
 PAIRED_UP_TO = 5
-VECTOR_TOKENS = 4 * P
-TURNED = T - VECTOR_TOKENS
+VECTOR_TOKENS = (3 * P, 5 * P)
+WIDE = max(VECTOR_TOKENS)
+TURNED_FROM = min(VECTOR_TOKENS)
 GATE_CUT = 2 * P
-CUTS = ((0, GATE_CUT, VECTOR_TOKENS), (0, GATE_CUT, 3 * P, VECTOR_TOKENS))
+CUTS = ((0, GATE_CUT, VECTOR_TOKENS[0]), (0, GATE_CUT, 4 * P, VECTOR_TOKENS[1]))
+
+
+HELPED = (1, 1, GATE_CUT)
 
 
 def tile_moe_pkd_lin_silu_kernel(tc, x_words, x_scales, w, b, gate, offs, pos1, pos2, out):
@@ -55,9 +59,9 @@ def tile_moe_pkd_lin_silu_kernel(tc, x_words, x_scales, w, b, gate, offs, pos1, 
         token_scales = keep.tile([P, T], U8, name="token_scales", align_bytes=ALIGN)
         slot_words = [keep.tile([P, GATHER_EXPERTS * C], U32, name="slot_words%d" % g, align_bytes=ALIGN) for g in range(groups)]
         slot_scales = [keep.tile([P, GATHER_EXPERTS * C], U8, name="slot_scales%d" % g, align_bytes=ALIGN) for g in range(groups)]
-        gates = keep.tile([P, LISTS, VECTOR_TOKENS], F32, name="gates", align_bytes=ALIGN)
-        gate_rows = keep.tile([P, TURNED], F32, name="gate_rows")
-        gate_cols = keep.tile([P, TURNED // P, LISTS], F32, name="gate_cols")
+        gates = keep.tile([P, LISTS, WIDE], F32, name="gates", align_bytes=ALIGN)
+        gate_rows = keep.tile([P, T - TURNED_FROM], F32, name="gate_rows")
+        gate_cols = keep.tile([P, (T - TURNED_FROM) // P, LISTS], F32, name="gate_cols")
         bias = keep.tile([P, HALVES, BIAS_ROW], F32, name="bias")
         y = [keep.tile([P, S], F32, name="y%d" % h) for h in range(HALVES)]
         identity = keep.tile([P, P], F32, name="identity")
@@ -92,7 +96,7 @@ def tile_moe_pkd_lin_silu_kernel(tc, x_words, x_scales, w, b, gate, offs, pos1, 
             else:
                 nc.sync.dma_start(landed[e, h][:], w[e].rearrange("(p j) n -> p j n", j=PACK)[:, :, h * P : (h + 1) * P])
             if e == 0:
-                nc.sync.dma_start(gate_rows[0:LISTS, :], gate[:, 0, VECTOR_TOKENS:T])
+                nc.sync.dma_start(gate_rows[0:LISTS, :], gate[:, 0, TURNED_FROM:T])
             if e == 1:
                 for r in range(4):
                     nc.sync.dma_start(token_scales[r:P:32, :].bitcast(I32), scale_rows[r].bitcast(I32))
@@ -100,12 +104,12 @@ def tile_moe_pkd_lin_silu_kernel(tc, x_words, x_scales, w, b, gate, offs, pos1, 
                 nc.sync.dma_start(bias[:, :, 0:E], b.rearrange("(h p) e -> p h e", p=P))
         nc.sync.dma_start(pos_sb[0][:], pos1)
         nc.sync.dma_start(pos_sb[1][:], pos2)
-        for a, z in ((0, GATE_CUT), (GATE_CUT, VECTOR_TOKENS)):
+        for a, z in ((0, GATE_CUT), (GATE_CUT, WIDE)):
             nc.sync.dma_start(gates[:, :, a:z], gate[:, 0:P, a:z].rearrange("r p t -> p r t"))
 
-        for t in range(0, TURNED, P):
+        for t in range(0, T - TURNED_FROM, P):
             nc.tensor.transpose(banks[-1][:, t : t + P], gate_rows[:, t : t + P], identity[:])
-        nc.scalar.copy(gate_cols[:], banks[-1][:, 0:TURNED].rearrange("p (j q) -> p j q", q=P)[:, :, 0:LISTS])
+        nc.scalar.copy(gate_cols[:], banks[-1][:, 0 : T - TURNED_FROM].rearrange("p (j q) -> p j q", q=P)[:, :, 0:LISTS])
 
         columns = GATHER_EXPERTS * C // LIST_ROWS
         for g in range(groups):
@@ -182,52 +186,56 @@ def tile_moe_pkd_lin_silu_kernel(tc, x_words, x_scales, w, b, gate, offs, pos1, 
                 terms = [keep.tile([P, z - a], F32, name=names[r], tag=tags[r], align_bytes=ALIGN) for r in range(LISTS)]
                 result = keep.tile([P, z - a], F32, name="result%d_%d" % (h, a), align_bytes=ALIGN)
                 for r in range(LISTS):
-                    nc.vector.tensor_tensor(terms[r][:], fetched(h, r, a, z), gates[:, r, a:z], MULT)
+                    value = helped[:] if (h, r, a) == HELPED else fetched(h, r, a, z)
+                    nc.vector.tensor_tensor(terms[r][:], value, gates[:, r, a:z], MULT)
                 nc.vector.tensor_tensor(result[:], terms[0][:], terms[1][:], ADD)
                 nc.sync.dma_start(out[h * P : (h + 1) * P, a:z], result[:])
-
-        def place(t, r):
-            return slice(LISTS * t + r * P, LISTS * t + (r + 1) * P)
 
         def fetch_and_turn(h, turned):
             names = ["values%d_%d" % (h, r) for r in range(LISTS)]
             tags = list(names)
             if h == 0:
                 tags = [names[0], tag_of("words", last_second)]
-            values = [keep.tile([P, TURNED], F32, name=names[r], tag=tags[r], align_bytes=ALIGN) for r in range(LISTS)]
+            count = T - VECTOR_TOKENS[h]
+            values = [keep.tile([P, count], F32, name=names[r], tag=tags[r], align_bytes=ALIGN) for r in range(LISTS)]
             for r in range(LISTS):
-                nc.scalar.activation(values[r][:], fetched(h, r, VECTOR_TOKENS, T), COPY)
+                nc.scalar.activation(values[r][:], fetched(h, r, VECTOR_TOKENS[h], T), COPY)
             for r in range(LISTS):
-                for t in range(0, TURNED, P):
-                    nc.tensor.transpose(turned[:, place(t, r)], values[r][:, t : t + P], identity[:])
+                for t in range(0, count, P):
+                    nc.tensor.transpose(turned[r][:, t : t + P], values[r][:, t : t + P], identity[:])
 
         def weigh_and_turn_back(h, turned, back):
-            scaled = keep.tile([P, LISTS, TURNED], F32, name="scaled%d" % h)
-            for t in range(0, TURNED, P):
+            count = T - VECTOR_TOKENS[h]
+            scaled = keep.tile([P, LISTS, count], F32, name="scaled%d" % h)
+            for t in range(0, count, P):
+                block = (VECTOR_TOKENS[h] + t - TURNED_FROM) // P
                 for r in range(LISTS):
-                    nc.scalar.activation(scaled[:, r, t : t + P], turned[:, place(t, r)], COPY, scale=gate_cols[:, t // P, r : r + 1])
-            for t in range(0, TURNED, P):
+                    nc.scalar.activation(scaled[:, r, t : t + P], turned[r][:, t : t + P], COPY, scale=gate_cols[:, block, r : r + 1])
+            for t in range(0, count, P):
                 for r in range(LISTS):
                     nc.tensor.matmul(
                         back[:, t : t + P], scaled[:, r, t : t + P], identity[:], start=(r == 0), stop=(r == LISTS - 1), is_transpose=True
                     )
 
         def store_turned(h, back):
-            result = keep.tile([P, TURNED], F32, name="turned_result%d" % h, align_bytes=ALIGN)
-            nc.scalar.copy(result[:], back[:, 0:TURNED])
-            nc.scalar.dma_start(out[h * P : (h + 1) * P, VECTOR_TOKENS:T], result[:])
+            count = T - VECTOR_TOKENS[h]
+            result = keep.tile([P, count], F32, name="turned_result%d" % h, align_bytes=ALIGN)
+            nc.scalar.copy(result[:], back[:, 0:count])
+            nc.scalar.dma_start(out[h * P : (h + 1) * P, VECTOR_TOKENS[h] : T], result[:])
 
         for unit in units:
             quantize(unit)
         for i, unit in enumerate(units):
             multiply(unit, banks[i % BANKS])
-        last_bank = len(units) - 1
-        turned = [banks[(last_bank + h) % BANKS] for h in range(HALVES)]
-        back = [banks[(last_bank + HALVES + h) % BANKS] for h in range(HALVES)]
+        free = [banks[(len(units) - 1 + i) % BANKS] for i in range(5)]
+        turned = [[free[0][:], free[1][:]], [free[2][:, 0 : BANK // 2], free[2][:, BANK // 2 : BANK]]]
+        back = free[3:5]
+        fetch_and_turn(0, turned[0])
+        fetch_and_turn(1, turned[1])
+        helped = keep.tile([P, GATE_CUT], F32, name="helped", align_bytes=ALIGN)
+        nc.scalar.activation(helped[:], fetched(HELPED[0], HELPED[1], HELPED[2], HELPED[2] + GATE_CUT), COPY)
         for h in range(HALVES):
             combine_on_vector(h)
-        for h in range(HALVES):
-            fetch_and_turn(h, turned[h])
         for h in range(HALVES):
             weigh_and_turn_back(h, turned[h], back[h])
         for h in range(HALVES):

@@ -25,7 +25,7 @@ SILU = mybir.ActivationFunctionType.Silu
 
 LIST_ROWS = 16
 GATHER_EXPERTS = 4
-LINE = 4
+PAIR = 2
 ALIGN = 256
 BIAS_ROW = 16
 BANK = 512
@@ -141,8 +141,8 @@ def tile_moe_pkd_lin_silu_kernel(tc, x_words, x_scales, w, b, gate, offs, pos1, 
                 for a, z in zip(cuts[:-1], cuts[1:]):
                     copy = nc.scalar.copy if on_scalar or (e == SHARED and a == SHARED_CUT) else nc.vector.tensor_copy
                     copy(
-                        grouped[:, i * width + a : i * width + z, :].rearrange("p (c i) j -> p c j i", i=LINE),
-                        source[:, :, a:z].rearrange("p j (c i) -> p c j i", i=LINE),
+                        grouped[:, i * width + a : i * width + z, :].rearrange("p (c i) j -> p c j i", i=PAIR),
+                        source[:, :, a:z].rearrange("p j (c i) -> p c j i", i=PAIR),
                     )
             words[unit] = keep.tile([P, count * width], U32, name=tag_of("words", unit), tag=words_tag, align_bytes=ALIGN)
             scales[unit] = keep.tile([P, count * width], U8, name=tag_of("scales", unit), align_bytes=ALIGN)

from contextlib import ExitStack

import concourse.mybir as mybir
from concourse.masks import make_identity

K, T, E, C, N = 512, 768, 12, 128, 256
S = E * C
P = 128
PACK = 4
HALVES = N // P
LISTS = 2
FLOPS = 2 * K * N * S

F32 = mybir.dt.float32
BF16 = mybir.dt.bfloat16
I32 = mybir.dt.int32
U32 = mybir.dt.uint32
U16 = mybir.dt.uint16
U8 = mybir.dt.uint8
FP8X4 = mybir.dt.float8_e4m3fn_x4
MULT = mybir.AluOpType.mult
ADD = mybir.AluOpType.add
COPY = mybir.ActivationFunctionType.Copy
SILU = mybir.ActivationFunctionType.Silu

LIST_ROWS = 16
GATHER_EXPERTS = 4
PAIR = 2
ALIGN = 256
BIAS_ROW = 16
BANK = 512
BANKS = 8
LAST = E - 1
VECTOR_FROM = 7
HALVES_FROM = 9
SHARED = HALVES_FROM - 1
SHARED_CUT = 3 * N // 4
PAIRED_UP_TO = 5
VECTOR_TOKENS = (3 * P, 5 * P)
WIDE = max(VECTOR_TOKENS)
TURNED_FROM = min(VECTOR_TOKENS)
GATE_CUT = 2 * P
CUTS = ((0, GATE_CUT, VECTOR_TOKENS[0]), (0, GATE_CUT, 4 * P, VECTOR_TOKENS[1]))


HELPED = (1, 1, GATE_CUT)


def tile_moe_pkd_lin_silu_kernel(tc, x_words, x_scales, w, b, gate, offs, pos1, pos2, out):
    nc = tc.nc
    with ExitStack() as ctx:
        keep = ctx.enter_context(tc.tile_pool(name="keep", bufs=1))
        psum = ctx.enter_context(tc.psum_pool(name="psum", bufs=1))

        groups = E // GATHER_EXPERTS
        offs_sb = keep.tile([P, S // LIST_ROWS], U16, name="offs_sb")
        pos_sb = [keep.tile([P, T // LIST_ROWS], U16, name="pos%d_sb" % r) for r in range(LISTS)]
        token_words = keep.tile([P, T], I32, name="token_words", align_bytes=ALIGN)
        token_scales = keep.tile([P, T], U8, name="token_scales", align_bytes=ALIGN)
        slot_words = [keep.tile([P, GATHER_EXPERTS * C], U32, name="slot_words%d" % g, align_bytes=ALIGN) for g in range(groups)]
        slot_scales = [keep.tile([P, GATHER_EXPERTS * C], U8, name="slot_scales%d" % g, align_bytes=ALIGN) for g in range(groups)]
        gates = keep.tile([P, LISTS, WIDE], F32, name="gates", align_bytes=ALIGN)
        gate_rows = keep.tile([P, T - TURNED_FROM], F32, name="gate_rows")
        gate_cols = keep.tile([P, (T - TURNED_FROM) // P, LISTS], F32, name="gate_cols")
        bias = keep.tile([P, HALVES, BIAS_ROW], F32, name="bias")
        y = [keep.tile([P, S], F32, name="y%d" % h) for h in range(HALVES)]
        identity = keep.tile([P, P], F32, name="identity")
        banks = [psum.tile([P, BANK], F32, name="bank%d" % i) for i in range(BANKS)]

        loads = [(e, 0, HALVES) for e in range(LAST)] + [(LAST, h, 1) for h in range(HALVES)]
        last_first = (LAST, 1, 0, 1)
        middle_seconds = (HALVES_FROM, LAST - 1 - HALVES_FROM, 1, 1)
        last_second = (LAST - 1, 2, 1, 1)
        units = [(0, 1, 0, HALVES)] + [(e, 2, 0, HALVES) for e in range(1, PAIRED_UP_TO, 2)]
        units = units + [(e, 1, 0, HALVES) for e in range(PAIRED_UP_TO, HALVES_FROM)]
        units = units + [(e, 1, 0, 1) for e in range(HALVES_FROM, E)] + [middle_seconds, last_second]

        landed = {}
        for e, h, halves in loads:
            name = "landed%d_%d" % (e, h)
            landed[e, h] = keep.tile([P, PACK, halves * P], F32, name=name, tag=name, align_bytes=ALIGN)

        warm = keep.tile([P, 2], F32, name="warm")
        nc.vector.memset(token_scales[:].bitcast(I32), 0)
        nc.gpsimd.memset(warm[:, 0:1], 0.0)
        nc.scalar.activation(warm[:, 1:2], warm[:, 0:1], SILU)
        make_identity(nc, identity[:])
        nc.vector.memset(gate_rows[:], 0.0)

        scale_rows = x_scales[0].rearrange("(q r) t -> r q t", r=4)
        nc.sync.dma_start(token_words[:], x_words[0].rearrange("p t r -> p (t r)").bitcast(I32))
        nc.sync.dma_start(offs_sb[:], offs)
        for e, h, halves in loads:
            if halves == HALVES:
                nc.sync.dma_start(landed[e, h][:].rearrange("p j n -> p (j n)"), w[e].rearrange("(p j) n -> p (j n)", j=PACK))
            else:
                nc.sync.dma_start(landed[e, h][:], w[e].rearrange("(p j) n -> p j n", j=PACK)[:, :, h * P : (h + 1) * P])
            if e == 0:
                nc.sync.dma_start(gate_rows[0:LISTS, :], gate[:, 0, TURNED_FROM:T])
            if e == 1:
                for r in range(4):
                    nc.sync.dma_start(token_scales[r:P:32, :].bitcast(I32), scale_rows[r].bitcast(I32))
            if e == VECTOR_FROM:
                nc.sync.dma_start(bias[:, :, 0:E], b.rearrange("(h p) e -> p h e", p=P))
        nc.sync.dma_start(pos_sb[0][:], pos1)
        nc.sync.dma_start(pos_sb[1][:], pos2)
        for a, z in ((0, GATE_CUT), (GATE_CUT, WIDE)):
            nc.sync.dma_start(gates[:, :, a:z], gate[:, 0:P, a:z].rearrange("r p t -> p r t"))

        for t in range(0, T - TURNED_FROM, P):
            nc.tensor.transpose(banks[-1][:, t : t + P], gate_rows[:, t : t + P], identity[:])
        nc.scalar.copy(gate_cols[:], banks[-1][:, 0 : T - TURNED_FROM].rearrange("p (j q) -> p j q", q=P)[:, :, 0:LISTS])

        columns = GATHER_EXPERTS * C // LIST_ROWS
        for g in range(groups):
            nc.vector.tensor_copy(slot_words[g][:], token_words[:].bitcast(U32).indirect(offs_sb[:, g * columns : (g + 1) * columns]))
        for g in range(groups):
            nc.vector.tensor_copy(slot_scales[g][:], token_scales[:].indirect(offs_sb[:, g * columns : (g + 1) * columns]))

        words, scales = {}, {}

        def tag_of(kind, unit):
            return "%s%d_%d" % (kind, unit[0], unit[2])

        def quantize(unit):
            first, count, h, halves = unit
            width = halves * P
            grouped_tag = tag_of("grouped", last_first if unit == last_second else unit)
            words_tag = tag_of("landed", last_first) if unit == middle_seconds else tag_of("words", unit)
            grouped = keep.tile([P, count * width, PACK], BF16, name=tag_of("grouped", unit), tag=grouped_tag, align_bytes=ALIGN)
            on_scalar = first < VECTOR_FROM or unit == middle_seconds
            if on_scalar or unit == last_second:
                cuts = [0, width]
            elif first == SHARED:
                cuts = [0, P, SHARED_CUT, N]
            else:
                cuts = [0, width // 2, width]
            for i in range(count):
                e = first + i
                source = landed[e, h][:] if e == LAST else landed[e, 0][:, :, h * P : h * P + width]
                for a, z in zip(cuts[:-1], cuts[1:]):
                    copy = nc.scalar.copy if on_scalar or (e == SHARED and a == SHARED_CUT) else nc.vector.tensor_copy
                    copy(
                        grouped[:, i * width + a : i * width + z, :].rearrange("p (c i) j -> p c j i", i=PAIR),
                        source[:, :, a:z].rearrange("p j (c i) -> p c j i", i=PAIR),
                    )
            words[unit] = keep.tile([P, count * width], U32, name=tag_of("words", unit), tag=words_tag, align_bytes=ALIGN)
            scales[unit] = keep.tile([P, count * width], U8, name=tag_of("scales", unit), align_bytes=ALIGN)
            if on_scalar:
                cuts = [0, count * width]
            elif unit == last_second:
                cuts = [0, width, count * width]
            for a, z in zip(cuts[:-1], cuts[1:]):
                nc.vector.quantize_mx(
                    out=words[unit][:, a:z].bitcast(FP8X4), scales=scales[unit][:, a:z], in_=grouped[:, a:z, :].rearrange("p n j -> p (n j)")
                )

        def multiply(unit, bank):
            first, count, h, halves = unit
            parts = [(first + i, h + d) for i in range(count) for d in range(halves)]
            for at, (e, half) in enumerate(parts):
                features = slice(at * P, (at + 1) * P)
                g, member = divmod(e, GATHER_EXPERTS)
                slots = slice(member * C, (member + 1) * C)
                nc.tensor.matmul_mx(
                    out=bank[:, at * C : (at + 1) * C],
                    lhsT=words[unit][:, features].bitcast(FP8X4),
                    lhsT_scale=scales[unit][:, features],
                    rhs=slot_words[g][:, slots].bitcast(FP8X4),
                    rhs_scale=slot_scales[g][:, slots],
                    start=True,
                    stop=True,
                )
            for at, (e, half) in enumerate(parts):
                nc.scalar.activation(y[half][:, e * C : (e + 1) * C], bank[:, at * C : (at + 1) * C], SILU, bias=bias[:, half, e : e + 1])

        def fetched(h, r, a, z):
            return y[h][:].indirect(pos_sb[r][:, a // LIST_ROWS : z // LIST_ROWS])

        def combine_on_vector(h):
            for a, z in zip(CUTS[h][:-1], CUTS[h][1:]):
                names = ["terms%d_%d_%d" % (h, a, r) for r in range(LISTS)]
                tags = list(names)
                if (h, a) == (1, GATE_CUT):
                    tags = [names[0], "terms1_0_0"]
                terms = [keep.tile([P, z - a], F32, name=names[r], tag=tags[r], align_bytes=ALIGN) for r in range(LISTS)]
                result = keep.tile([P, z - a], F32, name="result%d_%d" % (h, a), align_bytes=ALIGN)
                for r in range(LISTS):
                    value = helped[:] if (h, r, a) == HELPED else fetched(h, r, a, z)
                    nc.vector.tensor_tensor(terms[r][:], value, gates[:, r, a:z], MULT)
                nc.vector.tensor_tensor(result[:], terms[0][:], terms[1][:], ADD)
                nc.sync.dma_start(out[h * P : (h + 1) * P, a:z], result[:])

        def fetch_and_turn(h, turned):
            names = ["values%d_%d" % (h, r) for r in range(LISTS)]
            tags = list(names)
            if h == 0:
                tags = [names[0], tag_of("words", last_second)]
            count = T - VECTOR_TOKENS[h]
            values = [keep.tile([P, count], F32, name=names[r], tag=tags[r], align_bytes=ALIGN) for r in range(LISTS)]
            for r in range(LISTS):
                nc.scalar.activation(values[r][:], fetched(h, r, VECTOR_TOKENS[h], T), COPY)
            for r in range(LISTS):
                for t in range(0, count, P):
                    nc.tensor.transpose(turned[r][:, t : t + P], values[r][:, t : t + P], identity[:])

        def weigh_and_turn_back(h, turned, back):
            count = T - VECTOR_TOKENS[h]
            scaled = keep.tile([P, LISTS, count], F32, name="scaled%d" % h)
            for t in range(0, count, P):
                block = (VECTOR_TOKENS[h] + t - TURNED_FROM) // P
                for r in range(LISTS):
                    nc.scalar.activation(scaled[:, r, t : t + P], turned[r][:, t : t + P], COPY, scale=gate_cols[:, block, r : r + 1])
            for t in range(0, count, P):
                for r in range(LISTS):
                    nc.tensor.matmul(
                        back[:, t : t + P], scaled[:, r, t : t + P], identity[:], start=(r == 0), stop=(r == LISTS - 1), is_transpose=True
                    )

        def store_turned(h, back):
            count = T - VECTOR_TOKENS[h]
            result = keep.tile([P, count], F32, name="turned_result%d" % h, align_bytes=ALIGN)
            nc.scalar.copy(result[:], back[:, 0:count])
            nc.scalar.dma_start(out[h * P : (h + 1) * P, VECTOR_TOKENS[h] : T], result[:])

        for unit in units:
            quantize(unit)
        for i, unit in enumerate(units):
            multiply(unit, banks[i % BANKS])
        free = [banks[(len(units) - 1 + i) % BANKS] for i in range(5)]
        turned = [[free[0][:], free[1][:]], [free[2][:, 0 : BANK // 2], free[2][:, BANK // 2 : BANK]]]
        back = free[3:5]
        fetch_and_turn(0, turned[0])
        fetch_and_turn(1, turned[1])
        helped = keep.tile([P, GATE_CUT], F32, name="helped", align_bytes=ALIGN)
        nc.scalar.activation(helped[:], fetched(HELPED[0], HELPED[1], HELPED[2], HELPED[2] + GATE_CUT), COPY)
        for h in range(HALVES):
            combine_on_vector(h)
        for h in range(HALVES):
            weigh_and_turn_back(h, turned[h], back[h])
        for h in range(HALVES):
            store_turned(h, back[h])
